import numpy as np
import ml_dtypes


def mxq(x, axis, fmt="e4m3"):
    dtype, down = {"e4m3": (ml_dtypes.float8_e4m3fn, 7), "e5m2": (ml_dtypes.float8_e5m2, 14)}[fmt]
    v = np.moveaxis(np.asarray(x, np.float32).astype(ml_dtypes.bfloat16).astype(np.float64), axis, -1)
    blocks = v.reshape(v.shape[:-1] + (-1, 32))
    amax = np.abs(blocks).max(-1, keepdims=True)
    byte = np.maximum(np.where(amax > 0, np.frexp(amax)[1] - 1 + 127, 0) - down, 1)
    scale = np.exp2(byte - 127.0)
    codes = (blocks / scale).astype(np.float32).astype(dtype).astype(np.float64)
    return np.moveaxis((codes * scale).reshape(v.shape), -1, axis)


WIDE = False


def mx_kscale(k):
    if not WIDE:
        return np.ones(k)
    levels = np.array([24, -24, 12, -12, 0])
    if k % 512:
        return np.exp2(np.random.permutation(np.resize(levels, k // 32))).repeat(32)
    a = np.empty((k // 512, 16))
    for p in range(k // 512):
        a[p, :8] = np.random.permutation(np.resize(levels, 8))
        for g in range(8):
            far = levels[np.abs(levels - a[p, g]) >= 10]
            a[p, g + 8] = far[np.random.randint(len(far))]
    return np.exp2(a.ravel()).repeat(32)


def f64(x):
    return np.asarray(x).astype(np.float64)


E2M1 = np.array([0.0, 0.5, 1.0, 1.5, 2.0, 3.0, 4.0, 6.0, -0.0, -0.5, -1.0, -1.5, -2.0, -3.0, -4.0, -6.0])


def pack_weight(w, fmt):
    k, n = w.shape
    w = f64(np.asarray(w, np.float32).astype(ml_dtypes.bfloat16)).reshape(k // 32, 32, n)
    amax = np.abs(w).max(1)
    if fmt == "e4m3":
        byte = np.frexp(amax)[1] - 1 + 127 - 7
    else:
        mant, ex = np.frexp(amax / 6.0)
        byte = np.where(mant > 0.5, ex, ex - 1) + 127
    byte = np.clip(np.where(amax > 0, byte, 1), 1, 254)
    scaled = (w * np.exp2(127.0 - byte)[:, None, :]).reshape(k, n).astype(np.float32)
    by_word = np.ascontiguousarray(scaled.reshape(k // 512, 128, 4, n).transpose(0, 1, 3, 2))
    if fmt == "e4m3":
        words = by_word.astype(ml_dtypes.float8_e4m3fn).view(np.uint8)
    else:
        c = by_word.astype(ml_dtypes.float4_e2m1fn).view(np.uint8) & 0xF
        words = (c[..., 0::2] | (c[..., 1::2] << 4)).reshape(k // 512, 128, 2 * n)
    return np.ascontiguousarray(words), np.ascontiguousarray(byte.astype(np.uint8).reshape(k // 512, 16, n))


def unpack_weight(words, scales, fmt):
    g, _, n = scales.shape
    words = np.ascontiguousarray(words).reshape(g, 128, n, -1)
    if fmt == "e4m3":
        vals = words.view(ml_dtypes.float8_e4m3fn).astype(np.float64)
    else:
        nib = np.empty((g, 128, n, 4), np.uint8)
        nib[..., 0::2] = words & 0xF
        nib[..., 1::2] = words >> 4
        vals = E2M1[nib]
    vals = vals * np.repeat(np.exp2(scales.astype(np.float64) - 127.0), 8, axis=1)[..., None]
    return vals.transpose(0, 1, 3, 2).reshape(g * 512, n)


def planes(y):
    n, m = y.shape
    v = y.astype(np.float32).astype(ml_dtypes.bfloat16).astype(np.float64).reshape(n // 32, 32, m)
    top = np.abs(v).max(1)
    byte = np.clip(np.where(top > 0, np.frexp(top)[1] - 1 + 127 - 7, 1), 1, 254)
    codes = (v * np.exp2(127.0 - byte)[:, None, :]).reshape(n, m).astype(np.float32).astype(ml_dtypes.float8_e4m3fn).view(np.uint8)
    words = codes.reshape(n // 512, 128, 4, m).transpose(0, 1, 3, 2)
    return np.ascontiguousarray(words), np.ascontiguousarray(byte.astype(np.uint8).reshape(n // 512, 16, m))


K, D, M, J = 1024, 1024, 512, 1024


def setup_inputs():
    n = np.random.standard_normal
    u = mx_kscale(D)[:, None]
    s3 = mx_kscale(K)[:, None]
    s = mx_kscale(K)[:, None]
    x = n((K, M)); x[:512] *= 6.0
    w = n((K, D)) / np.sqrt(K) / s / u.T; w[:512] /= 2.0
    p_w8 = pack_weight(w[:512], "e4m3")
    p_w4 = pack_weight(w[512:], "e2m1")
    p_wk = pack_weight(n((K, D)) / np.sqrt(K) / s3 * u.T, "e4m3")
    return {
        "x": (x * s).astype(np.float32),
        "w8_words": p_w8[0],
        "w8_scales": p_w8[1],
        "w4_words": p_w4[0],
        "w4_scales": p_w4[1],
        "c": (n((K, J)) * s3).astype(np.float32),
        "wk_words": p_wk[0],
        "wk_scales": p_wk[1],
    }


def reference(x, w8_words, w8_scales, w4_words, w4_scales, c, wk_words, wk_scales):
    x_ = mxq(f64(x), 0, "e4m3")
    w8_ = unpack_weight(w8_words, w8_scales, "e4m3")
    w4_ = unpack_weight(w4_words, w4_scales, "e2m1")
    qr = w8_.T @ x_[:512] + w4_.T @ x_[512:]
    qr_ = mxq(qr, 0, "e4m3")
    c_ = mxq(f64(c), 0, "e4m3")
    wk_ = unpack_weight(wk_words, wk_scales, "e4m3")
    kc = wk_.T @ c_
    kc_ = mxq(kc, 0, "e4m3")
    sc = qr_.T @ kc_
    return (np.maximum(sc, 0.0) * 0.03125, kc) + planes(kc)

@@ -1,0 +1,285 @@
+from contextlib import ExitStack
+
+import concourse.mybir as mybir
+
+K, D, M, J = 1024, 1024, 512, 1024
+FLOPS = 2 * K * D * M + 2 * K * D * J + 2 * D * M * J
+
+F32 = mybir.dt.float32
+BF16 = mybir.dt.bfloat16
+I32 = mybir.dt.int32
+U32 = mybir.dt.uint32
+U8 = mybir.dt.uint8
+FP8X4 = mybir.dt.float8_e4m3fn_x4
+FP4X4 = mybir.dt.float4_e2m1fn_x4
+ACT = mybir.ActivationFunctionType
+ALU = mybir.AluOpType
+
+P = 128
+PACK = 4
+PASS = P * PACK
+BANK = 512
+SCORE_SCALE = 0.03125
+ROW_W4, ROW_W8, ROW_WK = 0, 4, 8
+
+
+def tile_mix_kvw_outl_relu_kernel(
+    tc, x, w8_words, w8_scales, w4_words, w4_scales, c, wk_words, wk_scales, out_0, out_1, out_2, out_3
+):
+    nc = tc.nc
+    with ExitStack() as ctx:
+        sb = ctx.enter_context(tc.tile_pool(name="sb", bufs=1))
+        psum = ctx.enter_context(tc.psum_pool(name="psum", bufs=1))
+        ctx.enter_context(tc.manual_schedule())
+
+        def tile(name, shape, dtype):
+            return sb.tile(shape, dtype, name=name, align_bytes=64)
+
+        def bank(i):
+            return psum.tile([P, BANK], F32, name="bank%d" % i)
+
+        def words_of(dram):
+            return dram.rearrange("p n i -> p (n i)").bitcast(I32)
+
+        wk_scales_raw = tile("wk_scales_raw", [P, D], U8)
+        wq_scales_raw = tile("wq_scales_raw", [P, D], U8)
+        nc.vector.memset(wk_scales_raw[:].bitcast(I32), 0)
+        nc.vector.memset(wq_scales_raw[:].bitcast(I32), 0)
+        wk_raw = [tile("wk_raw%d" % a, [P, D], U32) for a in range(2)]
+        c_raw = {(a, h): tile("c_raw%d%d" % (a, h), [P, PACK, BANK], F32) for a in range(2) for h in range(2)}
+
+        def load_c(a, h):
+            nc.sync.dma_start(
+                out=c_raw[a, h][:],
+                in_=c[PASS * a : PASS * (a + 1), BANK * h : BANK * (h + 1)].rearrange("(p t) j -> p t j", t=PACK),
+            )
+
+        def load_wq_scales(lo, hi):
+            for n in range(lo, hi):
+                row, dram = ((ROW_W8, w8_scales), (ROW_W4, w4_scales))[n // 4]
+                q = n % 4
+                nc.sync.dma_start(
+                    out=wq_scales_raw[32 * q + row : 32 * q + row + 4, :].bitcast(I32),
+                    in_=dram[0, 4 * q : 4 * q + 4, :].bitcast(I32),
+                )
+
+        nc.sync.dma_start(out=wk_raw[0][:].bitcast(I32), in_=words_of(wk_words[0]))
+        for q in range(4):
+            nc.sync.dma_start(
+                out=wk_scales_raw[32 * q + ROW_WK : 32 * q + ROW_WK + 8, :].bitcast(I32),
+                in_=wk_scales[:, 4 * q : 4 * q + 4, :].bitcast(I32),
+            )
+        nc.sync.dma_start(out=wk_raw[1][:].bitcast(I32), in_=words_of(wk_words[1]))
+        load_c(0, 0)
+        load_wq_scales(0, 6)
+        load_c(1, 0)
+        load_c(0, 1)
+        load_wq_scales(6, 8)
+        load_c(1, 1)
+        w8_raw = tile("w8_raw", [P, D], U32)
+        nc.sync.dma_start(out=w8_raw[:].bitcast(I32), in_=words_of(w8_words[0]))
+        w4_raw = tile("w4_raw", [P, 2 * D], U8)
+        nc.sync.dma_start(out=w4_raw[:].bitcast(I32), in_=w4_words[0].bitcast(I32))
+        x_raw = [tile("x_raw%d" % a, [P, PACK, M], F32) for a in range(2)]
+        for a in range(2):
+            nc.sync.dma_start(
+                out=x_raw[a][:], in_=x[PASS * a : PASS * (a + 1), :].rearrange("(p t) m -> p t m", t=PACK)
+            )
+
+        def deal(dst, src, e):
+            nc.vector.tensor_copy(
+                out=dst.rearrange("p (b t m e) -> p b t m e", b=2, t=PACK, e=e),
+                in_=src.rearrange("p (b m t e) -> p b t m e", b=2, t=PACK, e=e),
+            )
+
+        def interleave(copy, dst, src, lo, hi):
+            copy(
+                out=dst[:, PACK * lo : PACK * hi].rearrange("p (c i t) -> p c t i", i=4, t=PACK),
+                in_=src[:, :, lo:hi].rearrange("p t (c i) -> p c t i", i=4),
+            )
+
+        def act_copy(out, in_):
+            nc.scalar.activation(out=out, in_=in_, func=ACT.Copy)
+
+        def quantize(codes, scales, src, lo, hi):
+            nc.vector.quantize_mx(
+                out=codes[:, lo:hi].bitcast(FP8X4), scales=scales[:, lo:hi], in_=src[:, PACK * lo : PACK * hi]
+            )
+
+        vcopy = nc.vector.tensor_copy
+
+        wk_d = [tile("wk_d%d" % a, [P, D], U32) for a in range(2)]
+        for a in range(2):
+            deal(wk_d[a][:].bitcast(I32), wk_raw[a][:].bitcast(I32), 1)
+        wk_scales_d = tile("wk_scales_d", [P, D], U8)
+        deal(wk_scales_d[:], wk_scales_raw[:], 1)
+        wq_scales_d = tile("wq_scales_d", [P, D], U8)
+
+        c_codes, c_scales = {}, {}
+
+        def make_c(a, h, share):
+            bf = tile("c_bf%d%d" % (a, h), [P, PACK * BANK], BF16)
+            c_codes[a, h] = tile("c_codes%d%d" % (a, h), [P, BANK], U32)
+            c_scales[a, h] = tile("c_scales%d%d" % (a, h), [P, BANK], U8)
+            interleave(vcopy, bf, c_raw[a, h], 0, 256)
+            if share:
+                interleave(act_copy, bf, c_raw[a, h], 384, 512)
+                interleave(vcopy, bf, c_raw[a, h], 256, 384)
+            else:
+                interleave(vcopy, bf, c_raw[a, h], 256, 512)
+            quantize(c_codes[a, h], c_scales[a, h], bf, 0, 256)
+            quantize(c_codes[a, h], c_scales[a, h], bf, 256, 512)
+
+        kc32 = [tile("kc32_%d" % b, [P, PACK, J], F32) for b in range(2)]
+
+        def kc_pass(acc, i, h, a):
+            cols = slice(P * i, P * (i + 1))
+            nc.tensor.matmul_mx(
+                out=acc[:],
+                lhsT=wk_d[a][:, cols].bitcast(FP8X4),
+                lhsT_scale=wk_scales_d[ROW_WK + 4 * a :, cols],
+                rhs=c_codes[a, h][:].bitcast(FP8X4),
+                rhs_scale=c_scales[a, h][:],
+                start=(a == 0),
+                stop=(a == 1),
+            )
+
+        def kc_out(acc, i, h):
+            nc.scalar.copy(out=kc32[i // PACK][:, i % PACK, BANK * h : BANK * (h + 1)], in_=acc[:])
+
+        def store_kc32(b, u):
+            nc.sync.dma_start(
+                out=out_1[PASS * b : PASS * (b + 1), :].rearrange("(p t) j -> p t j", t=PACK)[:, 2 * u : 2 * u + 2, :],
+                in_=kc32[b][:, 2 * u : 2 * u + 2, :],
+            )
+
+        make_c(0, 0, True)
+        accs = [bank(i) for i in range(8)]
+        for i in range(8):
+            kc_pass(accs[i], i, 0, 0)
+        make_c(1, 0, True)
+        for i in range(8):
+            kc_pass(accs[i], i, 0, 1)
+            kc_out(accs[i], i, 0)
+        make_c(0, 1, False)
+        deal(wq_scales_d[:], wq_scales_raw[:], 1)
+        accs = [bank(i) for i in range(8)]
+        for i in range(6):
+            kc_pass(accs[i], i, 1, 0)
+        make_c(1, 1, False)
+        for i in range(8):
+            kc_pass(accs[i], i, 1, 1)
+            if i < 2:
+                kc_pass(accs[6 + i], 6 + i, 1, 0)
+            kc_out(accs[i], i, 1)
+            if i % 2 == 1:
+                store_kc32(i // PACK, (i % PACK) // 2)
+
+        w8_d = tile("w8_d", [P, D], U32)
+        deal(w8_d[:].bitcast(I32), w8_raw[:].bitcast(I32), 1)
+        w4_d = tile("w4_d", [P, 2 * D], U8)
+        deal(w4_d[:], w4_raw[:], 2)
+
+        kc_codes = [tile("kc_codes%d" % b, [P, J], U32) for b in range(2)]
+        kc_scales = tile("kc_scales", [P, 2 * J], U8)
+        kc_bf = {(b, h): tile("kc_bf%d%d" % (b, h), [P, PACK * BANK], BF16) for b in range(2) for h in range(2)}
+
+        def kc_round(copy, b, h, lo=0, hi=BANK):
+            interleave(copy, kc_bf[b, h], kc32[b][:, :, BANK * h : BANK * (h + 1)], lo, hi)
+
+        def kc_quant(b, h):
+            cols = slice(BANK * h, BANK * (h + 1))
+            quantize(kc_codes[b][:, cols], kc_scales[:, J * b : J * (b + 1)][:, cols], kc_bf[b, h], 0, BANK)
+
+        x_bf = [tile("x_bf%d" % a, [P, PACK * M], BF16) for a in range(2)]
+        x_codes = [tile("x_codes%d" % a, [P, M], U32) for a in range(2)]
+        x_scales = [tile("x_scales%d" % a, [P, M], U8) for a in range(2)]
+
+        kc_round(vcopy, 0, 0)
+        interleave(vcopy, x_bf[0], x_raw[0], 0, M)
+        kc_quant(0, 0)
+        quantize(x_codes[0], x_scales[0], x_bf[0], 0, M)
+        interleave(vcopy, x_bf[1], x_raw[1], 0, 256)
+        interleave(act_copy, x_bf[1], x_raw[1], 384, 512)
+        interleave(vcopy, x_bf[1], x_raw[1], 256, 384)
+        quantize(x_codes[1], x_scales[1], x_bf[1], 0, 256)
+        quantize(x_codes[1], x_scales[1], x_bf[1], 256, 512)
+        kc_round(act_copy, 1, 0, 256, 512)
+        kc_round(vcopy, 1, 0, 0, 256)
+        kc_round(vcopy, 0, 1)
+        kc_quant(1, 0)
+        kc_quant(0, 1)
+        nc.sync.dma_start(out=words_of(out_2[0]), in_=kc_codes[0][:].bitcast(I32))
+
+        qr_bf = [tile("qr_bf%d" % g, [P, 2 * PASS], BF16) for g in range(4)]
+        qr_codes = [tile("qr_codes%d" % g, [P, 2 * P], U32) for g in range(4)]
+        qr_scales = [tile("qr_scales%d" % g, [P, 2 * P], U8) for g in range(4)]
+
+        def qr_bank(g, b):
+            acc = bank(2 * g + b)
+            ms = slice(P * g, P * (g + 1))
+            for t in range(PACK):
+                i = PACK * b + t
+                cols = slice(P * i, P * (i + 1))
+                nc.tensor.matmul_mx(
+                    out=acc[:, P * t : P * (t + 1)],
+                    lhsT=w8_d[:, cols].bitcast(FP8X4),
+                    lhsT_scale=wq_scales_d[ROW_W8:, cols],
+                    rhs=x_codes[0][:, ms].bitcast(FP8X4),
+                    rhs_scale=x_scales[0][:, ms],
+                    start=True,
+                    stop=False,
+                )
+                nc.tensor.matmul_mx(
+                    out=acc[:, P * t : P * (t + 1)],
+                    lhsT=w4_d[:, 2 * P * i : 2 * P * (i + 1)].bitcast(FP4X4),
+                    lhsT_scale=wq_scales_d[:, cols],
+                    rhs=x_codes[1][:, ms].bitcast(FP8X4),
+                    rhs_scale=x_scales[1][:, ms],
+                    start=False,
+                    stop=True,
+                )
+            nc.scalar.copy(
+                out=qr_bf[g][:, PASS * b : PASS * (b + 1)].rearrange("p (m t) -> p m t", t=PACK),
+                in_=acc[:].rearrange("p (t m) -> p m t", t=PACK),
+            )
+
+        for g in range(4):
+            for b in range(2):
+                qr_bank(g, b)
+            if g == 1:
+                quantize(qr_codes[0], qr_scales[0], qr_bf[0], 0, 2 * P)
+                kc_round(vcopy, 1, 1)
+                quantize(qr_codes[1], qr_scales[1], qr_bf[1], 0, 2 * P)
+                kc_quant(1, 1)
+        nc.sync.dma_start(out=words_of(out_2[1]), in_=kc_codes[1][:].bitcast(I32))
+        for q in range(4):
+            nc.sync.dma_start(
+                out=out_3[:, 4 * q : 4 * q + 4, :].rearrange("a r j -> r a j").bitcast(I32),
+                in_=kc_scales[32 * q : 32 * q + 4, :].rearrange("r (a j) -> r a j", a=2).bitcast(I32),
+            )
+        for g in range(2, 4):
+            quantize(qr_codes[g], qr_scales[g], qr_bf[g], 0, 2 * P)
+
+        scores = [tile("scores%d" % g, [P, J], F32) for g in range(4)]
+        for g in range(4):
+            for h in range(2):
+                acc = bank(2 * g + h)
+                js = slice(BANK * h, BANK * (h + 1))
+                for b in range(2):
+                    nc.tensor.matmul_mx(
+                        out=acc[:],
+                        lhsT=qr_codes[g][:, P * b : P * (b + 1)].bitcast(FP8X4),
+                        lhsT_scale=qr_scales[g][:, P * b : P * (b + 1)],
+                        rhs=kc_codes[b][:, js].bitcast(FP8X4),
+                        rhs_scale=kc_scales[:, J * b : J * (b + 1)][:, js],
+                        start=(b == 0),
+                        stop=(b == 1),
+                    )
+                if h == 0:
+                    nc.scalar.activation(out=scores[g][:, js], in_=acc[:], func=ACT.Relu, scale=SCORE_SCALE)
+                else:
+                    nc.vector.tensor_scalar(
+                        out=scores[g][:, js], in0=acc[:], scalar1=0.0, scalar2=SCORE_SCALE, op0=ALU.max, op1=ALU.mult
+                    )
+            nc.sync.dma_start(out=out_0[P * g : P * (g + 1), :], in_=scores[g][:])

@@ -19,8 +19,16 @@ P = 128
 PACK = 4
 PASS = P * PACK
 BANK = 512
+BANKS = 8
+LINE = 4
 SCORE_SCALE = 0.03125
+
 ROW_W4, ROW_W8, ROW_WK = 0, 4, 8
+
+CHUNKS = ((0, 256), (256, 256), (512, 512))
+STEP = 256
+SCALAR_SHARE = 128
+QR_AHEAD = 5
 
 
 def tile_mix_kvw_outl_relu_kernel(
@@ -28,258 +36,290 @@ def tile_mix_kvw_outl_relu_kernel(
 ):
     nc = tc.nc
     with ExitStack() as ctx:
-        sb = ctx.enter_context(tc.tile_pool(name="sb", bufs=1))
+        sbuf = ctx.enter_context(tc.tile_pool(name="sbuf", bufs=1))
         psum = ctx.enter_context(tc.psum_pool(name="psum", bufs=1))
         ctx.enter_context(tc.manual_schedule())
 
         def tile(name, shape, dtype):
-            return sb.tile(shape, dtype, name=name, align_bytes=64)
+            return sbuf.tile(shape, dtype, name=name, align_bytes=64)
 
-        def bank(i):
-            return psum.tile([P, BANK], F32, name="bank%d" % i)
+        def bank(n):
+            return psum.tile([P, BANK], F32, name="bank%d" % n)
 
-        def words_of(dram):
-            return dram.rearrange("p n i -> p (n i)").bitcast(I32)
+        def as_words(codes):
+            return codes.rearrange("p n t -> p (n t)").bitcast(I32)
+
+        def four_rows(rows):
+            return rows.rearrange("(p t) n -> p t n", t=PACK)
 
         wk_scales_raw = tile("wk_scales_raw", [P, D], U8)
         wq_scales_raw = tile("wq_scales_raw", [P, D], U8)
-        nc.vector.memset(wk_scales_raw[:].bitcast(I32), 0)
-        nc.vector.memset(wq_scales_raw[:].bitcast(I32), 0)
         wk_raw = [tile("wk_raw%d" % a, [P, D], U32) for a in range(2)]
-        c_raw = {(a, h): tile("c_raw%d%d" % (a, h), [P, PACK, BANK], F32) for a in range(2) for h in range(2)}
+        w8_raw = tile("w8_raw", [P, D], U32)
+        w4_raw = tile("w4_raw", [P, 2 * D], U8)
+        c_raw = {(a, n): tile("c_raw%d%d" % (a, n), [P, PACK, CHUNKS[n][1]], F32) for a in range(2) for n in range(3)}
+        x_raw = [tile("x_raw%d" % a, [P, PACK, M], F32) for a in range(2)]
 
-        def load_c(a, h):
-            nc.sync.dma_start(
-                out=c_raw[a, h][:],
-                in_=c[PASS * a : PASS * (a + 1), BANK * h : BANK * (h + 1)].rearrange("(p t) j -> p t j", t=PACK),
-            )
+        nc.gpsimd.memset(wk_scales_raw[:].bitcast(I32), 0)
+        nc.vector.memset(wq_scales_raw[:].bitcast(I32), 0)
 
-        def load_wq_scales(lo, hi):
-            for n in range(lo, hi):
-                row, dram = ((ROW_W8, w8_scales), (ROW_W4, w4_scales))[n // 4]
-                q = n % 4
-                nc.sync.dma_start(
-                    out=wq_scales_raw[32 * q + row : 32 * q + row + 4, :].bitcast(I32),
-                    in_=dram[0, 4 * q : 4 * q + 4, :].bitcast(I32),
+        def load_scales(queue, dst, row, scales):
+            rows = 4 * scales.shape[0]
+            for q in range(4):
+                queue.dma_start(
+                    out=dst[32 * q + row : 32 * q + row + rows, :].bitcast(I32),
+                    in_=scales[:, 4 * q : 4 * q + 4, :].bitcast(I32),
                 )
 
-        nc.sync.dma_start(out=wk_raw[0][:].bitcast(I32), in_=words_of(wk_words[0]))
-        for q in range(4):
-            nc.sync.dma_start(
-                out=wk_scales_raw[32 * q + ROW_WK : 32 * q + ROW_WK + 8, :].bitcast(I32),
-                in_=wk_scales[:, 4 * q : 4 * q + 4, :].bitcast(I32),
-            )
-        nc.sync.dma_start(out=wk_raw[1][:].bitcast(I32), in_=words_of(wk_words[1]))
-        load_c(0, 0)
-        load_wq_scales(0, 6)
-        load_c(1, 0)
-        load_c(0, 1)
-        load_wq_scales(6, 8)
-        load_c(1, 1)
-        w8_raw = tile("w8_raw", [P, D], U32)
-        nc.sync.dma_start(out=w8_raw[:].bitcast(I32), in_=words_of(w8_words[0]))
-        w4_raw = tile("w4_raw", [P, 2 * D], U8)
+        def load_c(a, n):
+            j0, width = CHUNKS[n]
+            nc.sync.dma_start(out=c_raw[a, n][:], in_=four_rows(c[PASS * a : PASS * (a + 1), j0 : j0 + width]))
+
+        load_scales(nc.gpsimd, wk_scales_raw, ROW_WK, wk_scales)
+        load_scales(nc.gpsimd, wq_scales_raw, ROW_W8, w8_scales)
+        load_scales(nc.gpsimd, wq_scales_raw, ROW_W4, w4_scales)
         nc.sync.dma_start(out=w4_raw[:].bitcast(I32), in_=w4_words[0].bitcast(I32))
-        x_raw = [tile("x_raw%d" % a, [P, PACK, M], F32) for a in range(2)]
         for a in range(2):
-            nc.sync.dma_start(
-                out=x_raw[a][:], in_=x[PASS * a : PASS * (a + 1), :].rearrange("(p t) m -> p t m", t=PACK)
-            )
+            load_c(a, 0)
+            nc.sync.dma_start(out=wk_raw[a][:].bitcast(I32), in_=as_words(wk_words[a]))
+        for n in (1, 2):
+            for a in range(2):
+                load_c(a, n)
+        nc.sync.dma_start(out=w8_raw[:].bitcast(I32), in_=as_words(w8_words[0]))
+        for a in range(2):
+            nc.sync.dma_start(out=x_raw[a][:], in_=four_rows(x[PASS * a : PASS * (a + 1), :]))
 
-        def deal(dst, src, e):
+        def deal_words(dst, src):
             nc.vector.tensor_copy(
-                out=dst.rearrange("p (b t m e) -> p b t m e", b=2, t=PACK, e=e),
-                in_=src.rearrange("p (b m t e) -> p b t m e", b=2, t=PACK, e=e),
+                out=dst.bitcast(I32).rearrange("p (b t m) -> p b m t", b=2, t=PACK),
+                in_=src.bitcast(I32).rearrange("p (b m t) -> p b m t", b=2, t=PACK),
             )
 
-        def interleave(copy, dst, src, lo, hi):
-            copy(
-                out=dst[:, PACK * lo : PACK * hi].rearrange("p (c i t) -> p c t i", i=4, t=PACK),
-                in_=src[:, :, lo:hi].rearrange("p t (c i) -> p c t i", i=4),
+        def deal_bytes(dst, src, per_column):
+            nc.vector.tensor_copy(
+                out=dst.rearrange("p (b t m e) -> p b t m e", b=2, t=PACK, e=per_column),
+                in_=src.rearrange("p (b m t e) -> p b t m e", b=2, t=PACK, e=per_column),
             )
 
-        def act_copy(out, in_):
+        def on_vector(out, in_):
+            nc.vector.tensor_copy(out=out, in_=in_)
+
+        def on_scalar(out, in_):
             nc.scalar.activation(out=out, in_=in_, func=ACT.Copy)
 
-        def quantize(codes, scales, src, lo, hi):
-            nc.vector.quantize_mx(
-                out=codes[:, lo:hi].bitcast(FP8X4), scales=scales[:, lo:hi], in_=src[:, PACK * lo : PACK * hi]
+        def round_columns(copy, dst, src, lo, hi):
+            copy(
+                dst[:, PACK * lo : PACK * hi].rearrange("p (n i t) -> p n t i", i=LINE, t=PACK),
+                src[:, :, lo:hi].rearrange("p t (n i) -> p n t i", i=LINE),
             )
 
-        vcopy = nc.vector.tensor_copy
+        def quantize_columns(operand, lo, hi):
+            rounded, codes, scales = operand
+            nc.vector.quantize_mx(
+                out=codes[:, lo:hi].bitcast(FP8X4), scales=scales[:, lo:hi], in_=rounded[:, PACK * lo : PACK * hi]
+            )
 
-        wk_d = [tile("wk_d%d" % a, [P, D], U32) for a in range(2)]
-        for a in range(2):
-            deal(wk_d[a][:].bitcast(I32), wk_raw[a][:].bitcast(I32), 1)
-        wk_scales_d = tile("wk_scales_d", [P, D], U8)
-        deal(wk_scales_d[:], wk_scales_raw[:], 1)
-        wq_scales_d = tile("wq_scales_d", [P, D], U8)
+        def mx_operand(name, width):
+            return (
+                tile(name + "_rounded", [P, PACK * width], BF16),
+                tile(name + "_codes", [P, width], U32),
+                tile(name + "_scales", [P, width], U8),
+            )
 
-        c_codes, c_scales = {}, {}
+        def make_operand(operand, raw):
+            half = raw.shape[2] // 2
+            for lo in (0, half):
+                round_columns(on_vector, operand[0], raw, lo, lo + half)
+            for lo in (0, half):
+                quantize_columns(operand, lo, lo + half)
 
-        def make_c(a, h, share):
-            bf = tile("c_bf%d%d" % (a, h), [P, PACK * BANK], BF16)
-            c_codes[a, h] = tile("c_codes%d%d" % (a, h), [P, BANK], U32)
-            c_scales[a, h] = tile("c_scales%d%d" % (a, h), [P, BANK], U8)
-            interleave(vcopy, bf, c_raw[a, h], 0, 256)
-            if share:
-                interleave(act_copy, bf, c_raw[a, h], 384, 512)
-                interleave(vcopy, bf, c_raw[a, h], 256, 384)
-            else:
-                interleave(vcopy, bf, c_raw[a, h], 256, 512)
-            quantize(c_codes[a, h], c_scales[a, h], bf, 0, 256)
-            quantize(c_codes[a, h], c_scales[a, h], bf, 256, 512)
+        wk_dealt = [tile("wk_dealt%d" % a, [P, D], U32) for a in range(2)]
+        w8_dealt = tile("w8_dealt", [P, D], U32)
+        w4_dealt = tile("w4_dealt", [P, 2 * D], U8)
+        wk_scales_dealt = tile("wk_scales_dealt", [P, D], U8)
+        wq_scales_dealt = tile("wq_scales_dealt", [P, D], U8)
+        c_mx = {(a, n): mx_operand("c%d%d" % (a, n), CHUNKS[n][1]) for a in range(2) for n in range(3)}
+        x_mx = [mx_operand("x%d" % a, M) for a in range(2)]
 
         kc32 = [tile("kc32_%d" % b, [P, PACK, J], F32) for b in range(2)]
+        kc_scales = tile("kc_scales", [P, 2 * J], U8)
+        kc_mx = [
+            (
+                tile("kc_rounded%d" % b, [P, PACK * J], BF16),
+                tile("kc_codes%d" % b, [P, J], U32),
+                kc_scales[:, J * b : J * (b + 1)],
+            )
+            for b in range(2)
+        ]
 
-        def kc_pass(acc, i, h, a):
+        def kc_pass(banks, n, a, i):
+            width = CHUNKS[n][1]
+            per_bank = BANK // width
+            place = i % per_bank
             cols = slice(P * i, P * (i + 1))
             nc.tensor.matmul_mx(
-                out=acc[:],
-                lhsT=wk_d[a][:, cols].bitcast(FP8X4),
-                lhsT_scale=wk_scales_d[ROW_WK + 4 * a :, cols],
-                rhs=c_codes[a, h][:].bitcast(FP8X4),
-                rhs_scale=c_scales[a, h][:],
-                start=(a == 0),
-                stop=(a == 1),
+                out=banks[i // per_bank][:, width * place : width * (place + 1)],
+                lhsT=wk_dealt[a][:, cols].bitcast(FP8X4),
+                lhsT_scale=wk_scales_dealt[ROW_WK + 4 * a :, cols],
+                rhs=c_mx[a, n][1][:].bitcast(FP8X4),
+                rhs_scale=c_mx[a, n][2][:],
+                start=(a == 0 and place == 0),
+                stop=(a == 1 and place == per_bank - 1),
             )
 
-        def kc_out(acc, i, h):
-            nc.scalar.copy(out=kc32[i // PACK][:, i % PACK, BANK * h : BANK * (h + 1)], in_=acc[:])
+        def kc_first_passes(n, first_bank):
+            banks = [bank(first_bank + u) for u in range(BANKS * CHUNKS[n][1] // BANK)]
+            for i in range(D // P):
+                kc_pass(banks, n, 0, i)
+            return banks
 
-        def store_kc32(b, u):
-            nc.sync.dma_start(
-                out=out_1[PASS * b : PASS * (b + 1), :].rearrange("(p t) j -> p t j", t=PACK)[:, 2 * u : 2 * u + 2, :],
-                in_=kc32[b][:, 2 * u : 2 * u + 2, :],
-            )
+        def kc_second_passes(n, banks):
+            j0, width = CHUNKS[n]
+            per_bank = BANK // width
+            for i in range(D // P):
+                kc_pass(banks, n, 1, i)
+                if i % per_bank == per_bank - 1:
+                    b, t = divmod(i - per_bank + 1, PACK)
+                    nc.scalar.copy(
+                        out=kc32[b][:, t : t + per_bank, j0 : j0 + width],
+                        in_=banks[i // per_bank][:].rearrange("p (s j) -> p s j", s=per_bank),
+                    )
 
-        make_c(0, 0, True)
-        accs = [bank(i) for i in range(8)]
-        for i in range(8):
-            kc_pass(accs[i], i, 0, 0)
-        make_c(1, 0, True)
-        for i in range(8):
-            kc_pass(accs[i], i, 0, 1)
-            kc_out(accs[i], i, 0)
-        make_c(0, 1, False)
-        deal(wq_scales_d[:], wq_scales_raw[:], 1)
-        accs = [bank(i) for i in range(8)]
-        for i in range(6):
-            kc_pass(accs[i], i, 1, 0)
-        make_c(1, 1, False)
-        for i in range(8):
-            kc_pass(accs[i], i, 1, 1)
-            if i < 2:
-                kc_pass(accs[6 + i], 6 + i, 1, 0)
-            kc_out(accs[i], i, 1)
-            if i % 2 == 1:
-                store_kc32(i // PACK, (i % PACK) // 2)
+        def kc_round(copy, b, lo, hi):
+            round_columns(copy, kc_mx[b][0], kc32[b], lo, hi)
 
-        w8_d = tile("w8_d", [P, D], U32)
-        deal(w8_d[:].bitcast(I32), w8_raw[:].bitcast(I32), 1)
-        w4_d = tile("w4_d", [P, 2 * D], U8)
-        deal(w4_d[:], w4_raw[:], 2)
+        def store_kc32(b, lo, hi):
+            nc.sync.dma_start(out=four_rows(out_1[PASS * b : PASS * (b + 1), lo:hi]), in_=kc32[b][:, :, lo:hi])
 
-        kc_codes = [tile("kc_codes%d" % b, [P, J], U32) for b in range(2)]
-        kc_scales = tile("kc_scales", [P, 2 * J], U8)
-        kc_bf = {(b, h): tile("kc_bf%d%d" % (b, h), [P, PACK * BANK], BF16) for b in range(2) for h in range(2)}
+        def store_codes(b):
+            nc.sync.dma_start(out=as_words(out_2[b]), in_=kc_mx[b][1][:].bitcast(I32))
 
-        def kc_round(copy, b, h, lo=0, hi=BANK):
-            interleave(copy, kc_bf[b, h], kc32[b][:, :, BANK * h : BANK * (h + 1)], lo, hi)
+        deal_bytes(w4_dealt[:], w4_raw[:], 2)
+        round_columns(on_vector, c_mx[0, 0][0], c_raw[0, 0], 0, STEP)
+        deal_words(wk_dealt[0][:], wk_raw[0][:])
+        quantize_columns(c_mx[0, 0], 0, STEP)
+        round_columns(on_scalar, c_mx[1, 0][0], c_raw[1, 0], 0, STEP)
+        deal_bytes(wk_scales_dealt[:], wk_scales_raw[:], 1)
+        banks = kc_first_passes(0, 0)
+        deal_words(wk_dealt[1][:], wk_raw[1][:])
+        quantize_columns(c_mx[1, 0], 0, STEP)
+        kc_second_passes(0, banks)
 
-        def kc_quant(b, h):
-            cols = slice(BANK * h, BANK * (h + 1))
-            quantize(kc_codes[b][:, cols], kc_scales[:, J * b : J * (b + 1)][:, cols], kc_bf[b, h], 0, BANK)
+        make_operand(c_mx[0, 1], c_raw[0, 1])
+        banks = kc_first_passes(1, BANKS // 2)
+        make_operand(c_mx[1, 1], c_raw[1, 1])
+        kc_second_passes(1, banks)
+        store_kc32(0, 0, BANK)
 
-        x_bf = [tile("x_bf%d" % a, [P, PACK * M], BF16) for a in range(2)]
-        x_codes = [tile("x_codes%d" % a, [P, M], U32) for a in range(2)]
-        x_scales = [tile("x_scales%d" % a, [P, M], U8) for a in range(2)]
+        kc_round(on_vector, 0, 0, STEP)
+        round_columns(on_vector, c_mx[0, 2][0], c_raw[0, 2], 0, STEP)
+        quantize_columns(kc_mx[0], 0, STEP)
+        round_columns(on_vector, c_mx[0, 2][0], c_raw[0, 2], STEP, BANK)
+        quantize_columns(c_mx[0, 2], 0, STEP)
+        quantize_columns(c_mx[0, 2], STEP, BANK)
+        kc_round(on_scalar, 1, 0, STEP)
+        kc_round(on_scalar, 0, STEP, BANK)
+        kc_round(on_scalar, 1, STEP, BANK)
+        banks = kc_first_passes(2, 0)
+        make_operand(c_mx[1, 2], c_raw[1, 2])
+        kc_second_passes(2, banks)
+        store_kc32(0, BANK, J)
+        store_kc32(1, 0, J)
 
-        kc_round(vcopy, 0, 0)
-        interleave(vcopy, x_bf[0], x_raw[0], 0, M)
-        kc_quant(0, 0)
-        quantize(x_codes[0], x_scales[0], x_bf[0], 0, M)
-        interleave(vcopy, x_bf[1], x_raw[1], 0, 256)
-        interleave(act_copy, x_bf[1], x_raw[1], 384, 512)
-        interleave(vcopy, x_bf[1], x_raw[1], 256, 384)
-        quantize(x_codes[1], x_scales[1], x_bf[1], 0, 256)
-        quantize(x_codes[1], x_scales[1], x_bf[1], 256, 512)
-        kc_round(act_copy, 1, 0, 256, 512)
-        kc_round(vcopy, 1, 0, 0, 256)
-        kc_round(vcopy, 0, 1)
-        kc_quant(1, 0)
-        kc_quant(0, 1)
-        nc.sync.dma_start(out=words_of(out_2[0]), in_=kc_codes[0][:].bitcast(I32))
+        qr_mx = [mx_operand("qr%d" % u, 4 * P) for u in range(2)]
 
-        qr_bf = [tile("qr_bf%d" % g, [P, 2 * PASS], BF16) for g in range(4)]
-        qr_codes = [tile("qr_codes%d" % g, [P, 2 * P], U32) for g in range(4)]
-        qr_scales = [tile("qr_scales%d" % g, [P, 2 * P], U8) for g in range(4)]
-
-        def qr_bank(g, b):
-            acc = bank(2 * g + b)
-            ms = slice(P * g, P * (g + 1))
+        def qr_passes(acc, n, a):
+            g, b = divmod(n, 2)
+            tokens = slice(P * g, P * (g + 1))
             for t in range(PACK):
                 i = PACK * b + t
-                cols = slice(P * i, P * (i + 1))
-                nc.tensor.matmul_mx(
-                    out=acc[:, P * t : P * (t + 1)],
-                    lhsT=w8_d[:, cols].bitcast(FP8X4),
-                    lhsT_scale=wq_scales_d[ROW_W8:, cols],
-                    rhs=x_codes[0][:, ms].bitcast(FP8X4),
-                    rhs_scale=x_scales[0][:, ms],
-                    start=True,
-                    stop=False,
-                )
-                nc.tensor.matmul_mx(
-                    out=acc[:, P * t : P * (t + 1)],
-                    lhsT=w4_d[:, 2 * P * i : 2 * P * (i + 1)].bitcast(FP4X4),
-                    lhsT_scale=wq_scales_d[:, cols],
-                    rhs=x_codes[1][:, ms].bitcast(FP8X4),
-                    rhs_scale=x_scales[1][:, ms],
-                    start=False,
-                    stop=True,
-                )
-            nc.scalar.copy(
-                out=qr_bf[g][:, PASS * b : PASS * (b + 1)].rearrange("p (m t) -> p m t", t=PACK),
-                in_=acc[:].rearrange("p (t m) -> p m t", t=PACK),
-            )
-
-        for g in range(4):
-            for b in range(2):
-                qr_bank(g, b)
-            if g == 1:
-                quantize(qr_codes[0], qr_scales[0], qr_bf[0], 0, 2 * P)
-                kc_round(vcopy, 1, 1)
-                quantize(qr_codes[1], qr_scales[1], qr_bf[1], 0, 2 * P)
-                kc_quant(1, 1)
-        nc.sync.dma_start(out=words_of(out_2[1]), in_=kc_codes[1][:].bitcast(I32))
-        for q in range(4):
-            nc.sync.dma_start(
-                out=out_3[:, 4 * q : 4 * q + 4, :].rearrange("a r j -> r a j").bitcast(I32),
-                in_=kc_scales[32 * q : 32 * q + 4, :].rearrange("r (a j) -> r a j", a=2).bitcast(I32),
-            )
-        for g in range(2, 4):
-            quantize(qr_codes[g], qr_scales[g], qr_bf[g], 0, 2 * P)
-
-        scores = [tile("scores%d" % g, [P, J], F32) for g in range(4)]
-        for g in range(4):
-            for h in range(2):
-                acc = bank(2 * g + h)
-                js = slice(BANK * h, BANK * (h + 1))
-                for b in range(2):
-                    nc.tensor.matmul_mx(
-                        out=acc[:],
-                        lhsT=qr_codes[g][:, P * b : P * (b + 1)].bitcast(FP8X4),
-                        lhsT_scale=qr_scales[g][:, P * b : P * (b + 1)],
-                        rhs=kc_codes[b][:, js].bitcast(FP8X4),
-                        rhs_scale=kc_scales[:, J * b : J * (b + 1)][:, js],
-                        start=(b == 0),
-                        stop=(b == 1),
-                    )
-                if h == 0:
-                    nc.scalar.activation(out=scores[g][:, js], in_=acc[:], func=ACT.Relu, scale=SCORE_SCALE)
+                if a == 0:
+                    weights = w8_dealt[:, P * i : P * (i + 1)].bitcast(FP8X4)
+                    weight_scales = wq_scales_dealt[ROW_W8:, P * i : P * (i + 1)]
                 else:
-                    nc.vector.tensor_scalar(
-                        out=scores[g][:, js], in0=acc[:], scalar1=0.0, scalar2=SCORE_SCALE, op0=ALU.max, op1=ALU.mult
-                    )
-            nc.sync.dma_start(out=out_0[P * g : P * (g + 1), :], in_=scores[g][:])
+                    weights = w4_dealt[:, 2 * P * i : 2 * P * (i + 1)].bitcast(FP4X4)
+                    weight_scales = wq_scales_dealt[ROW_W4:, P * i : P * (i + 1)]
+                nc.tensor.matmul_mx(
+                    out=acc[:, P * t : P * (t + 1)],
+                    lhsT=weights,
+                    lhsT_scale=weight_scales,
+                    rhs=x_mx[a][1][:, tokens].bitcast(FP8X4),
+                    rhs_scale=x_mx[a][2][:, tokens],
+                    start=(a == 0 and t == 0),
+                    stop=(a == 1 and t == PACK - 1),
+                )
+
+        def qr_quantize(g):
+            lo = 2 * P * (g % 2)
+            quantize_columns(qr_mx[g // 2], lo, lo + 2 * P)
+
+        deal_bytes(wq_scales_dealt[:], wq_scales_raw[:], 1)
+        deal_words(w8_dealt[:], w8_raw[:])
+        make_operand(x_mx[0], x_raw[0])
+        banks = [bank(n) for n in range(BANKS)]
+        for n in range(QR_AHEAD):
+            qr_passes(banks[n], n, 0)
+        make_operand(x_mx[1], x_raw[1])
+        kc_round(on_scalar, 1, J - SCALAR_SHARE, J)
+        for n in range(BANKS):
+            qr_passes(banks[n], n, 1)
+            if n + QR_AHEAD < BANKS:
+                qr_passes(banks[n + QR_AHEAD], n + QR_AHEAD, 0)
+            nc.scalar.copy(
+                out=qr_mx[n // 4][0][:, PASS * (n % 4) : PASS * (n % 4 + 1)].rearrange("p (m t) -> p m t", t=PACK),
+                in_=banks[n][:].rearrange("p (t m) -> p m t", t=PACK),
+            )
+
+        kc_round(on_vector, 0, BANK, J)
+        quantize_columns(kc_mx[0], STEP, BANK)
+        quantize_columns(kc_mx[1], 0, BANK)
+        quantize_columns(kc_mx[0], BANK, J)
+        store_codes(0)
+        kc_round(on_vector, 1, BANK, J - SCALAR_SHARE)
+        qr_quantize(0)
+        quantize_columns(kc_mx[1], BANK, J)
+        store_codes(1)
+        for q in range(4):
+            queue = nc.gpsimd if q < 2 else nc.sync
+            queue.dma_start(
+                out=out_3[:, 4 * q : 4 * q + 4, :].rearrange("b r j -> r b j").bitcast(I32),
+                in_=kc_scales[32 * q : 32 * q + 4, :].rearrange("r (b j) -> r b j", b=2).bitcast(I32),
+            )
+
+        scores = [tile("scores%d" % u, [P, 2, J], F32) for u in range(2)]
+
+        def score_bank(g, h, engine):
+            acc = bank(2 * g + h)
+            keys = slice(BANK * h, BANK * (h + 1))
+            for b in range(2):
+                n = 2 * g + b
+                cols = slice(P * (n % 4), P * (n % 4 + 1))
+                nc.tensor.matmul_mx(
+                    out=acc[:],
+                    lhsT=qr_mx[n // 4][1][:, cols].bitcast(FP8X4),
+                    lhsT_scale=qr_mx[n // 4][2][:, cols],
+                    rhs=kc_mx[b][1][:, keys].bitcast(FP8X4),
+                    rhs_scale=kc_mx[b][2][:, keys],
+                    start=(b == 0),
+                    stop=(b == 1),
+                )
+            dst = scores[g // 2][:, g % 2, keys]
+            if engine == "vector":
+                nc.vector.tensor_scalar(
+                    out=dst, in0=acc[:], scalar1=0.0, scalar2=SCORE_SCALE, op0=ALU.max, op1=ALU.mult
+                )
+            else:
+                nc.scalar.activation(out=dst, in_=acc[:], func=ACT.Relu, scale=SCORE_SCALE)
+
+        def store_scores(u):
+            nc.sync.dma_start(
+                out=out_0[2 * P * u : 2 * P * (u + 1), :].rearrange("(e p) j -> p e j", p=P), in_=scores[u][:]
+            )
+
+        for g in range(4):
+            if g + 1 < 4:
+                qr_quantize(g + 1)
+            score_bank(g, 0, "scalar")
+            score_bank(g, 1, "vector")
+            if g % 2 == 1:
+                store_scores(g // 2)

@@ -60,13 +60,13 @@ def tile_mix_kvw_outl_relu_kernel(
         c_raw = {(a, n): tile("c_raw%d%d" % (a, n), [P, PACK, CHUNKS[n][1]], F32) for a in range(2) for n in range(3)}
         x_raw = [tile("x_raw%d" % a, [P, PACK, M], F32) for a in range(2)]
 
-        nc.gpsimd.memset(wk_scales_raw[:].bitcast(I32), 0)
+        nc.vector.memset(wk_scales_raw[:].bitcast(I32), 0)
         nc.vector.memset(wq_scales_raw[:].bitcast(I32), 0)
 
-        def load_scales(queue, dst, row, scales):
+        def load_scales(dst, row, scales):
             rows = 4 * scales.shape[0]
             for q in range(4):
-                queue.dma_start(
+                nc.sync.dma_start(
                     out=dst[32 * q + row : 32 * q + row + rows, :].bitcast(I32),
                     in_=scales[:, 4 * q : 4 * q + 4, :].bitcast(I32),
                 )
@@ -75,16 +75,17 @@ def tile_mix_kvw_outl_relu_kernel(
             j0, width = CHUNKS[n]
             nc.sync.dma_start(out=c_raw[a, n][:], in_=four_rows(c[PASS * a : PASS * (a + 1), j0 : j0 + width]))
 
-        load_scales(nc.gpsimd, wk_scales_raw, ROW_WK, wk_scales)
-        load_scales(nc.gpsimd, wq_scales_raw, ROW_W8, w8_scales)
-        load_scales(nc.gpsimd, wq_scales_raw, ROW_W4, w4_scales)
         nc.sync.dma_start(out=w4_raw[:].bitcast(I32), in_=w4_words[0].bitcast(I32))
+        load_scales(wk_scales_raw, ROW_WK, wk_scales)
         for a in range(2):
             load_c(a, 0)
             nc.sync.dma_start(out=wk_raw[a][:].bitcast(I32), in_=as_words(wk_words[a]))
-        for n in (1, 2):
-            for a in range(2):
-                load_c(a, n)
+        for a in range(2):
+            load_c(a, 1)
+        load_c(0, 2)
+        load_scales(wq_scales_raw, ROW_W8, w8_scales)
+        load_c(1, 2)
+        load_scales(wq_scales_raw, ROW_W4, w4_scales)
         nc.sync.dma_start(out=w8_raw[:].bitcast(I32), in_=as_words(w8_words[0]))
         for a in range(2):
             nc.sync.dma_start(out=x_raw[a][:], in_=four_rows(x[PASS * a : PASS * (a + 1), :]))
@@ -280,8 +281,7 @@ def tile_mix_kvw_outl_relu_kernel(
         quantize_columns(kc_mx[1], BANK, J)
         store_codes(1)
         for q in range(4):
-            queue = nc.gpsimd if q < 2 else nc.sync
-            queue.dma_start(
+            nc.sync.dma_start(
                 out=out_3[:, 4 * q : 4 * q + 4, :].rearrange("b r j -> r b j").bitcast(I32),
                 in_=kc_scales[32 * q : 32 * q + 4, :].rearrange("r (b j) -> r b j", b=2).bitcast(I32),
             )

@@ -9,6 +9,7 @@ F32 = mybir.dt.float32
 BF16 = mybir.dt.bfloat16
 I32 = mybir.dt.int32
 U32 = mybir.dt.uint32
+U16 = mybir.dt.uint16
 U8 = mybir.dt.uint8
 FP8X4 = mybir.dt.float8_e4m3fn_x4
 FP4X4 = mybir.dt.float4_e2m1fn_x4
@@ -71,24 +72,29 @@ def tile_mix_kvw_outl_relu_kernel(
                     in_=scales[:, 4 * q : 4 * q + 4, :].bitcast(I32),
                 )
 
+        def load_scale_rows(dst, row, scales):
+            for r in range(4):
+                nc.sync.dma_start(out=dst[row + r : P : 32, :].bitcast(I32), in_=scales[0, r:16:4, :].bitcast(I32))
+
         def load_c(a, n):
             j0, width = CHUNKS[n]
             nc.sync.dma_start(out=c_raw[a, n][:], in_=four_rows(c[PASS * a : PASS * (a + 1), j0 : j0 + width]))
 
-        nc.sync.dma_start(out=w4_raw[:].bitcast(I32), in_=w4_words[0].bitcast(I32))
+        load_c(0, 0)
         load_scales(wk_scales_raw, ROW_WK, wk_scales)
-        for a in range(2):
-            load_c(a, 0)
-            nc.sync.dma_start(out=wk_raw[a][:].bitcast(I32), in_=as_words(wk_words[a]))
+        nc.sync.dma_start(out=wk_raw[0][:].bitcast(I32), in_=as_words(wk_words[0]))
+        load_c(1, 0)
+        nc.sync.dma_start(out=wk_raw[1][:].bitcast(I32), in_=as_words(wk_words[1]))
         for a in range(2):
             load_c(a, 1)
         load_c(0, 2)
-        load_scales(wq_scales_raw, ROW_W8, w8_scales)
         load_c(1, 2)
-        load_scales(wq_scales_raw, ROW_W4, w4_scales)
+        load_scale_rows(wq_scales_raw, ROW_W8, w8_scales)
         nc.sync.dma_start(out=w8_raw[:].bitcast(I32), in_=as_words(w8_words[0]))
-        for a in range(2):
-            nc.sync.dma_start(out=x_raw[a][:], in_=four_rows(x[PASS * a : PASS * (a + 1), :]))
+        load_scale_rows(wq_scales_raw, ROW_W4, w4_scales)
+        nc.sync.dma_start(out=x_raw[0][:], in_=four_rows(x[0:PASS, :]))
+        nc.sync.dma_start(out=w4_raw[:].bitcast(I32), in_=w4_words[0].bitcast(I32))
+        nc.sync.dma_start(out=x_raw[1][:], in_=four_rows(x[PASS : 2 * PASS, :]))
 
         def deal_words(dst, src):
             nc.vector.tensor_copy(
@@ -96,10 +102,10 @@ def tile_mix_kvw_outl_relu_kernel(
                 in_=src.bitcast(I32).rearrange("p (b m t) -> p b m t", b=2, t=PACK),
             )
 
-        def deal_bytes(dst, src, per_column):
+        def deal_narrow(dst, src):
             nc.vector.tensor_copy(
-                out=dst.rearrange("p (b t m e) -> p b t m e", b=2, t=PACK, e=per_column),
-                in_=src.rearrange("p (b m t e) -> p b t m e", b=2, t=PACK, e=per_column),
+                out=dst.rearrange("p (b t m) -> p b t m", b=2, t=PACK),
+                in_=src.rearrange("p (b m t) -> p b t m", b=2, t=PACK),
             )
 
         def on_vector(out, in_):
@@ -144,47 +150,67 @@ def tile_mix_kvw_outl_relu_kernel(
 
         kc32 = [tile("kc32_%d" % b, [P, PACK, J], F32) for b in range(2)]
         kc_scales = tile("kc_scales", [P, 2 * J], U8)
+        kc_codes = tile("kc_codes", [P, 2 * J], U32)
         kc_mx = [
             (
                 tile("kc_rounded%d" % b, [P, PACK * J], BF16),
-                tile("kc_codes%d" % b, [P, J], U32),
+                kc_codes[:, J * b : J * (b + 1)],
                 kc_scales[:, J * b : J * (b + 1)],
             )
             for b in range(2)
         ]
 
+        def c_piece(a, n):
+            load = min(n, 2)
+            return c_mx[a, load], c_raw[a, load], STEP * n - CHUNKS[load][0]
+
+        def c_round(copy, a, n):
+            operand, raw, lo = c_piece(a, n)
+            round_columns(copy, operand[0], raw, lo, lo + STEP)
+
+        def c_quantize(a, n):
+            operand, raw, lo = c_piece(a, n)
+            quantize_columns(operand, lo, lo + STEP)
+
         def kc_pass(banks, n, a, i):
-            width = CHUNKS[n][1]
-            per_bank = BANK // width
-            place = i % per_bank
+            operand, raw, lo = c_piece(a, n)
+            place = i % 2
             cols = slice(P * i, P * (i + 1))
             nc.tensor.matmul_mx(
-                out=banks[i // per_bank][:, width * place : width * (place + 1)],
+                out=banks[i // 2][:, STEP * place : STEP * (place + 1)],
                 lhsT=wk_dealt[a][:, cols].bitcast(FP8X4),
                 lhsT_scale=wk_scales_dealt[ROW_WK + 4 * a :, cols],
-                rhs=c_mx[a, n][1][:].bitcast(FP8X4),
-                rhs_scale=c_mx[a, n][2][:],
+                rhs=operand[1][:, lo : lo + STEP].bitcast(FP8X4),
+                rhs_scale=operand[2][:, lo : lo + STEP],
                 start=(a == 0 and place == 0),
-                stop=(a == 1 and place == per_bank - 1),
+                stop=(a == 1 and place == 1),
             )
 
-        def kc_first_passes(n, first_bank):
-            banks = [bank(first_bank + u) for u in range(BANKS * CHUNKS[n][1] // BANK)]
+        def kc_first_passes(n):
+            banks = [bank(4 * (n % 2) + u) for u in range(4)]
             for i in range(D // P):
                 kc_pass(banks, n, 0, i)
             return banks
 
         def kc_second_passes(n, banks):
-            j0, width = CHUNKS[n]
-            per_bank = BANK // width
             for i in range(D // P):
                 kc_pass(banks, n, 1, i)
-                if i % per_bank == per_bank - 1:
-                    b, t = divmod(i - per_bank + 1, PACK)
+                if i % 2 == 1:
+                    b, t = divmod(i - 1, PACK)
                     nc.scalar.copy(
-                        out=kc32[b][:, t : t + per_bank, j0 : j0 + width],
-                        in_=banks[i // per_bank][:].rearrange("p (s j) -> p s j", s=per_bank),
+                        out=kc32[b][:, t : t + 2, STEP * n : STEP * (n + 1)],
+                        in_=banks[i // 2][:].rearrange("p (s j) -> p s j", s=2),
                     )
+
+        def kc_piece(copy, b, n):
+            kc_round(copy, b, STEP * n, STEP * (n + 1))
+
+        def x_operand(a):
+            for g in range(5):
+                if g < 4:
+                    round_columns(on_vector, x_mx[a][0], x_raw[a], P * g, P * (g + 1))
+                if g > 0:
+                    quantize_columns(x_mx[a], P * (g - 1), P * g)
 
         def kc_round(copy, b, lo, hi):
             round_columns(copy, kc_mx[b][0], kc32[b], lo, hi)
@@ -192,40 +218,11 @@ def tile_mix_kvw_outl_relu_kernel(
         def store_kc32(b, lo, hi):
             nc.sync.dma_start(out=four_rows(out_1[PASS * b : PASS * (b + 1), lo:hi]), in_=kc32[b][:, :, lo:hi])
 
-        def store_codes(b):
-            nc.sync.dma_start(out=as_words(out_2[b]), in_=kc_mx[b][1][:].bitcast(I32))
-
-        deal_bytes(w4_dealt[:], w4_raw[:], 2)
-        round_columns(on_vector, c_mx[0, 0][0], c_raw[0, 0], 0, STEP)
-        deal_words(wk_dealt[0][:], wk_raw[0][:])
-        quantize_columns(c_mx[0, 0], 0, STEP)
-        round_columns(on_scalar, c_mx[1, 0][0], c_raw[1, 0], 0, STEP)
-        deal_bytes(wk_scales_dealt[:], wk_scales_raw[:], 1)
-        banks = kc_first_passes(0, 0)
-        deal_words(wk_dealt[1][:], wk_raw[1][:])
-        quantize_columns(c_mx[1, 0], 0, STEP)
-        kc_second_passes(0, banks)
-
-        make_operand(c_mx[0, 1], c_raw[0, 1])
-        banks = kc_first_passes(1, BANKS // 2)
-        make_operand(c_mx[1, 1], c_raw[1, 1])
-        kc_second_passes(1, banks)
-        store_kc32(0, 0, BANK)
-
-        kc_round(on_vector, 0, 0, STEP)
-        round_columns(on_vector, c_mx[0, 2][0], c_raw[0, 2], 0, STEP)
-        quantize_columns(kc_mx[0], 0, STEP)
-        round_columns(on_vector, c_mx[0, 2][0], c_raw[0, 2], STEP, BANK)
-        quantize_columns(c_mx[0, 2], 0, STEP)
-        quantize_columns(c_mx[0, 2], STEP, BANK)
-        kc_round(on_scalar, 1, 0, STEP)
-        kc_round(on_scalar, 0, STEP, BANK)
-        kc_round(on_scalar, 1, STEP, BANK)
-        banks = kc_first_passes(2, 0)
-        make_operand(c_mx[1, 2], c_raw[1, 2])
-        kc_second_passes(2, banks)
-        store_kc32(0, BANK, J)
-        store_kc32(1, 0, J)
+        def store_codes():
+            nc.sync.dma_start(
+                out=out_2.rearrange("b p n t -> p b (n t)").bitcast(I32),
+                in_=kc_codes[:].bitcast(I32).rearrange("p (b n) -> p b n", b=2),
+            )
 
         qr_mx = [mx_operand("qr%d" % u, 4 * P) for u in range(2)]
 
@@ -254,42 +251,10 @@ def tile_mix_kvw_outl_relu_kernel(
             lo = 2 * P * (g % 2)
             quantize_columns(qr_mx[g // 2], lo, lo + 2 * P)
 
-        deal_bytes(wq_scales_dealt[:], wq_scales_raw[:], 1)
-        deal_words(w8_dealt[:], w8_raw[:])
-        make_operand(x_mx[0], x_raw[0])
-        banks = [bank(n) for n in range(BANKS)]
-        for n in range(QR_AHEAD):
-            qr_passes(banks[n], n, 0)
-        make_operand(x_mx[1], x_raw[1])
-        kc_round(on_scalar, 1, J - SCALAR_SHARE, J)
-        for n in range(BANKS):
-            qr_passes(banks[n], n, 1)
-            if n + QR_AHEAD < BANKS:
-                qr_passes(banks[n + QR_AHEAD], n + QR_AHEAD, 0)
-            nc.scalar.copy(
-                out=qr_mx[n // 4][0][:, PASS * (n % 4) : PASS * (n % 4 + 1)].rearrange("p (m t) -> p m t", t=PACK),
-                in_=banks[n][:].rearrange("p (t m) -> p m t", t=PACK),
-            )
-
-        kc_round(on_vector, 0, BANK, J)
-        quantize_columns(kc_mx[0], STEP, BANK)
-        quantize_columns(kc_mx[1], 0, BANK)
-        quantize_columns(kc_mx[0], BANK, J)
-        store_codes(0)
-        kc_round(on_vector, 1, BANK, J - SCALAR_SHARE)
-        qr_quantize(0)
-        quantize_columns(kc_mx[1], BANK, J)
-        store_codes(1)
-        for q in range(4):
-            nc.sync.dma_start(
-                out=out_3[:, 4 * q : 4 * q + 4, :].rearrange("b r j -> r b j").bitcast(I32),
-                in_=kc_scales[32 * q : 32 * q + 4, :].rearrange("r (b j) -> r b j", b=2).bitcast(I32),
-            )
-
         scores = [tile("scores%d" % u, [P, 2, J], F32) for u in range(2)]
 
-        def score_bank(g, h, engine):
-            acc = bank(2 * g + h)
+        def score_bank(g, h, engine, place):
+            acc = bank(place)
             keys = slice(BANK * h, BANK * (h + 1))
             for b in range(2):
                 n = 2 * g + b
@@ -316,10 +281,82 @@ def tile_mix_kvw_outl_relu_kernel(
                 out=out_0[2 * P * u : 2 * P * (u + 1), :].rearrange("(e p) j -> p e j", p=P), in_=scores[u][:]
             )
 
-        for g in range(4):
-            if g + 1 < 4:
-                qr_quantize(g + 1)
-            score_bank(g, 0, "scalar")
-            score_bank(g, 1, "vector")
-            if g % 2 == 1:
-                store_scores(g // 2)
+        def store_scales():
+            for r in range(4):
+                nc.sync.dma_start(
+                    out=out_3[:, r:16:4, :].rearrange("b q j -> q b j").bitcast(I32),
+                    in_=kc_scales[r:P:32, :].rearrange("q (b j) -> q b j", b=2).bitcast(I32),
+                )
+
+        def qr_copy(copy, banks, n):
+            copy(
+                qr_mx[n // 4][0][:, PASS * (n % 4) : PASS * (n % 4 + 1)].rearrange("p (m t) -> p m t", t=PACK),
+                banks[n][:].rearrange("p (t m) -> p m t", t=PACK),
+            )
+
+        def scalar_copy(out, in_):
+            nc.scalar.copy(out=out, in_=in_)
+
+        c_round(on_vector, 0, 0)
+        deal_narrow(wk_scales_dealt[:], wk_scales_raw[:])
+        c_quantize(0, 0)
+        deal_words(wk_dealt[0][:], wk_raw[0][:])
+        banks = kc_first_passes(0)
+        c_round(on_vector, 1, 0)
+        deal_words(wk_dealt[1][:], wk_raw[1][:])
+        c_quantize(1, 0)
+        kc_second_passes(0, banks)
+
+        make_operand(c_mx[0, 1], c_raw[0, 1])
+        banks = kc_first_passes(1)
+        make_operand(c_mx[1, 1], c_raw[1, 1])
+        kc_second_passes(1, banks)
+        store_kc32(1, 0, BANK)
+
+        kc_piece(on_vector, 0, 0)
+        make_operand(c_mx[0, 2], c_raw[0, 2])
+        kc_piece(on_scalar, 1, 0)
+        kc_piece(on_scalar, 0, 1)
+        banks = [kc_first_passes(n) for n in (2, 3)]
+        make_operand(c_mx[1, 2], c_raw[1, 2])
+        kc_second_passes(2, banks[0])
+        kc_second_passes(3, banks[1])
+        store_kc32(0, 0, J)
+        store_kc32(1, BANK, J)
+        kc_piece(on_vector, 1, 1)
+        deal_words(w8_dealt[:], w8_raw[:])
+        deal_narrow(wq_scales_dealt[:], wq_scales_raw[:])
+        quantize_columns(kc_mx[0], 0, BANK)
+
+        x_operand(0)
+        banks = [bank(n) for n in range(BANKS)]
+        for n in range(BANKS):
+            qr_passes(banks[n], n, 0)
+        quantize_columns(kc_mx[1], 0, BANK)
+        deal_narrow(w4_dealt[:].bitcast(U16), w4_raw[:].bitcast(U16))
+        kc_piece(on_scalar, 0, 2)
+        kc_piece(on_scalar, 1, 2)
+        x_operand(1)
+        for n in range(BANKS):
+            qr_passes(banks[n], n, 1)
+            qr_copy(scalar_copy, banks, n)
+        kc_piece(on_vector, 0, 3)
+        kc_piece(on_vector, 1, 3)
+        qr_quantize(0)
+        quantize_columns(kc_mx[0], BANK, J)
+        qr_quantize(1)
+        quantize_columns(kc_mx[1], BANK, J)
+        store_codes()
+        store_scales()
+        score_bank(0, 0, "vector", 0)
+        qr_quantize(2)
+        score_bank(1, 0, "vector", 1)
+        qr_quantize(3)
+        score_bank(0, 1, "scalar", 2)
+        score_bank(1, 1, "vector", 3)
+        store_scores(0)
+        score_bank(2, 0, "scalar", 4)
+        score_bank(2, 1, "vector", 5)
+        score_bank(3, 0, "scalar", 6)
+        score_bank(3, 1, "vector", 7)
+        store_scores(1)

@@ -26,7 +26,7 @@ SCORE_SCALE = 0.03125
 
 ROW_W4, ROW_W8, ROW_WK = 0, 4, 8
 
-CHUNKS = ((0, 256), (256, 256), (512, 512))
+CHUNKS = (((0, 256), (256, 256), (512, 512)),) * 2
 STEP = 256
 SCALAR_SHARE = 128
 QR_AHEAD = 5
@@ -58,7 +58,11 @@ def tile_mix_kvw_outl_relu_kernel(
         wk_raw = [tile("wk_raw%d" % a, [P, D], U32) for a in range(2)]
         w8_raw = tile("w8_raw", [P, D], U32)
         w4_raw = tile("w4_raw", [P, 2 * D], U8)
-        c_raw = {(a, n): tile("c_raw%d%d" % (a, n), [P, PACK, CHUNKS[n][1]], F32) for a in range(2) for n in range(3)}
+        c_raw = {
+            (a, n): tile("c_raw%d%d" % (a, n), [P, PACK, width], F32)
+            for a in range(2)
+            for n, (j0, width) in enumerate(CHUNKS[a])
+        }
         x_raw = [tile("x_raw%d" % a, [P, PACK, M], F32) for a in range(2)]
 
         nc.vector.memset(wk_scales_raw[:].bitcast(I32), 0)
@@ -77,24 +81,24 @@ def tile_mix_kvw_outl_relu_kernel(
                 nc.sync.dma_start(out=dst[row + r : P : 32, :].bitcast(I32), in_=scales[0, r:16:4, :].bitcast(I32))
 
         def load_c(a, n):
-            j0, width = CHUNKS[n]
+            j0, width = CHUNKS[a][n]
             nc.sync.dma_start(out=c_raw[a, n][:], in_=four_rows(c[PASS * a : PASS * (a + 1), j0 : j0 + width]))
 
-        load_c(0, 0)
+        nc.sync.dma_start(out=w4_raw[:].bitcast(I32), in_=w4_words[0].bitcast(I32))
         load_scales(wk_scales_raw, ROW_WK, wk_scales)
+        load_c(0, 0)
         nc.sync.dma_start(out=wk_raw[0][:].bitcast(I32), in_=as_words(wk_words[0]))
         load_c(1, 0)
         nc.sync.dma_start(out=wk_raw[1][:].bitcast(I32), in_=as_words(wk_words[1]))
-        for a in range(2):
-            load_c(a, 1)
+        load_c(0, 1)
+        load_c(1, 1)
         load_c(0, 2)
-        load_c(1, 2)
         load_scale_rows(wq_scales_raw, ROW_W8, w8_scales)
-        nc.sync.dma_start(out=w8_raw[:].bitcast(I32), in_=as_words(w8_words[0]))
+        load_c(1, 2)
         load_scale_rows(wq_scales_raw, ROW_W4, w4_scales)
-        nc.sync.dma_start(out=x_raw[0][:], in_=four_rows(x[0:PASS, :]))
-        nc.sync.dma_start(out=w4_raw[:].bitcast(I32), in_=w4_words[0].bitcast(I32))
-        nc.sync.dma_start(out=x_raw[1][:], in_=four_rows(x[PASS : 2 * PASS, :]))
+        nc.sync.dma_start(out=w8_raw[:].bitcast(I32), in_=as_words(w8_words[0]))
+        nc.sync.dma_start(out=x_raw[0][:], in_=four_rows(x[PASS * 0 : PASS * 1, :]))
+        nc.sync.dma_start(out=x_raw[1][:], in_=four_rows(x[PASS * 1 : PASS * 2, :]))
 
         def deal_words(dst, src):
             nc.vector.tensor_copy(
@@ -145,7 +149,7 @@ def tile_mix_kvw_outl_relu_kernel(
         w4_dealt = tile("w4_dealt", [P, 2 * D], U8)
         wk_scales_dealt = tile("wk_scales_dealt", [P, D], U8)
         wq_scales_dealt = tile("wq_scales_dealt", [P, D], U8)
-        c_mx = {(a, n): mx_operand("c%d%d" % (a, n), CHUNKS[n][1]) for a in range(2) for n in range(3)}
+        c_mx = [mx_operand("c%d" % a, J) for a in range(2)]
         x_mx = [mx_operand("x%d" % a, M) for a in range(2)]
 
         kc32 = [tile("kc32_%d" % b, [P, PACK, J], F32) for b in range(2)]
@@ -160,47 +164,71 @@ def tile_mix_kvw_outl_relu_kernel(
             for b in range(2)
         ]
 
-        def c_piece(a, n):
-            load = min(n, 2)
-            return c_mx[a, load], c_raw[a, load], STEP * n - CHUNKS[load][0]
-
-        def c_round(copy, a, n):
-            operand, raw, lo = c_piece(a, n)
-            round_columns(copy, operand[0], raw, lo, lo + STEP)
-
-        def c_quantize(a, n):
-            operand, raw, lo = c_piece(a, n)
-            quantize_columns(operand, lo, lo + STEP)
-
-        def kc_pass(banks, n, a, i):
-            operand, raw, lo = c_piece(a, n)
-            place = i % 2
-            cols = slice(P * i, P * (i + 1))
-            nc.tensor.matmul_mx(
-                out=banks[i // 2][:, STEP * place : STEP * (place + 1)],
-                lhsT=wk_dealt[a][:, cols].bitcast(FP8X4),
-                lhsT_scale=wk_scales_dealt[ROW_WK + 4 * a :, cols],
-                rhs=operand[1][:, lo : lo + STEP].bitcast(FP8X4),
-                rhs_scale=operand[2][:, lo : lo + STEP],
-                start=(a == 0 and place == 0),
-                stop=(a == 1 and place == 1),
+        def c_round(copy, a, lo, hi):
+            n = max(u for u, (j0, width) in enumerate(CHUNKS[a]) if j0 <= lo)
+            j0 = CHUNKS[a][n][0]
+            copy(
+                c_mx[a][0][:, PACK * lo : PACK * hi].rearrange("p (n i t) -> p n t i", i=LINE, t=PACK),
+                c_raw[a, n][:, :, lo - j0 : hi - j0].rearrange("p t (n i) -> p n t i", i=LINE),
             )
 
-        def kc_first_passes(n):
-            banks = [bank(4 * (n % 2) + u) for u in range(4)]
-            for i in range(D // P):
-                kc_pass(banks, n, 0, i)
+        def c_quantize(a, lo, hi):
+            quantize_columns(c_mx[a], lo, hi)
+
+        def c_operand(a, lo, hi):
+            mid = (lo + hi) // 2
+            c_round(on_vector, a, lo, mid)
+            c_round(on_vector, a, mid, hi)
+            c_quantize(a, lo, mid)
+            c_quantize(a, mid, hi)
+
+        def kc_pass(acc, lo, width, a, i):
+            per_bank = BANK // width
+            place = i % per_bank
+            cols = slice(P * i, P * (i + 1))
+            nc.tensor.matmul_mx(
+                out=acc[:, width * place : width * (place + 1)],
+                lhsT=wk_dealt[a][:, cols].bitcast(FP8X4),
+                lhsT_scale=wk_scales_dealt[ROW_WK + 4 * a :, cols],
+                rhs=c_mx[a][1][:, lo : lo + width].bitcast(FP8X4),
+                rhs_scale=c_mx[a][2][:, lo : lo + width],
+                start=(a == 0 and place == 0),
+                stop=(a == 1 and place == per_bank - 1),
+            )
+
+        def kc_bank_pass(acc, lo, width, a, u):
+            per_bank = BANK // width
+            for i in range(per_bank * u, per_bank * (u + 1)):
+                kc_pass(acc, lo, width, a, i)
+
+        def kc_drain(copy, acc, lo, width, u):
+            per_bank = BANK // width
+            b, t = divmod(per_bank * u, PACK)
+            copy(kc32[b][:, t : t + per_bank, lo : lo + width], acc[:].rearrange("p (s j) -> p s j", s=per_bank))
+
+        def kc_first_passes(lo, width, first_bank):
+            banks = [bank(first_bank + u) for u in range(BANKS * width // BANK)]
+            for u, acc in enumerate(banks):
+                kc_bank_pass(acc, lo, width, 0, u)
             return banks
 
-        def kc_second_passes(n, banks):
-            for i in range(D // P):
-                kc_pass(banks, n, 1, i)
-                if i % 2 == 1:
-                    b, t = divmod(i - 1, PACK)
-                    nc.scalar.copy(
-                        out=kc32[b][:, t : t + 2, STEP * n : STEP * (n + 1)],
-                        in_=banks[i // 2][:].rearrange("p (s j) -> p s j", s=2),
-                    )
+        def kc_second_passes(lo, width, banks):
+            for u, acc in enumerate(banks):
+                kc_bank_pass(acc, lo, width, 1, u)
+                kc_drain(scalar_copy, acc, lo, width, u)
+
+        def word_pass(acc, lo, a, b):
+            for t in range(PACK):
+                kc_pass(acc, lo, P, a, PACK * b + t)
+
+        def word_drain(acc, lo, b):
+            nc.scalar.copy(out=kc32[b][:, :, lo : lo + P], in_=acc[:].rearrange("p (t j) -> p t j", t=PACK))
+
+        def word_round(acc, lo, b):
+            nc.scalar.copy(
+                out=kc_mx[b][0][:, PACK * lo : PACK * (lo + P)].rearrange("p (j t) -> p j t", t=PACK),
+                in_=acc[:].rearrange("p (t j) -> p j t", t=PACK),
+            )
 
         def kc_piece(copy, b, n):
             kc_round(copy, b, STEP * n, STEP * (n + 1))
@@ -218,10 +246,10 @@ def tile_mix_kvw_outl_relu_kernel(
         def store_kc32(b, lo, hi):
             nc.sync.dma_start(out=four_rows(out_1[PASS * b : PASS * (b + 1), lo:hi]), in_=kc32[b][:, :, lo:hi])
 
-        def store_codes():
+        def store_codes(lo, hi):
             nc.sync.dma_start(
-                out=out_2.rearrange("b p n t -> p b (n t)").bitcast(I32),
-                in_=kc_codes[:].bitcast(I32).rearrange("p (b n) -> p b n", b=2),
+                out=out_2.rearrange("b p n t -> p b (n t)").bitcast(I32)[:, :, lo:hi],
+                in_=kc_codes[:].bitcast(I32).rearrange("p (b n) -> p b n", b=2)[:, :, lo:hi],
             )
 
         qr_mx = [mx_operand("qr%d" % u, 4 * P) for u in range(2)]
@@ -251,7 +279,7 @@ def tile_mix_kvw_outl_relu_kernel(
             lo = 2 * P * (g % 2)
             quantize_columns(qr_mx[g // 2], lo, lo + 2 * P)
 
-        scores = [tile("scores%d" % u, [P, 2, J], F32) for u in range(2)]
+        scores = tile("scores", [P, 4, J], F32)
 
         def score_bank(g, h, engine, place):
             acc = bank(place)
@@ -268,7 +296,7 @@ def tile_mix_kvw_outl_relu_kernel(
                     start=(b == 0),
                     stop=(b == 1),
                 )
-            dst = scores[g // 2][:, g % 2, keys]
+            dst = scores[:, g, keys]
             if engine == "vector":
                 nc.vector.tensor_scalar(
                     out=dst, in0=acc[:], scalar1=0.0, scalar2=SCORE_SCALE, op0=ALU.max, op1=ALU.mult
@@ -276,9 +304,9 @@ def tile_mix_kvw_outl_relu_kernel(
             else:
                 nc.scalar.activation(out=dst, in_=acc[:], func=ACT.Relu, scale=SCORE_SCALE)
 
-        def store_scores(u):
+        def store_scores(g0, g1, lo, hi):
             nc.sync.dma_start(
-                out=out_0[2 * P * u : 2 * P * (u + 1), :].rearrange("(e p) j -> p e j", p=P), in_=scores[u][:]
+                out=out_0[P * g0 : P * g1, lo:hi].rearrange("(g p) j -> p g j", p=P), in_=scores[:, g0:g1, lo:hi]
             )
 
         def store_scales():
@@ -297,66 +325,93 @@ def tile_mix_kvw_outl_relu_kernel(
         def scalar_copy(out, in_):
             nc.scalar.copy(out=out, in_=in_)
 
-        c_round(on_vector, 0, 0)
+        deal_narrow(w4_dealt[:].bitcast(U16), w4_raw[:].bitcast(U16))
         deal_narrow(wk_scales_dealt[:], wk_scales_raw[:])
-        c_quantize(0, 0)
+        c_round(on_vector, 0, 0, 256)
         deal_words(wk_dealt[0][:], wk_raw[0][:])
-        banks = kc_first_passes(0)
-        c_round(on_vector, 1, 0)
+        c_quantize(0, 0, 256)
+        banks = [bank(u) for u in range(4)]
+        for u in range(4):
+            word_pass(banks[u], P * (u % 2), 0, u // 2)
+        c_round(on_vector, 1, 0, 256)
         deal_words(wk_dealt[1][:], wk_raw[1][:])
-        c_quantize(1, 0)
-        kc_second_passes(0, banks)
-
-        make_operand(c_mx[0, 1], c_raw[0, 1])
-        banks = kc_first_passes(1)
-        make_operand(c_mx[1, 1], c_raw[1, 1])
-        kc_second_passes(1, banks)
+        c_quantize(1, 0, 256)
+        for u in range(4):
+            word_pass(banks[u], P * (u % 2), 1, u // 2)
+            word_drain(banks[u], P * (u % 2), u // 2)
+        for u in (3,):
+            word_round(banks[u], P * (u % 2), u // 2)
+        c_operand(0, 256, 512)
+        banks = [bank(4 + u) for u in range(4)]
+        for u in range(4):
+            word_pass(banks[u], 256 + P * (u // 2), 0, u % 2)
+        c_operand(1, 256, 512)
+        for u in range(4):
+            word_pass(banks[u], 256 + P * (u // 2), 1, u % 2)
+            word_drain(banks[u], 256 + P * (u // 2), u % 2)
+            if u > 0:
+                word_round(banks[u - 1], 256 + P * ((u - 1) // 2), (u - 1) % 2)
+        word_round(banks[3], 256 + P, 1)
         store_kc32(1, 0, BANK)
-
         kc_piece(on_vector, 0, 0)
-        make_operand(c_mx[0, 2], c_raw[0, 2])
-        kc_piece(on_scalar, 1, 0)
-        kc_piece(on_scalar, 0, 1)
-        banks = [kc_first_passes(n) for n in (2, 3)]
-        make_operand(c_mx[1, 2], c_raw[1, 2])
-        kc_second_passes(2, banks[0])
-        kc_second_passes(3, banks[1])
-        store_kc32(0, 0, J)
+        kc_round(on_vector, 1, 0, P)
+        c_round(on_vector, 0, 512, 768)
+        c_round(on_vector, 0, 768, 1024)
+        c_quantize(0, 512, 768)
+        banks0 = kc_first_passes(512, 256, 0)
+        c_quantize(0, 768, 1024)
+        quantize_columns(kc_mx[0], 0, 256)
+        c_round(on_vector, 1, 512, 768)
+        quantize_columns(kc_mx[1], 0, 256)
+        c_quantize(1, 512, 768)
+        c_round(on_vector, 1, 768, 1024)
+        quantize_columns(kc_mx[0], 256, 512)
+        c_quantize(1, 768, 1024)
+        banks1 = [bank(4 + u) for u in range(4)]
+        for b in range(2):
+            for u in (2 * b, 2 * b + 1):
+                kc_bank_pass(banks0[u], 512, 256, 1, u)
+                kc_drain(scalar_copy, banks0[u], 512, 256, u)
+            for u in (2 * b, 2 * b + 1):
+                word_pass(banks1[u], 768 + P * (u % 2), 0, b)
+                word_pass(banks1[u], 768 + P * (u % 2), 1, b)
+                word_drain(banks1[u], 768 + P * (u % 2), b)
+            if b == 0:
+                store_kc32(0, 0, J)
         store_kc32(1, BANK, J)
-        kc_piece(on_vector, 1, 1)
+        for u in (2, 3):
+            word_round(banks1[u], 768 + P * (u % 2), u // 2)
         deal_words(w8_dealt[:], w8_raw[:])
         deal_narrow(wq_scales_dealt[:], wq_scales_raw[:])
-        quantize_columns(kc_mx[0], 0, BANK)
 
         x_operand(0)
         banks = [bank(n) for n in range(BANKS)]
-        for n in range(BANKS):
+        for n in range(QR_AHEAD):
             qr_passes(banks[n], n, 0)
-        quantize_columns(kc_mx[1], 0, BANK)
-        deal_narrow(w4_dealt[:].bitcast(U16), w4_raw[:].bitcast(U16))
-        kc_piece(on_scalar, 0, 2)
-        kc_piece(on_scalar, 1, 2)
         x_operand(1)
         for n in range(BANKS):
             qr_passes(banks[n], n, 1)
+            if n + QR_AHEAD < BANKS:
+                qr_passes(banks[n + QR_AHEAD], n + QR_AHEAD, 0)
             qr_copy(scalar_copy, banks, n)
-        kc_piece(on_vector, 0, 3)
-        kc_piece(on_vector, 1, 3)
+        kc_round(on_vector, 0, BANK, J)
+        quantize_columns(kc_mx[1], 256, 512)
+        kc_round(on_vector, 1, BANK, 768)
         qr_quantize(0)
+        score_bank(0, 0, "scalar", 0)
         quantize_columns(kc_mx[0], BANK, J)
         qr_quantize(1)
+        score_bank(1, 0, "scalar", 1)
         quantize_columns(kc_mx[1], BANK, J)
-        store_codes()
+        store_codes(0, J)
         store_scales()
-        score_bank(0, 0, "vector", 0)
         qr_quantize(2)
-        score_bank(1, 0, "vector", 1)
         qr_quantize(3)
-        score_bank(0, 1, "scalar", 2)
+        score_bank(0, 1, "vector", 2)
         score_bank(1, 1, "vector", 3)
-        store_scores(0)
+        store_scores(0, 2, 0, J)
         score_bank(2, 0, "scalar", 4)
         score_bank(2, 1, "vector", 5)
         score_bank(3, 0, "scalar", 6)
         score_bank(3, 1, "vector", 7)
-        store_scores(1)
+        store_scores(2, 4, 0, J)

@@ -24,9 +24,9 @@ BANKS = 8
 LINE = 4
 SCORE_SCALE = 0.03125
 
-ROW_W4, ROW_W8, ROW_WK = 0, 4, 8
+ROW_W4, ROW_W8, ROW_WK = 0, 4, 0
 
-CHUNKS = (((0, 256), (256, 256), (512, 512)),) * 2
+CHUNKS = (((0, 1024),), ((0, 256), (256, 512), (768, 256)))
 STEP = 256
 SCALAR_SHARE = 128
 QR_AHEAD = 5
@@ -53,7 +53,7 @@ def tile_mix_kvw_outl_relu_kernel(
         def four_rows(rows):
             return rows.rearrange("(p t) n -> p t n", t=PACK)
 
-        wk_scales_raw = tile("wk_scales_raw", [P, D], U8)
+        wk_scales_raw = tile("wk_scales_raw", [P, 2 * D], U8)
         wq_scales_raw = tile("wq_scales_raw", [P, D], U8)
         wk_raw = [tile("wk_raw%d" % a, [P, D], U32) for a in range(2)]
         w8_raw = tile("w8_raw", [P, D], U32)
@@ -69,16 +69,11 @@ def tile_mix_kvw_outl_relu_kernel(
         nc.vector.memset(wq_scales_raw[:].bitcast(I32), 0)
 
         def load_scales(dst, row, scales):
-            rows = 4 * scales.shape[0]
-            for q in range(4):
-                nc.sync.dma_start(
-                    out=dst[32 * q + row : 32 * q + row + rows, :].bitcast(I32),
-                    in_=scales[:, 4 * q : 4 * q + 4, :].bitcast(I32),
-                )
-
-        def load_scale_rows(dst, row, scales):
             for r in range(4):
-                nc.sync.dma_start(out=dst[row + r : P : 32, :].bitcast(I32), in_=scales[0, r:16:4, :].bitcast(I32))
+                nc.sync.dma_start(
+                    out=dst[row + r : P : 32, :].rearrange("q (a d) -> q a d", d=D).bitcast(I32),
+                    in_=scales[:, r:16:4, :].rearrange("a q d -> q a d").bitcast(I32),
+                )
 
         def load_c(a, n):
             j0, width = CHUNKS[a][n]
@@ -87,15 +82,13 @@ def tile_mix_kvw_outl_relu_kernel(
         nc.sync.dma_start(out=w4_raw[:].bitcast(I32), in_=w4_words[0].bitcast(I32))
         load_scales(wk_scales_raw, ROW_WK, wk_scales)
         load_c(0, 0)
+        load_scales(wq_scales_raw, ROW_W8, w8_scales)
         nc.sync.dma_start(out=wk_raw[0][:].bitcast(I32), in_=as_words(wk_words[0]))
-        load_c(1, 0)
         nc.sync.dma_start(out=wk_raw[1][:].bitcast(I32), in_=as_words(wk_words[1]))
-        load_c(0, 1)
+        load_c(1, 0)
+        load_scales(wq_scales_raw, ROW_W4, w4_scales)
         load_c(1, 1)
-        load_c(0, 2)
-        load_scale_rows(wq_scales_raw, ROW_W8, w8_scales)
         load_c(1, 2)
-        load_scale_rows(wq_scales_raw, ROW_W4, w4_scales)
         nc.sync.dma_start(out=w8_raw[:].bitcast(I32), in_=as_words(w8_words[0]))
         nc.sync.dma_start(out=x_raw[0][:], in_=four_rows(x[PASS * 0 : PASS * 1, :]))
         nc.sync.dma_start(out=x_raw[1][:], in_=four_rows(x[PASS * 1 : PASS * 2, :]))
@@ -108,8 +101,8 @@ def tile_mix_kvw_outl_relu_kernel(
 
         def deal_narrow(dst, src):
             nc.vector.tensor_copy(
-                out=dst.rearrange("p (b t m) -> p b t m", b=2, t=PACK),
-                in_=src.rearrange("p (b m t) -> p b t m", b=2, t=PACK),
+                out=dst.rearrange("p (b t m) -> p b t m", m=P, t=PACK),
+                in_=src.rearrange("p (b m t) -> p b t m", m=P, t=PACK),
             )
 
         def on_vector(out, in_):
@@ -147,7 +140,7 @@ def tile_mix_kvw_outl_relu_kernel(
         wk_dealt = [tile("wk_dealt%d" % a, [P, D], U32) for a in range(2)]
         w8_dealt = tile("w8_dealt", [P, D], U32)
         w4_dealt = tile("w4_dealt", [P, 2 * D], U8)
-        wk_scales_dealt = tile("wk_scales_dealt", [P, D], U8)
+        wk_scales_dealt = tile("wk_scales_dealt", [P, 2 * D], U8)
         wq_scales_dealt = tile("wq_scales_dealt", [P, D], U8)
         c_mx = [mx_operand("c%d" % a, J) for a in range(2)]
         x_mx = [mx_operand("x%d" % a, M) for a in range(2)]
@@ -189,7 +182,7 @@ def tile_mix_kvw_outl_relu_kernel(
             nc.tensor.matmul_mx(
                 out=acc[:, width * place : width * (place + 1)],
                 lhsT=wk_dealt[a][:, cols].bitcast(FP8X4),
-                lhsT_scale=wk_scales_dealt[ROW_WK + 4 * a :, cols],
+                lhsT_scale=wk_scales_dealt[:, D * a + P * i : D * a + P * (i + 1)],
                 rhs=c_mx[a][1][:, lo : lo + width].bitcast(FP8X4),
                 rhs_scale=c_mx[a][2][:, lo : lo + width],
                 start=(a == 0 and place == 0),
@@ -233,12 +226,21 @@ def tile_mix_kvw_outl_relu_kernel(
         def kc_piece(copy, b, n):
             kc_round(copy, b, STEP * n, STEP * (n + 1))
 
+        def x_round(a, u, lo, hi):
+            dst = x_mx[a][0][:, 2 * PASS * u : 2 * PASS * (u + 1)].rearrange("p (e n t) -> p e n t", e=2, t=PACK)
+            nc.vector.tensor_copy(
+                out=dst[:, :, lo:hi, :].rearrange("p e (n i) t -> p n t i e", i=2),
+                in_=x_raw[a][:, :, 2 * (P * u + lo) : 2 * (P * u + hi)].rearrange("p t (n i e) -> p n t i e", i=2, e=2),
+            )
+
         def x_operand(a):
-            for g in range(5):
-                if g < 4:
-                    round_columns(on_vector, x_mx[a][0], x_raw[a], P * g, P * (g + 1))
-                if g > 0:
-                    quantize_columns(x_mx[a], P * (g - 1), P * g)
+            x_round(a, 0, 0, P)
+            x_round(a, 1, 0, P // 2)
+            quantize_columns(x_mx[a], 0, 2 * P)
+            x_round(a, 1, P // 2, P)
+
+        def x_finish(a):
+            quantize_columns(x_mx[a], 2 * P, 4 * P)
 
         def kc_round(copy, b, lo, hi):
             round_columns(copy, kc_mx[b][0], kc32[b], lo, hi)
@@ -306,7 +308,7 @@ def tile_mix_kvw_outl_relu_kernel(
 
         def store_scores(g0, g1, lo, hi):
             nc.sync.dma_start(
-                out=out_0[P * g0 : P * g1, lo:hi].rearrange("(g p) j -> p g j", p=P), in_=scores[:, g0:g1, lo:hi]
+                out=out_0[P * g0 : P * g1, lo:hi].rearrange("(p e) j -> p e j", p=P), in_=scores[:, g0:g1, lo:hi]
             )
 
         def store_scales():
@@ -325,93 +327,111 @@ def tile_mix_kvw_outl_relu_kernel(
         def scalar_copy(out, in_):
             nc.scalar.copy(out=out, in_=in_)
 
+        def words(n, a, b, banks):
+            for v in range(2):
+                word_pass(banks[v], STEP * n + P * v, a, b)
+
+        def drains(n, b, banks):
+            for v in range(2):
+                word_drain(banks[v], STEP * n + P * v, b)
+
+        def rounds(n, b, banks):
+            for v in range(2):
+                word_round(banks[v], STEP * n + P * v, b)
+
+        def store_rows(b, t0, t1):
+            nc.sync.dma_start(out=four_rows(out_1[PASS * b : PASS * (b + 1), :])[:, t0:t1, :], in_=kc32[b][:, t0:t1, :])
+
+        def pair(u):
+            return [bank(2 * u), bank(2 * u + 1)]
+
+        def low_pass(n, a, banks):
+            for u in range(2):
+                kc_bank_pass(banks[u], STEP * n, STEP, a, u)
+
+        def low_drains(n, banks):
+            for u in range(2):
+                kc_drain(scalar_copy, banks[u], STEP * n, STEP, u)
+
+        def high(n, banks, rounded):
+            words(n, 0, 1, banks)
+            words(n, 1, 1, banks)
+            drains(n, 1, banks)
+            if rounded:
+                rounds(n, 1, banks)
+
         deal_narrow(w4_dealt[:].bitcast(U16), w4_raw[:].bitcast(U16))
+        c_round(on_scalar, 0, 512, 768)
+        c_round(on_scalar, 0, 768, 1024)
         deal_narrow(wk_scales_dealt[:], wk_scales_raw[:])
         c_round(on_vector, 0, 0, 256)
+        c_round(on_vector, 0, 256, 512)
         deal_words(wk_dealt[0][:], wk_raw[0][:])
-        c_quantize(0, 0, 256)
-        banks = [bank(u) for u in range(4)]
-        for u in range(4):
-            word_pass(banks[u], P * (u % 2), 0, u // 2)
-        c_round(on_vector, 1, 0, 256)
+        c_quantize(0, 0, 512)
         deal_words(wk_dealt[1][:], wk_raw[1][:])
-        c_quantize(1, 0, 256)
-        for u in range(4):
-            word_pass(banks[u], P * (u % 2), 1, u // 2)
-            word_drain(banks[u], P * (u % 2), u // 2)
-        for u in (3,):
-            word_round(banks[u], P * (u % 2), u // 2)
-        c_operand(0, 256, 512)
-        banks = [bank(4 + u) for u in range(4)]
-        for u in range(4):
-            word_pass(banks[u], 256 + P * (u // 2), 0, u % 2)
-        c_operand(1, 256, 512)
-        for u in range(4):
-            word_pass(banks[u], 256 + P * (u // 2), 1, u % 2)
-            word_drain(banks[u], 256 + P * (u // 2), u % 2)
-            if u > 0:
-                word_round(banks[u - 1], 256 + P * ((u - 1) // 2), (u - 1) % 2)
-        word_round(banks[3], 256 + P, 1)
-        store_kc32(1, 0, BANK)
-        kc_piece(on_vector, 0, 0)
-        kc_round(on_vector, 1, 0, P)
-        c_round(on_vector, 0, 512, 768)
-        c_round(on_vector, 0, 768, 1024)
-        c_quantize(0, 512, 768)
-        banks0 = kc_first_passes(512, 256, 0)
-        c_quantize(0, 768, 1024)
-        quantize_columns(kc_mx[0], 0, 256)
-        c_round(on_vector, 1, 512, 768)
-        quantize_columns(kc_mx[1], 0, 256)
-        c_quantize(1, 512, 768)
-        c_round(on_vector, 1, 768, 1024)
-        quantize_columns(kc_mx[0], 256, 512)
-        c_quantize(1, 768, 1024)
-        banks1 = [bank(4 + u) for u in range(4)]
-        for b in range(2):
-            for u in (2 * b, 2 * b + 1):
-                kc_bank_pass(banks0[u], 512, 256, 1, u)
-                kc_drain(scalar_copy, banks0[u], 512, 256, u)
-            for u in (2 * b, 2 * b + 1):
-                word_pass(banks1[u], 768 + P * (u % 2), 0, b)
-                word_pass(banks1[u], 768 + P * (u % 2), 1, b)
-                word_drain(banks1[u], 768 + P * (u % 2), b)
-            if b == 0:
-                store_kc32(0, 0, J)
-        store_kc32(1, BANK, J)
-        for u in (2, 3):
-            word_round(banks1[u], 768 + P * (u % 2), u // 2)
-        deal_words(w8_dealt[:], w8_raw[:])
+        low = [pair(n) for n in range(3)]
+        low_pass(0, 0, low[0])
+        banks = pair(3)
+        words(0, 0, 1, banks)
+        c_quantize(0, 512, 1024)
+        c_operand(1, 0, 256)
+        low_pass(0, 1, low[0])
+        low_drains(0, low[0])
+        words(0, 1, 1, banks)
+        drains(0, 1, banks)
+        word_round(banks[0], 0, 1)
+        low_pass(1, 0, low[1])
+        low_pass(2, 0, low[2])
+        low.append(pair(0))
+        low_pass(3, 0, low[3])
         deal_narrow(wq_scales_dealt[:], wq_scales_raw[:])
+        for n in (1, 2, 3):
+            c_operand(1, STEP * n, STEP * (n + 1))
+            low_pass(n, 1, low[n])
+            low_drains(n, low[n])
+        store_rows(0, 0, 2)
+        store_rows(0, 2, 4)
+        for n in (1, 2, 3):
+            high(n, pair((3, 1, 2)[n - 1]), n in (1, 3))
+        store_kc32(1, 0, J)
+        deal_words(w8_dealt[:], w8_raw[:])
+        kc_round(on_vector, 0, 0, BANK)
 
         x_operand(0)
-        banks = [bank(n) for n in range(BANKS)]
+        quantize_columns(kc_mx[0], 0, BANK)
+        x_finish(0)
+        order = (0, 3, 1, 2)
+        banks = [bank(2 * order[n // 2] + n % 2) for n in range(BANKS)]
         for n in range(QR_AHEAD):
             qr_passes(banks[n], n, 0)
         x_operand(1)
+        kc_piece(on_vector, 0, 2)
+        x_finish(1)
         for n in range(BANKS):
             qr_passes(banks[n], n, 1)
             if n + QR_AHEAD < BANKS:
                 qr_passes(banks[n + QR_AHEAD], n + QR_AHEAD, 0)
             qr_copy(scalar_copy, banks, n)
-        kc_round(on_vector, 0, BANK, J)
-        quantize_columns(kc_mx[1], 256, 512)
-        kc_round(on_vector, 1, BANK, 768)
-        qr_quantize(0)
-        score_bank(0, 0, "scalar", 0)
+        kc_piece(on_vector, 0, 3)
+        kc_piece(on_vector, 1, 2)
+        kc_round(on_vector, 1, P, STEP)
         quantize_columns(kc_mx[0], BANK, J)
+        quantize_columns(kc_mx[1], 0, BANK)
+        qr_quantize(0)
+        place = [2 * order[n // 2] + n % 2 for n in range(BANKS)]
+        score_bank(0, 0, "scalar", place[0])
         qr_quantize(1)
-        score_bank(1, 0, "scalar", 1)
+        score_bank(1, 0, "scalar", place[1])
         quantize_columns(kc_mx[1], BANK, J)
         store_codes(0, J)
         store_scales()
         qr_quantize(2)
         qr_quantize(3)
-        score_bank(0, 1, "vector", 2)
-        score_bank(1, 1, "vector", 3)
+        score_bank(0, 1, "vector", place[2])
+        score_bank(1, 1, "vector", place[3])
         store_scores(0, 2, 0, J)
-        score_bank(2, 0, "scalar", 4)
-        score_bank(2, 1, "vector", 5)
-        score_bank(3, 0, "scalar", 6)
-        score_bank(3, 1, "vector", 7)
+        score_bank(2, 0, "scalar", place[4])
+        score_bank(2, 1, "vector", place[5])
+        score_bank(3, 0, "scalar", place[6])
+        score_bank(3, 1, "vector", place[7])
         store_scores(2, 4, 0, J)

@@ -55,7 +55,7 @@ def tile_mix_kvw_outl_relu_kernel(
 
         wk_scales_raw = tile("wk_scales_raw", [P, 2 * D], U8)
         wq_scales_raw = tile("wq_scales_raw", [P, D], U8)
-        wk_raw = [tile("wk_raw%d" % a, [P, D], U32) for a in range(2)]
+        wk_raw = [tile("wk_raw%d" % b, [P, 2, PASS], U32) for b in range(2)]
         w8_raw = tile("w8_raw", [P, D], U32)
         w4_raw = tile("w4_raw", [P, 2 * D], U8)
         c_raw = {
@@ -68,12 +68,16 @@ def tile_mix_kvw_outl_relu_kernel(
         nc.vector.memset(wk_scales_raw[:].bitcast(I32), 0)
         nc.vector.memset(wq_scales_raw[:].bitcast(I32), 0)
 
-        def load_scales(dst, row, scales):
+        def load_scales(dst, row, scales, queue=nc.sync):
             for r in range(4):
-                nc.sync.dma_start(
+                queue.dma_start(
                     out=dst[row + r : P : 32, :].rearrange("q (a d) -> q a d", d=D).bitcast(I32),
                     in_=scales[:, r:16:4, :].rearrange("a q d -> q a d").bitcast(I32),
                 )
+
+        def load_wk(b):
+            words = wk_words.rearrange("a p n t -> p a (n t)").bitcast(I32)
+            nc.sync.dma_start(out=wk_raw[b][:].bitcast(I32), in_=words[:, :, PASS * b : PASS * (b + 1)])
 
         def load_c(a, n):
             j0, width = CHUNKS[a][n]
@@ -83,9 +87,9 @@ def tile_mix_kvw_outl_relu_kernel(
         load_scales(wk_scales_raw, ROW_WK, wk_scales)
         load_c(0, 0)
         load_scales(wq_scales_raw, ROW_W8, w8_scales)
-        nc.sync.dma_start(out=wk_raw[0][:].bitcast(I32), in_=as_words(wk_words[0]))
-        nc.sync.dma_start(out=wk_raw[1][:].bitcast(I32), in_=as_words(wk_words[1]))
+        load_wk(0)
         load_c(1, 0)
+        load_wk(1)
         load_scales(wq_scales_raw, ROW_W4, w4_scales)
         load_c(1, 1)
         load_c(1, 2)
@@ -137,7 +141,7 @@ def tile_mix_kvw_outl_relu_kernel(
             for lo in (0, half):
                 quantize_columns(operand, lo, lo + half)
 
-        wk_dealt = [tile("wk_dealt%d" % a, [P, D], U32) for a in range(2)]
+        wk_dealt = [tile("wk_dealt%d" % b, [P, 2 * PASS], U32) for b in range(2)]
         w8_dealt = tile("w8_dealt", [P, D], U32)
         w4_dealt = tile("w4_dealt", [P, 2 * D], U8)
         wk_scales_dealt = tile("wk_scales_dealt", [P, 2 * D], U8)
@@ -181,7 +185,7 @@ def tile_mix_kvw_outl_relu_kernel(
             cols = slice(P * i, P * (i + 1))
             nc.tensor.matmul_mx(
                 out=acc[:, width * place : width * (place + 1)],
-                lhsT=wk_dealt[a][:, cols].bitcast(FP8X4),
+                lhsT=wk_dealt[i // PACK][:, PASS * a + P * (i % PACK) : PASS * a + P * (i % PACK + 1)].bitcast(FP8X4),
                 lhsT_scale=wk_scales_dealt[:, D * a + P * i : D * a + P * (i + 1)],
                 rhs=c_mx[a][1][:, lo : lo + width].bitcast(FP8X4),
                 rhs_scale=c_mx[a][2][:, lo : lo + width],
@@ -342,6 +346,9 @@ def tile_mix_kvw_outl_relu_kernel(
         def store_rows(b, t0, t1):
             nc.sync.dma_start(out=four_rows(out_1[PASS * b : PASS * (b + 1), :])[:, t0:t1, :], in_=kc32[b][:, t0:t1, :])
 
+        def store_half_codes(b):
+            nc.sync.dma_start(out=as_words(out_2[b]), in_=kc_mx[b][1].bitcast(I32))
+
         def pair(u):
             return [bank(2 * u), bank(2 * u + 1)]
 
@@ -366,36 +373,43 @@ def tile_mix_kvw_outl_relu_kernel(
         deal_narrow(wk_scales_dealt[:], wk_scales_raw[:])
         c_round(on_vector, 0, 0, 256)
         c_round(on_vector, 0, 256, 512)
-        deal_words(wk_dealt[0][:], wk_raw[0][:])
-        c_quantize(0, 0, 512)
-        deal_words(wk_dealt[1][:], wk_raw[1][:])
+        c_quantize(0, 0, 256)
+        deal_words(wk_dealt[0][:], wk_raw[0][:].rearrange("p a n -> p (a n)"))
         low = [pair(n) for n in range(3)]
-        low_pass(0, 0, low[0])
+        words(0, 0, 0, low[0])
+        c_operand(1, 0, 256)
+        words(0, 1, 0, low[0])
+        drains(0, 0, low[0])
+        word_round(low[0][0], 0, 0)
+        c_quantize(0, 256, 512)
+        low_pass(1, 0, low[1])
+        deal_words(wk_dealt[1][:], wk_raw[1][:].rearrange("p a n -> p (a n)"))
         banks = pair(3)
         words(0, 0, 1, banks)
-        c_quantize(0, 512, 1024)
-        c_operand(1, 0, 256)
-        low_pass(0, 1, low[0])
-        low_drains(0, low[0])
         words(0, 1, 1, banks)
         drains(0, 1, banks)
-        word_round(banks[0], 0, 1)
-        low_pass(1, 0, low[1])
+        rounds(0, 1, banks)
+        c_quantize(0, 512, 1024)
         low_pass(2, 0, low[2])
         low.append(pair(0))
         low_pass(3, 0, low[3])
         deal_narrow(wq_scales_dealt[:], wq_scales_raw[:])
+        kc_round(on_vector, 0, 128, 256)
         for n in (1, 2, 3):
             c_operand(1, STEP * n, STEP * (n + 1))
             low_pass(n, 1, low[n])
             low_drains(n, low[n])
         store_rows(0, 0, 2)
         store_rows(0, 2, 4)
+        held = {n: pair((3, 1, 2)[n - 1]) for n in (1, 2, 3)}
         for n in (1, 2, 3):
-            high(n, pair((3, 1, 2)[n - 1]), n in (1, 3))
+            high(n, held[n], n in ())
         store_kc32(1, 0, J)
+        for n in (3,):
+            rounds(n, 1, held[n])
         deal_words(w8_dealt[:], w8_raw[:])
-        kc_round(on_vector, 0, 0, BANK)
+        kc_piece(on_vector, 0, 1)
+        kc_piece(on_vector, 0, 2)
 
         x_operand(0)
         quantize_columns(kc_mx[0], 0, BANK)
@@ -405,29 +419,29 @@ def tile_mix_kvw_outl_relu_kernel(
         for n in range(QR_AHEAD):
             qr_passes(banks[n], n, 0)
         x_operand(1)
-        kc_piece(on_vector, 0, 2)
+        kc_piece(on_vector, 1, 1)
         x_finish(1)
         for n in range(BANKS):
             qr_passes(banks[n], n, 1)
             if n + QR_AHEAD < BANKS:
                 qr_passes(banks[n + QR_AHEAD], n + QR_AHEAD, 0)
             qr_copy(scalar_copy, banks, n)
-        kc_piece(on_vector, 0, 3)
-        kc_piece(on_vector, 1, 2)
-        kc_round(on_vector, 1, P, STEP)
-        quantize_columns(kc_mx[0], BANK, J)
-        quantize_columns(kc_mx[1], 0, BANK)
-        qr_quantize(0)
         place = [2 * order[n // 2] + n % 2 for n in range(BANKS)]
+        kc_piece(on_vector, 0, 3)
+        quantize_columns(kc_mx[1], 0, 512)
+        kc_piece(on_vector, 1, 2)
+        qr_quantize(0)
         score_bank(0, 0, "scalar", place[0])
+        quantize_columns(kc_mx[0], BANK, J)
+        store_half_codes(0)
         qr_quantize(1)
         score_bank(1, 0, "scalar", place[1])
         quantize_columns(kc_mx[1], BANK, J)
-        store_codes(0, J)
+        store_half_codes(1)
         store_scales()
         qr_quantize(2)
-        qr_quantize(3)
         score_bank(0, 1, "vector", place[2])
+        qr_quantize(3)
         score_bank(1, 1, "vector", place[3])
         store_scores(0, 2, 0, J)
         score_bank(2, 0, "scalar", place[4])

@@ -317,7 +317,7 @@ def tile_mix_kvw_outl_relu_kernel(
 
         def store_scales():
             for r in range(4):
-                nc.sync.dma_start(
+                nc.gpsimd.dma_start(
                     out=out_3[:, r:16:4, :].rearrange("b q j -> q b j").bitcast(I32),
                     in_=kc_scales[r:P:32, :].rearrange("q (b j) -> q b j", b=2).bitcast(I32),
                 )
@@ -380,7 +380,7 @@ def tile_mix_kvw_outl_relu_kernel(
         c_operand(1, 0, 256)
         words(0, 1, 0, low[0])
         drains(0, 0, low[0])
-        word_round(low[0][0], 0, 0)
+        rounds(0, 0, low[0])
         c_quantize(0, 256, 512)
         low_pass(1, 0, low[1])
         deal_words(wk_dealt[1][:], wk_raw[1][:].rearrange("p a n -> p (a n)"))
@@ -388,13 +388,12 @@ def tile_mix_kvw_outl_relu_kernel(
         words(0, 0, 1, banks)
         words(0, 1, 1, banks)
         drains(0, 1, banks)
-        rounds(0, 1, banks)
+        word_round(banks[0], 0, 1)
         c_quantize(0, 512, 1024)
         low_pass(2, 0, low[2])
         low.append(pair(0))
         low_pass(3, 0, low[3])
         deal_narrow(wq_scales_dealt[:], wq_scales_raw[:])
-        kc_round(on_vector, 0, 128, 256)
         for n in (1, 2, 3):
             c_operand(1, STEP * n, STEP * (n + 1))
             low_pass(n, 1, low[n])
@@ -403,7 +402,7 @@ def tile_mix_kvw_outl_relu_kernel(
         store_rows(0, 2, 4)
         held = {n: pair((3, 1, 2)[n - 1]) for n in (1, 2, 3)}
         for n in (1, 2, 3):
-            high(n, held[n], n in ())
+            high(n, held[n], n in (1,))
         store_kc32(1, 0, J)
         for n in (3,):
             rounds(n, 1, held[n])
@@ -419,7 +418,7 @@ def tile_mix_kvw_outl_relu_kernel(
         for n in range(QR_AHEAD):
             qr_passes(banks[n], n, 0)
         x_operand(1)
-        kc_piece(on_vector, 1, 1)
+        kc_round(on_vector, 1, 128, 256)
         x_finish(1)
         for n in range(BANKS):
             qr_passes(banks[n], n, 1)

@@ -24,11 +24,10 @@ BANKS = 8
 LINE = 4
 SCORE_SCALE = 0.03125
 
-ROW_W4, ROW_W8, ROW_WK = 0, 4, 0
+ROW_W4, ROW_W8 = 0, 4
 
-CHUNKS = (((0, 1024),), ((0, 256), (256, 512), (768, 256)))
-STEP = 256
-SCALAR_SHARE = 128
+CHUNK = 256
+C_LOADS = (((0, 1024),), ((0, 256), (256, 512), (768, 256)))
 QR_AHEAD = 5
 
 
@@ -61,16 +60,16 @@ def tile_mix_kvw_outl_relu_kernel(
         c_raw = {
             (a, n): tile("c_raw%d%d" % (a, n), [P, PACK, width], F32)
             for a in range(2)
-            for n, (j0, width) in enumerate(CHUNKS[a])
+            for n, (first, width) in enumerate(C_LOADS[a])
         }
         x_raw = [tile("x_raw%d" % a, [P, PACK, M], F32) for a in range(2)]
 
         nc.vector.memset(wk_scales_raw[:].bitcast(I32), 0)
         nc.vector.memset(wq_scales_raw[:].bitcast(I32), 0)
 
-        def load_scales(dst, row, scales, queue=nc.sync):
+        def load_scales(dst, row, scales):
             for r in range(4):
-                queue.dma_start(
+                nc.sync.dma_start(
                     out=dst[row + r : P : 32, :].rearrange("q (a d) -> q a d", d=D).bitcast(I32),
                     in_=scales[:, r:16:4, :].rearrange("a q d -> q a d").bitcast(I32),
                 )
@@ -80,11 +79,11 @@ def tile_mix_kvw_outl_relu_kernel(
             nc.sync.dma_start(out=wk_raw[b][:].bitcast(I32), in_=words[:, :, PASS * b : PASS * (b + 1)])
 
         def load_c(a, n):
-            j0, width = CHUNKS[a][n]
-            nc.sync.dma_start(out=c_raw[a, n][:], in_=four_rows(c[PASS * a : PASS * (a + 1), j0 : j0 + width]))
+            first, width = C_LOADS[a][n]
+            nc.sync.dma_start(out=c_raw[a, n][:], in_=four_rows(c[PASS * a : PASS * (a + 1), first : first + width]))
 
         nc.sync.dma_start(out=w4_raw[:].bitcast(I32), in_=w4_words[0].bitcast(I32))
-        load_scales(wk_scales_raw, ROW_WK, wk_scales)
+        load_scales(wk_scales_raw, 0, wk_scales)
         load_c(0, 0)
         load_scales(wq_scales_raw, ROW_W8, w8_scales)
         load_wk(0)
@@ -94,19 +93,19 @@ def tile_mix_kvw_outl_relu_kernel(
         load_c(1, 1)
         load_c(1, 2)
         nc.sync.dma_start(out=w8_raw[:].bitcast(I32), in_=as_words(w8_words[0]))
-        nc.sync.dma_start(out=x_raw[0][:], in_=four_rows(x[PASS * 0 : PASS * 1, :]))
-        nc.sync.dma_start(out=x_raw[1][:], in_=four_rows(x[PASS * 1 : PASS * 2, :]))
+        for a in range(2):
+            nc.sync.dma_start(out=x_raw[a][:], in_=four_rows(x[PASS * a : PASS * (a + 1), :]))
 
         def deal_words(dst, src):
             nc.vector.tensor_copy(
-                out=dst.bitcast(I32).rearrange("p (b t m) -> p b m t", b=2, t=PACK),
-                in_=src.bitcast(I32).rearrange("p (b m t) -> p b m t", b=2, t=PACK),
+                out=dst.bitcast(I32).rearrange("p (s t m) -> p s m t", s=2, t=PACK),
+                in_=src.bitcast(I32).rearrange("p (s m t) -> p s m t", s=2, t=PACK),
             )
 
         def deal_narrow(dst, src):
             nc.vector.tensor_copy(
-                out=dst.rearrange("p (b t m) -> p b t m", m=P, t=PACK),
-                in_=src.rearrange("p (b m t) -> p b t m", m=P, t=PACK),
+                out=dst.rearrange("p (s t m) -> p s t m", m=P, t=PACK),
+                in_=src.rearrange("p (s m t) -> p s t m", m=P, t=PACK),
             )
 
         def on_vector(out, in_):
@@ -115,13 +114,18 @@ def tile_mix_kvw_outl_relu_kernel(
         def on_scalar(out, in_):
             nc.scalar.activation(out=out, in_=in_, func=ACT.Copy)
 
-        def round_columns(copy, dst, src, lo, hi):
+        def round_columns(copy, dst, src):
             copy(
-                dst[:, PACK * lo : PACK * hi].rearrange("p (n i t) -> p n t i", i=LINE, t=PACK),
-                src[:, :, lo:hi].rearrange("p t (n i) -> p n t i", i=LINE),
+                dst.rearrange("p (n i t) -> p n t i", i=LINE, t=PACK),
+                src.rearrange("p t (n i) -> p n t i", i=LINE),
             )
 
-        def quantize_columns(operand, lo, hi):
+        def round_bank(dst, acc):
+            nc.scalar.copy(
+                out=dst.rearrange("p (n t) -> p n t", t=PACK), in_=acc[:].rearrange("p (t n) -> p n t", t=PACK)
+            )
+
+        def quantize(operand, lo, hi):
             rounded, codes, scales = operand
             nc.vector.quantize_mx(
                 out=codes[:, lo:hi].bitcast(FP8X4), scales=scales[:, lo:hi], in_=rounded[:, PACK * lo : PACK * hi]
@@ -134,13 +138,6 @@ def tile_mix_kvw_outl_relu_kernel(
                 tile(name + "_scales", [P, width], U8),
             )
 
-        def make_operand(operand, raw):
-            half = raw.shape[2] // 2
-            for lo in (0, half):
-                round_columns(on_vector, operand[0], raw, lo, lo + half)
-            for lo in (0, half):
-                quantize_columns(operand, lo, lo + half)
-
         wk_dealt = [tile("wk_dealt%d" % b, [P, 2 * PASS], U32) for b in range(2)]
         w8_dealt = tile("w8_dealt", [P, D], U32)
         w4_dealt = tile("w4_dealt", [P, 2 * D], U8)
@@ -149,86 +146,20 @@ def tile_mix_kvw_outl_relu_kernel(
         c_mx = [mx_operand("c%d" % a, J) for a in range(2)]
         x_mx = [mx_operand("x%d" % a, M) for a in range(2)]
 
-        kc32 = [tile("kc32_%d" % b, [P, PACK, J], F32) for b in range(2)]
-        kc_scales = tile("kc_scales", [P, 2 * J], U8)
-        kc_codes = tile("kc_codes", [P, 2 * J], U32)
-        kc_mx = [
-            (
-                tile("kc_rounded%d" % b, [P, PACK * J], BF16),
-                kc_codes[:, J * b : J * (b + 1)],
-                kc_scales[:, J * b : J * (b + 1)],
-            )
-            for b in range(2)
-        ]
+        def deal_wk(b):
+            deal_words(wk_dealt[b][:], wk_raw[b][:].rearrange("p a n -> p (a n)"))
 
         def c_round(copy, a, lo, hi):
-            n = max(u for u, (j0, width) in enumerate(CHUNKS[a]) if j0 <= lo)
-            j0 = CHUNKS[a][n][0]
-            copy(
-                c_mx[a][0][:, PACK * lo : PACK * hi].rearrange("p (n i t) -> p n t i", i=LINE, t=PACK),
-                c_raw[a, n][:, :, lo - j0 : hi - j0].rearrange("p t (n i) -> p n t i", i=LINE),
-            )
+            n = max(u for u, (first, width) in enumerate(C_LOADS[a]) if first <= lo)
+            first = C_LOADS[a][n][0]
+            round_columns(copy, c_mx[a][0][:, PACK * lo : PACK * hi], c_raw[a, n][:, :, lo - first : hi - first])
 
-        def c_quantize(a, lo, hi):
-            quantize_columns(c_mx[a], lo, hi)
-
-        def c_operand(a, lo, hi):
-            mid = (lo + hi) // 2
-            c_round(on_vector, a, lo, mid)
-            c_round(on_vector, a, mid, hi)
-            c_quantize(a, lo, mid)
-            c_quantize(a, mid, hi)
-
-        def kc_pass(acc, lo, width, a, i):
-            per_bank = BANK // width
-            place = i % per_bank
-            cols = slice(P * i, P * (i + 1))
-            nc.tensor.matmul_mx(
-                out=acc[:, width * place : width * (place + 1)],
-                lhsT=wk_dealt[i // PACK][:, PASS * a + P * (i % PACK) : PASS * a + P * (i % PACK + 1)].bitcast(FP8X4),
-                lhsT_scale=wk_scales_dealt[:, D * a + P * i : D * a + P * (i + 1)],
-                rhs=c_mx[a][1][:, lo : lo + width].bitcast(FP8X4),
-                rhs_scale=c_mx[a][2][:, lo : lo + width],
-                start=(a == 0 and place == 0),
-                stop=(a == 1 and place == per_bank - 1),
-            )
-
-        def kc_bank_pass(acc, lo, width, a, u):
-            per_bank = BANK // width
-            for i in range(per_bank * u, per_bank * (u + 1)):
-                kc_pass(acc, lo, width, a, i)
-
-        def kc_drain(copy, acc, lo, width, u):
-            per_bank = BANK // width
-            b, t = divmod(per_bank * u, PACK)
-            copy(kc32[b][:, t : t + per_bank, lo : lo + width], acc[:].rearrange("p (s j) -> p s j", s=per_bank))
-
-        def kc_first_passes(lo, width, first_bank):
-            banks = [bank(first_bank + u) for u in range(BANKS * width // BANK)]
-            for u, acc in enumerate(banks):
-                kc_bank_pass(acc, lo, width, 0, u)
-            return banks
-
-        def kc_second_passes(lo, width, banks):
-            for u, acc in enumerate(banks):
-                kc_bank_pass(acc, lo, width, 1, u)
-                kc_drain(scalar_copy, acc, lo, width, u)
-
-        def word_pass(acc, lo, a, b):
-            for t in range(PACK):
-                kc_pass(acc, lo, P, a, PACK * b + t)
-
-        def word_drain(acc, lo, b):
-            nc.scalar.copy(out=kc32[b][:, :, lo : lo + P], in_=acc[:].rearrange("p (t j) -> p t j", t=PACK))
-
-        def word_round(acc, lo, b):
-            nc.scalar.copy(
-                out=kc_mx[b][0][:, PACK * lo : PACK * (lo + P)].rearrange("p (j t) -> p j t", t=PACK),
-                in_=acc[:].rearrange("p (t j) -> p j t", t=PACK),
-            )
-
-        def kc_piece(copy, b, n):
-            kc_round(copy, b, STEP * n, STEP * (n + 1))
+        def c_chunk(n):
+            parts = (CHUNK * n, CHUNK * n + P)
+            for lo in parts:
+                c_round(on_vector, 1, lo, lo + P)
+            for lo in parts:
+                quantize(c_mx[1], lo, lo + P)
 
         def x_round(a, u, lo, hi):
             dst = x_mx[a][0][:, 2 * PASS * u : 2 * PASS * (u + 1)].rearrange("p (e n t) -> p e n t", e=2, t=PACK)
@@ -237,28 +168,69 @@ def tile_mix_kvw_outl_relu_kernel(
                 in_=x_raw[a][:, :, 2 * (P * u + lo) : 2 * (P * u + hi)].rearrange("p t (n i e) -> p n t i e", i=2, e=2),
             )
 
-        def x_operand(a):
+        def x_begin(a):
             x_round(a, 0, 0, P)
             x_round(a, 1, 0, P // 2)
-            quantize_columns(x_mx[a], 0, 2 * P)
+            quantize(x_mx[a], 0, 2 * P)
             x_round(a, 1, P // 2, P)
 
-        def x_finish(a):
-            quantize_columns(x_mx[a], 2 * P, 4 * P)
+        def x_end(a):
+            quantize(x_mx[a], 2 * P, 4 * P)
 
-        def kc_round(copy, b, lo, hi):
-            round_columns(copy, kc_mx[b][0], kc32[b], lo, hi)
-
-        def store_kc32(b, lo, hi):
-            nc.sync.dma_start(out=four_rows(out_1[PASS * b : PASS * (b + 1), lo:hi]), in_=kc32[b][:, :, lo:hi])
-
-        def store_codes(lo, hi):
-            nc.sync.dma_start(
-                out=out_2.rearrange("b p n t -> p b (n t)").bitcast(I32)[:, :, lo:hi],
-                in_=kc_codes[:].bitcast(I32).rearrange("p (b n) -> p b n", b=2)[:, :, lo:hi],
+        kc32 = [tile("kc32_%d" % b, [P, PACK, J], F32) for b in range(2)]
+        kc_scales = tile("kc_scales", [P, 2 * J], U8)
+        kc_mx = [
+            (
+                tile("kc_rounded%d" % b, [P, PACK * J], BF16),
+                tile("kc_codes%d" % b, [P, J], U32),
+                kc_scales[:, J * b : J * (b + 1)],
             )
+            for b in range(2)
+        ]
+
+        def kc_banks(n, b, pair, by_column):
+            if by_column:
+                return [(bank(2 * pair + v), b, 0, CHUNK * n + P * v, P) for v in range(2)]
+            return [(bank(2 * pair + v), b, 2 * v, CHUNK * n, CHUNK) for v in range(2)]
+
+        def kc_passes(banks, a):
+            for acc, b, t0, lo, width in banks:
+                tiles = BANK // width
+                for s in range(tiles):
+                    t = t0 + s
+                    scale_col = D * a + PASS * b + P * t
+                    nc.tensor.matmul_mx(
+                        out=acc[:, width * s : width * (s + 1)],
+                        lhsT=wk_dealt[b][:, PASS * a + P * t : PASS * a + P * (t + 1)].bitcast(FP8X4),
+                        lhsT_scale=wk_scales_dealt[:, scale_col : scale_col + P],
+                        rhs=c_mx[a][1][:, lo : lo + width].bitcast(FP8X4),
+                        rhs_scale=c_mx[a][2][:, lo : lo + width],
+                        start=(a == 0 and s == 0),
+                        stop=(a == 1 and s == tiles - 1),
+                    )
+
+        def kc_copy_out(banks):
+            for acc, b, t0, lo, width in banks:
+                tiles = BANK // width
+                nc.scalar.copy(
+                    out=kc32[b][:, t0 : t0 + tiles, lo : lo + width], in_=acc[:].rearrange("p (s j) -> p s j", s=tiles)
+                )
+
+        def kc_round_from_psum(banks):
+            for acc, b, t0, lo, width in banks:
+                round_bank(kc_mx[b][0][:, PACK * lo : PACK * (lo + width)], acc)
+
+        def kc_round(b, lo, hi):
+            round_columns(on_vector, kc_mx[b][0][:, PACK * lo : PACK * hi], kc32[b][:, :, lo:hi])
+
+        def store_kc32(b, t0, t1):
+            nc.sync.dma_start(out=four_rows(out_1[PASS * b : PASS * (b + 1), :])[:, t0:t1, :], in_=kc32[b][:, t0:t1, :])
+
+        def store_codes(b):
+            nc.sync.dma_start(out=as_words(out_2[b]), in_=kc_mx[b][1][:].bitcast(I32))
 
         qr_mx = [mx_operand("qr%d" % u, 4 * P) for u in range(2)]
+        scores = tile("scores", [P, 4, J], F32)
 
         def qr_passes(acc, n, a):
             g, b = divmod(n, 2)
@@ -283,11 +255,9 @@ def tile_mix_kvw_outl_relu_kernel(
 
         def qr_quantize(g):
             lo = 2 * P * (g % 2)
-            quantize_columns(qr_mx[g // 2], lo, lo + 2 * P)
+            quantize(qr_mx[g // 2], lo, lo + 2 * P)
 
-        scores = tile("scores", [P, 4, J], F32)
-
-        def score_bank(g, h, engine, place):
+        def score_bank(g, h, on_vector_engine, place):
             acc = bank(place)
             keys = slice(BANK * h, BANK * (h + 1))
             for b in range(2):
@@ -302,149 +272,99 @@ def tile_mix_kvw_outl_relu_kernel(
                     start=(b == 0),
                     stop=(b == 1),
                 )
-            dst = scores[:, g, keys]
-            if engine == "vector":
+            if on_vector_engine:
                 nc.vector.tensor_scalar(
-                    out=dst, in0=acc[:], scalar1=0.0, scalar2=SCORE_SCALE, op0=ALU.max, op1=ALU.mult
+                    out=scores[:, g, keys], in0=acc[:], scalar1=0.0, scalar2=SCORE_SCALE, op0=ALU.max, op1=ALU.mult
                 )
             else:
-                nc.scalar.activation(out=dst, in_=acc[:], func=ACT.Relu, scale=SCORE_SCALE)
+                nc.scalar.activation(out=scores[:, g, keys], in_=acc[:], func=ACT.Relu, scale=SCORE_SCALE)
 
-        def store_scores(g0, g1, lo, hi):
+        def store_scores(u):
             nc.sync.dma_start(
-                out=out_0[P * g0 : P * g1, lo:hi].rearrange("(p e) j -> p e j", p=P), in_=scores[:, g0:g1, lo:hi]
+                out=out_0[2 * P * u : 2 * P * (u + 1), :].rearrange("(p e) j -> p e j", e=2),
+                in_=scores[:, 2 * u : 2 * u + 2, :],
             )
-
-        def store_scales():
-            for r in range(4):
-                nc.gpsimd.dma_start(
-                    out=out_3[:, r:16:4, :].rearrange("b q j -> q b j").bitcast(I32),
-                    in_=kc_scales[r:P:32, :].rearrange("q (b j) -> q b j", b=2).bitcast(I32),
-                )
-
-        def qr_copy(copy, banks, n):
-            copy(
-                qr_mx[n // 4][0][:, PASS * (n % 4) : PASS * (n % 4 + 1)].rearrange("p (m t) -> p m t", t=PACK),
-                banks[n][:].rearrange("p (t m) -> p m t", t=PACK),
-            )
-
-        def scalar_copy(out, in_):
-            nc.scalar.copy(out=out, in_=in_)
-
-        def words(n, a, b, banks):
-            for v in range(2):
-                word_pass(banks[v], STEP * n + P * v, a, b)
-
-        def drains(n, b, banks):
-            for v in range(2):
-                word_drain(banks[v], STEP * n + P * v, b)
-
-        def rounds(n, b, banks):
-            for v in range(2):
-                word_round(banks[v], STEP * n + P * v, b)
-
-        def store_rows(b, t0, t1):
-            nc.sync.dma_start(out=four_rows(out_1[PASS * b : PASS * (b + 1), :])[:, t0:t1, :], in_=kc32[b][:, t0:t1, :])
-
-        def store_half_codes(b):
-            nc.sync.dma_start(out=as_words(out_2[b]), in_=kc_mx[b][1].bitcast(I32))
-
-        def pair(u):
-            return [bank(2 * u), bank(2 * u + 1)]
-
-        def low_pass(n, a, banks):
-            for u in range(2):
-                kc_bank_pass(banks[u], STEP * n, STEP, a, u)
-
-        def low_drains(n, banks):
-            for u in range(2):
-                kc_drain(scalar_copy, banks[u], STEP * n, STEP, u)
-
-        def high(n, banks, rounded):
-            words(n, 0, 1, banks)
-            words(n, 1, 1, banks)
-            drains(n, 1, banks)
-            if rounded:
-                rounds(n, 1, banks)
 
         deal_narrow(w4_dealt[:].bitcast(U16), w4_raw[:].bitcast(U16))
-        c_round(on_scalar, 0, 512, 768)
-        c_round(on_scalar, 0, 768, 1024)
+        for n in (2, 3):
+            c_round(on_scalar, 0, CHUNK * n, CHUNK * (n + 1))
         deal_narrow(wk_scales_dealt[:], wk_scales_raw[:])
-        c_round(on_vector, 0, 0, 256)
-        c_round(on_vector, 0, 256, 512)
-        c_quantize(0, 0, 256)
-        deal_words(wk_dealt[0][:], wk_raw[0][:].rearrange("p a n -> p (a n)"))
-        low = [pair(n) for n in range(3)]
-        words(0, 0, 0, low[0])
-        c_operand(1, 0, 256)
-        words(0, 1, 0, low[0])
-        drains(0, 0, low[0])
-        rounds(0, 0, low[0])
-        c_quantize(0, 256, 512)
-        low_pass(1, 0, low[1])
-        deal_words(wk_dealt[1][:], wk_raw[1][:].rearrange("p a n -> p (a n)"))
-        banks = pair(3)
-        words(0, 0, 1, banks)
-        words(0, 1, 1, banks)
-        drains(0, 1, banks)
-        word_round(banks[0], 0, 1)
-        c_quantize(0, 512, 1024)
-        low_pass(2, 0, low[2])
-        low.append(pair(0))
-        low_pass(3, 0, low[3])
+        for n in (0, 1):
+            c_round(on_vector, 0, CHUNK * n, CHUNK * (n + 1))
+        quantize(c_mx[0], 0, CHUNK)
+        deal_wk(0)
+        low = [kc_banks(0, 0, 0, True), kc_banks(1, 0, 1, False), kc_banks(2, 0, 2, False)]
+        kc_passes(low[0], 0)
+        c_chunk(0)
+        kc_passes(low[0], 1)
+        kc_copy_out(low[0])
+        kc_round_from_psum(low[0])
+        quantize(c_mx[0], CHUNK, 2 * CHUNK)
+        kc_passes(low[1], 0)
+        deal_wk(1)
+        high = kc_banks(0, 1, 3, True)
+        kc_passes(high, 0)
+        kc_passes(high, 1)
+        kc_copy_out(high)
+        kc_round_from_psum(high[:1])
+        quantize(c_mx[0], 2 * CHUNK, J)
+        kc_passes(low[2], 0)
+        low.append(kc_banks(3, 0, 0, False))
+        kc_passes(low[3], 0)
         deal_narrow(wq_scales_dealt[:], wq_scales_raw[:])
-        for n in (1, 2, 3):
-            c_operand(1, STEP * n, STEP * (n + 1))
-            low_pass(n, 1, low[n])
-            low_drains(n, low[n])
-        store_rows(0, 0, 2)
-        store_rows(0, 2, 4)
-        held = {n: pair((3, 1, 2)[n - 1]) for n in (1, 2, 3)}
-        for n in (1, 2, 3):
-            high(n, held[n], n in (1,))
-        store_kc32(1, 0, J)
-        for n in (3,):
-            rounds(n, 1, held[n])
-        deal_words(w8_dealt[:], w8_raw[:])
-        kc_piece(on_vector, 0, 1)
-        kc_piece(on_vector, 0, 2)
 
-        x_operand(0)
-        quantize_columns(kc_mx[0], 0, BANK)
-        x_finish(0)
-        order = (0, 3, 1, 2)
-        banks = [bank(2 * order[n // 2] + n % 2) for n in range(BANKS)]
+        for n in (1, 2, 3):
+            c_chunk(n)
+            kc_passes(low[n], 1)
+            kc_copy_out(low[n])
+        store_kc32(0, 0, 2)
+        store_kc32(0, 2, 4)
+        high = {n: kc_banks(n, 1, pair, n != 2) for n, pair in ((1, 3), (2, 1), (3, 2))}
+        for n in (1, 2, 3):
+            kc_passes(high[n], 0)
+            kc_passes(high[n], 1)
+            kc_copy_out(high[n])
+        store_kc32(1, 0, 4)
+        for n in (1, 3):
+            kc_round_from_psum(high[n])
+        deal_words(w8_dealt[:], w8_raw[:])
+        for n in (1, 2):
+            kc_round(0, CHUNK * n, CHUNK * (n + 1))
+
+        places = [2 * pair + v for pair in (0, 1, 3, 2) for v in range(2)]
+        x_begin(0)
+        quantize(kc_mx[0], 0, BANK)
+        x_end(0)
+        banks = [bank(place) for place in places]
         for n in range(QR_AHEAD):
             qr_passes(banks[n], n, 0)
-        x_operand(1)
-        kc_round(on_vector, 1, 128, 256)
-        x_finish(1)
+        x_begin(1)
+        kc_round(1, P, CHUNK)
+        x_end(1)
         for n in range(BANKS):
             qr_passes(banks[n], n, 1)
             if n + QR_AHEAD < BANKS:
                 qr_passes(banks[n + QR_AHEAD], n + QR_AHEAD, 0)
-            qr_copy(scalar_copy, banks, n)
-        place = [2 * order[n // 2] + n % 2 for n in range(BANKS)]
-        kc_piece(on_vector, 0, 3)
-        quantize_columns(kc_mx[1], 0, 512)
-        kc_piece(on_vector, 1, 2)
-        qr_quantize(0)
-        score_bank(0, 0, "scalar", place[0])
-        quantize_columns(kc_mx[0], BANK, J)
-        store_half_codes(0)
-        qr_quantize(1)
-        score_bank(1, 0, "scalar", place[1])
-        quantize_columns(kc_mx[1], BANK, J)
-        store_half_codes(1)
-        store_scales()
-        qr_quantize(2)
-        score_bank(0, 1, "vector", place[2])
-        qr_quantize(3)
-        score_bank(1, 1, "vector", place[3])
-        store_scores(0, 2, 0, J)
-        score_bank(2, 0, "scalar", place[4])
-        score_bank(2, 1, "vector", place[5])
-        score_bank(3, 0, "scalar", place[6])
-        score_bank(3, 1, "vector", place[7])
-        store_scores(2, 4, 0, J)
+            round_bank(qr_mx[n // 4][0][:, PASS * (n % 4) : PASS * (n % 4 + 1)], banks[n])
+
+        kc_round(0, 3 * CHUNK, J)
+        quantize(kc_mx[1], 0, BANK)
+        kc_round(1, 2 * CHUNK, 3 * CHUNK)
+        for g in range(2):
+            qr_quantize(g)
+            score_bank(g, 0, False, places[g])
+            quantize(kc_mx[g], BANK, J)
+            store_codes(g)
+        for r in range(4):
+            nc.sync.dma_start(
+                out=out_3[:, r:16:4, :].rearrange("b q j -> q b j").bitcast(I32),
+                in_=kc_scales[r:P:32, :].rearrange("q (b j) -> q b j", b=2).bitcast(I32),
+            )
+        for g in range(2):
+            qr_quantize(2 + g)
+            score_bank(g, 1, True, places[2 + g])
+        store_scores(0)
+        for g in (2, 3):
+            score_bank(g, 0, False, places[2 * g])
+            score_bank(g, 1, True, places[2 * g + 1])
+        store_scores(1)

@@ -83,10 +83,10 @@ def tile_mix_kvw_outl_relu_kernel(
             nc.sync.dma_start(out=c_raw[a, n][:], in_=four_rows(c[PASS * a : PASS * (a + 1), first : first + width]))
 
         nc.sync.dma_start(out=w4_raw[:].bitcast(I32), in_=w4_words[0].bitcast(I32))
+        load_wk(0)
         load_scales(wk_scales_raw, 0, wk_scales)
         load_c(0, 0)
         load_scales(wq_scales_raw, ROW_W8, w8_scales)
-        load_wk(0)
         load_c(1, 0)
         load_wk(1)
         load_scales(wq_scales_raw, ROW_W4, w4_scales)
@@ -288,11 +288,11 @@ def tile_mix_kvw_outl_relu_kernel(
         deal_narrow(w4_dealt[:].bitcast(U16), w4_raw[:].bitcast(U16))
         for n in (2, 3):
             c_round(on_scalar, 0, CHUNK * n, CHUNK * (n + 1))
+        deal_wk(0)
         deal_narrow(wk_scales_dealt[:], wk_scales_raw[:])
         for n in (0, 1):
             c_round(on_vector, 0, CHUNK * n, CHUNK * (n + 1))
         quantize(c_mx[0], 0, CHUNK)
-        deal_wk(0)
         low = [kc_banks(0, 0, 0, True), kc_banks(1, 0, 1, False), kc_banks(2, 0, 2, False)]
         kc_passes(low[0], 0)
         c_chunk(0)
@@ -302,11 +302,10 @@ def tile_mix_kvw_outl_relu_kernel(
         quantize(c_mx[0], CHUNK, 2 * CHUNK)
         kc_passes(low[1], 0)
         deal_wk(1)
-        high = kc_banks(0, 1, 3, True)
+        high = kc_banks(0, 1, 3, False)
         kc_passes(high, 0)
         kc_passes(high, 1)
         kc_copy_out(high)
-        kc_round_from_psum(high[:1])
         quantize(c_mx[0], 2 * CHUNK, J)
         kc_passes(low[2], 0)
         low.append(kc_banks(3, 0, 0, False))
@@ -339,7 +338,7 @@ def tile_mix_kvw_outl_relu_kernel(
         for n in range(QR_AHEAD):
             qr_passes(banks[n], n, 0)
         x_begin(1)
-        kc_round(1, P, CHUNK)
+        kc_round(1, 0, CHUNK)
         x_end(1)
         for n in range(BANKS):
             qr_passes(banks[n], n, 1)
@@ -350,11 +349,11 @@ def tile_mix_kvw_outl_relu_kernel(
         kc_round(0, 3 * CHUNK, J)
         quantize(kc_mx[1], 0, BANK)
         kc_round(1, 2 * CHUNK, 3 * CHUNK)
-        for g in range(2):
+        for g, b in ((0, 0), (1, 1)):
             qr_quantize(g)
             score_bank(g, 0, False, places[g])
-            quantize(kc_mx[g], BANK, J)
-            store_codes(g)
+            quantize(kc_mx[b], BANK, J)
+            store_codes(b)
         for r in range(4):
             nc.sync.dma_start(
                 out=out_3[:, r:16:4, :].rearrange("b q j -> q b j").bitcast(I32),

@@ -24,7 +24,7 @@ BANKS = 8
 LINE = 4
 SCORE_SCALE = 0.03125
 
-ROW_W4, ROW_W8 = 0, 4
+ROW_W4, ROW_W8, ROW_WK, ROW_KC = 0, 4, 8, 12
 
 CHUNK = 256
 C_LOADS = (((0, 1024),), ((0, 256), (256, 512), (768, 256)))
@@ -84,7 +84,7 @@ def tile_mix_kvw_outl_relu_kernel(
 
         nc.sync.dma_start(out=w4_raw[:].bitcast(I32), in_=w4_words[0].bitcast(I32))
         load_wk(0)
-        load_scales(wk_scales_raw, 0, wk_scales)
+        load_scales(wk_scales_raw, ROW_WK, wk_scales)
         load_c(0, 0)
         load_scales(wq_scales_raw, ROW_W8, w8_scales)
         load_c(1, 0)
@@ -183,7 +183,7 @@ def tile_mix_kvw_outl_relu_kernel(
             (
                 tile("kc_rounded%d" % b, [P, PACK * J], BF16),
                 tile("kc_codes%d" % b, [P, J], U32),
-                kc_scales[:, J * b : J * (b + 1)],
+                kc_scales[ROW_KC:, J * b : J * (b + 1)],
             )
             for b in range(2)
         ]
@@ -202,7 +202,7 @@ def tile_mix_kvw_outl_relu_kernel(
                     nc.tensor.matmul_mx(
                         out=acc[:, width * s : width * (s + 1)],
                         lhsT=wk_dealt[b][:, PASS * a + P * t : PASS * a + P * (t + 1)].bitcast(FP8X4),
-                        lhsT_scale=wk_scales_dealt[:, scale_col : scale_col + P],
+                        lhsT_scale=wk_scales_dealt[ROW_WK:, scale_col : scale_col + P],
                         rhs=c_mx[a][1][:, lo : lo + width].bitcast(FP8X4),
                         rhs_scale=c_mx[a][2][:, lo : lo + width],
                         start=(a == 0 and s == 0),
@@ -357,7 +357,7 @@ def tile_mix_kvw_outl_relu_kernel(
         for r in range(4):
             nc.sync.dma_start(
                 out=out_3[:, r:16:4, :].rearrange("b q j -> q b j").bitcast(I32),
-                in_=kc_scales[r:P:32, :].rearrange("q (b j) -> q b j", b=2).bitcast(I32),
+                in_=kc_scales[ROW_KC + r : P : 32, :].rearrange("q (b j) -> q b j", b=2).bitcast(I32),
             )
         for g in range(2):
             qr_quantize(2 + g)

@@ -27,7 +27,7 @@ SCORE_SCALE = 0.03125
 ROW_W4, ROW_W8, ROW_WK, ROW_KC = 0, 4, 8, 12
 
 CHUNK = 256
-C_LOADS = (((0, 1024),), ((0, 256), (256, 512), (768, 256)))
+C_LOADS = (((0, 512), (512, 512)), ((0, 256), (256, 512), (768, 256)))
 QR_AHEAD = 5
 
 
@@ -78,23 +78,33 @@ def tile_mix_kvw_outl_relu_kernel(
             words = wk_words.rearrange("a p n t -> p a (n t)").bitcast(I32)
             nc.sync.dma_start(out=wk_raw[b][:].bitcast(I32), in_=words[:, :, PASS * b : PASS * (b + 1)])
 
+        def load_w8():
+            nc.sync.dma_start(out=w8_raw[:].bitcast(I32), in_=as_words(w8_words[0]))
+
+        def load_w4():
+            nc.sync.dma_start(out=w4_raw[:].bitcast(I32), in_=w4_words[0].bitcast(I32))
+
+        def load_x(a):
+            nc.sync.dma_start(out=x_raw[a][:], in_=four_rows(x[PASS * a : PASS * (a + 1), :]))
+
         def load_c(a, n):
             first, width = C_LOADS[a][n]
             nc.sync.dma_start(out=c_raw[a, n][:], in_=four_rows(c[PASS * a : PASS * (a + 1), first : first + width]))
 
-        nc.sync.dma_start(out=w4_raw[:].bitcast(I32), in_=w4_words[0].bitcast(I32))
         load_wk(0)
-        load_scales(wk_scales_raw, ROW_WK, wk_scales)
         load_c(0, 0)
-        load_scales(wq_scales_raw, ROW_W8, w8_scales)
+        load_scales(wk_scales_raw, ROW_WK, wk_scales)
         load_c(1, 0)
         load_wk(1)
+        load_scales(wq_scales_raw, ROW_W8, w8_scales)
+        load_c(0, 1)
         load_scales(wq_scales_raw, ROW_W4, w4_scales)
         load_c(1, 1)
         load_c(1, 2)
-        nc.sync.dma_start(out=w8_raw[:].bitcast(I32), in_=as_words(w8_words[0]))
-        for a in range(2):
-            nc.sync.dma_start(out=x_raw[a][:], in_=four_rows(x[PASS * a : PASS * (a + 1), :]))
+        load_w8()
+        load_w4()
+        load_x(0)
+        load_x(1)
 
         def deal_words(dst, src):
             nc.vector.tensor_copy(
@@ -220,14 +230,21 @@ def tile_mix_kvw_outl_relu_kernel(
             for acc, b, t0, lo, width in banks:
                 round_bank(kc_mx[b][0][:, PACK * lo : PACK * (lo + width)], acc)
 
-        def kc_round(b, lo, hi):
-            round_columns(on_vector, kc_mx[b][0][:, PACK * lo : PACK * hi], kc32[b][:, :, lo:hi])
+        def kc_round(b, lo, hi, copy=on_vector):
+            round_columns(copy, kc_mx[b][0][:, PACK * lo : PACK * hi], kc32[b][:, :, lo:hi])
 
         def store_kc32(b, t0, t1):
             nc.sync.dma_start(out=four_rows(out_1[PASS * b : PASS * (b + 1), :])[:, t0:t1, :], in_=kc32[b][:, t0:t1, :])
 
         def store_codes(b):
             nc.sync.dma_start(out=as_words(out_2[b]), in_=kc_mx[b][1][:].bitcast(I32))
+
+        def store_scales():
+            for r in range(4):
+                nc.sync.dma_start(
+                    out=out_3[:, r:16:4, :].rearrange("b q j -> q b j").bitcast(I32),
+                    in_=kc_scales[ROW_KC + r : P : 32, :].rearrange("q (b j) -> q b j", b=2).bitcast(I32),
+                )
 
         qr_mx = [mx_operand("qr%d" % u, 4 * P) for u in range(2)]
         scores = tile("scores", [P, 4, J], F32)
@@ -285,85 +302,98 @@ def tile_mix_kvw_outl_relu_kernel(
                 in_=scores[:, 2 * u : 2 * u + 2, :],
             )
 
-        deal_narrow(w4_dealt[:].bitcast(U16), w4_raw[:].bitcast(U16))
-        for n in (2, 3):
-            c_round(on_scalar, 0, CHUNK * n, CHUNK * (n + 1))
         deal_wk(0)
-        deal_narrow(wk_scales_dealt[:], wk_scales_raw[:])
-        for n in (0, 1):
-            c_round(on_vector, 0, CHUNK * n, CHUNK * (n + 1))
+        c_round(on_scalar, 0, CHUNK, 2 * CHUNK)
+        c_round(on_vector, 0, 0, CHUNK)
+        deal_narrow(wk_scales_dealt[:, :D], wk_scales_raw[:, :D])
         quantize(c_mx[0], 0, CHUNK)
         low = [kc_banks(0, 0, 0, True), kc_banks(1, 0, 1, False), kc_banks(2, 0, 2, False)]
         kc_passes(low[0], 0)
-        c_chunk(0)
+        deal_narrow(wk_scales_dealt[:, D:], wk_scales_raw[:, D:])
+        c_round(on_scalar, 1, P, CHUNK)
+        c_round(on_vector, 1, 0, P)
+        quantize(c_mx[0], CHUNK, 2 * CHUNK)
+        quantize(c_mx[1], 0, CHUNK)
         kc_passes(low[0], 1)
         kc_copy_out(low[0])
         kc_round_from_psum(low[0])
-        quantize(c_mx[0], CHUNK, 2 * CHUNK)
-        kc_passes(low[1], 0)
         deal_wk(1)
-        high = kc_banks(0, 1, 3, False)
+        high = kc_banks(0, 1, 3, True)
         kc_passes(high, 0)
         kc_passes(high, 1)
         kc_copy_out(high)
-        quantize(c_mx[0], 2 * CHUNK, J)
+        kc_round_from_psum(high)
+        kc_passes(low[1], 0)
+        for n in (2, 3):
+            c_round(on_vector, 0, CHUNK * n, CHUNK * (n + 1))
+        for n in (2, 3):
+            quantize(c_mx[0], CHUNK * n, CHUNK * (n + 1))
         kc_passes(low[2], 0)
         low.append(kc_banks(3, 0, 0, False))
         kc_passes(low[3], 0)
         deal_narrow(wq_scales_dealt[:], wq_scales_raw[:])
+        high = {1: kc_banks(1, 1, 3, False)}
+        kc_passes(high[1], 0)
 
-        for n in (1, 2, 3):
-            c_chunk(n)
+        c_round(on_scalar, 1, 2 * CHUNK, 3 * CHUNK)
+        c_chunk(1)
+        kc_passes(low[1], 1)
+        c_round(on_vector, 1, 3 * CHUNK, J)
+        for n in (2, 3):
+            quantize(c_mx[1], n * CHUNK, (n + 1) * CHUNK)
             kc_passes(low[n], 1)
-            kc_copy_out(low[n])
+        kc_passes(high[1], 1)
+        kc_copy_out(low[1] + low[2][:1] + low[3][:1])
         store_kc32(0, 0, 2)
+        kc_copy_out(low[2][1:] + low[3][1:])
         store_kc32(0, 2, 4)
-        high = {n: kc_banks(n, 1, pair, n != 2) for n, pair in ((1, 3), (2, 1), (3, 2))}
-        for n in (1, 2, 3):
+        kc_copy_out(high[1])
+        high.update({n: kc_banks(n, 1, pair, n == 3) for n, pair in ((2, 1), (3, 2))})
+        for n in (2, 3):
             kc_passes(high[n], 0)
             kc_passes(high[n], 1)
             kc_copy_out(high[n])
         store_kc32(1, 0, 4)
-        for n in (1, 3):
-            kc_round_from_psum(high[n])
+        kc_round_from_psum(high[3])
         deal_words(w8_dealt[:], w8_raw[:])
-        for n in (1, 2):
-            kc_round(0, CHUNK * n, CHUNK * (n + 1))
+        kc_round(0, CHUNK, 2 * CHUNK)
+        quantize(kc_mx[1], 0, CHUNK)
+        quantize(kc_mx[0], 0, 2 * CHUNK)
 
-        places = [2 * pair + v for pair in (0, 1, 3, 2) for v in range(2)]
+        places = [2 * pair + v for pair in (0, 3, 1, 2) for v in range(2)]
         x_begin(0)
-        quantize(kc_mx[0], 0, BANK)
+        deal_narrow(w4_dealt[:].bitcast(U16), w4_raw[:].bitcast(U16))
         x_end(0)
         banks = [bank(place) for place in places]
-        for n in range(QR_AHEAD):
+        for n in range(6):
             qr_passes(banks[n], n, 0)
         x_begin(1)
-        kc_round(1, 0, CHUNK)
+        kc_round(1, CHUNK, 2 * CHUNK)
         x_end(1)
         for n in range(BANKS):
             qr_passes(banks[n], n, 1)
-            if n + QR_AHEAD < BANKS:
-                qr_passes(banks[n + QR_AHEAD], n + QR_AHEAD, 0)
+            if n in (1, 2):
+                qr_passes(banks[n + 5], n + 5, 0)
             round_bank(qr_mx[n // 4][0][:, PASS * (n % 4) : PASS * (n % 4 + 1)], banks[n])
 
-        kc_round(0, 3 * CHUNK, J)
-        quantize(kc_mx[1], 0, BANK)
+        quantize(kc_mx[1], CHUNK, 2 * CHUNK)
+        kc_round(0, 2 * CHUNK, J)
+        qr_quantize(0)
+        quantize(kc_mx[0], BANK, J)
+        store_codes(0)
         kc_round(1, 2 * CHUNK, 3 * CHUNK)
-        for g, b in ((0, 0), (1, 1)):
-            qr_quantize(g)
-            score_bank(g, 0, False, places[g])
-            quantize(kc_mx[b], BANK, J)
-            store_codes(b)
-        for r in range(4):
-            nc.sync.dma_start(
-                out=out_3[:, r:16:4, :].rearrange("b q j -> q b j").bitcast(I32),
-                in_=kc_scales[ROW_KC + r : P : 32, :].rearrange("q (b j) -> q b j", b=2).bitcast(I32),
-            )
-        for g in range(2):
-            qr_quantize(2 + g)
-            score_bank(g, 1, True, places[2 + g])
+        qr_quantize(1)
+        quantize(kc_mx[1], BANK, J)
+        store_codes(1)
+        store_scales()
+        qr_quantize(2)
+        score_bank(0, 0, True, places[0])
+        qr_quantize(3)
+        score_bank(1, 0, False, places[1])
+        score_bank(0, 1, True, places[2])
+        score_bank(1, 1, False, places[3])
         store_scores(0)
         for g in (2, 3):
-            score_bank(g, 0, False, places[2 * g])
-            score_bank(g, 1, True, places[2 * g + 1])
+            score_bank(g, 0, True, places[2 * g])
+            score_bank(g, 1, False, places[2 * g + 1])
         store_scores(1)

@@ -27,7 +27,7 @@ SCORE_SCALE = 0.03125
 ROW_W4, ROW_W8, ROW_WK, ROW_KC = 0, 4, 8, 12
 
 CHUNK = 256
-C_LOADS = (((0, 512), (512, 512)), ((0, 256), (256, 512), (768, 256)))
+C_LOADS = (((0, 1024),), ((0, 256), (256, 512), (768, 256)))
 QR_AHEAD = 5
 
 
@@ -92,18 +92,17 @@ def tile_mix_kvw_outl_relu_kernel(
             nc.sync.dma_start(out=c_raw[a, n][:], in_=four_rows(c[PASS * a : PASS * (a + 1), first : first + width]))
 
         load_wk(0)
-        load_c(0, 0)
         load_scales(wk_scales_raw, ROW_WK, wk_scales)
+        load_c(0, 0)
+        load_scales(wq_scales_raw, ROW_W8, w8_scales)
         load_c(1, 0)
         load_wk(1)
-        load_scales(wq_scales_raw, ROW_W8, w8_scales)
-        load_c(0, 1)
         load_scales(wq_scales_raw, ROW_W4, w4_scales)
         load_c(1, 1)
         load_c(1, 2)
         load_w8()
-        load_w4()
         load_x(0)
+        load_w4()
         load_x(1)
 
         def deal_words(dst, src):
@@ -303,17 +302,15 @@ def tile_mix_kvw_outl_relu_kernel(
             )
 
         deal_wk(0)
-        c_round(on_scalar, 0, CHUNK, 2 * CHUNK)
+        deal_narrow(wk_scales_dealt[:], wk_scales_raw[:])
+        for n in (2, 3):
+            c_round(on_scalar, 0, CHUNK * n, CHUNK * (n + 1))
         c_round(on_vector, 0, 0, CHUNK)
-        deal_narrow(wk_scales_dealt[:, :D], wk_scales_raw[:, :D])
+        c_round(on_vector, 0, CHUNK, CHUNK + P)
         quantize(c_mx[0], 0, CHUNK)
-        low = [kc_banks(0, 0, 0, True), kc_banks(1, 0, 1, False), kc_banks(2, 0, 2, False)]
+        low = [kc_banks(0, 0, 0, True)] + [kc_banks(n, 0, n, False) for n in (1, 2)]
         kc_passes(low[0], 0)
-        deal_narrow(wk_scales_dealt[:, D:], wk_scales_raw[:, D:])
-        c_round(on_scalar, 1, P, CHUNK)
-        c_round(on_vector, 1, 0, P)
-        quantize(c_mx[0], CHUNK, 2 * CHUNK)
-        quantize(c_mx[1], 0, CHUNK)
+        c_chunk(0)
         kc_passes(low[0], 1)
         kc_copy_out(low[0])
         kc_round_from_psum(low[0])
@@ -323,25 +320,20 @@ def tile_mix_kvw_outl_relu_kernel(
         kc_passes(high, 1)
         kc_copy_out(high)
         kc_round_from_psum(high)
+        c_round(on_vector, 0, CHUNK + P, BANK)
+        quantize(c_mx[0], BANK, J)
+        quantize(c_mx[0], CHUNK, BANK)
         kc_passes(low[1], 0)
-        for n in (2, 3):
-            c_round(on_vector, 0, CHUNK * n, CHUNK * (n + 1))
-        for n in (2, 3):
-            quantize(c_mx[0], CHUNK * n, CHUNK * (n + 1))
         kc_passes(low[2], 0)
         low.append(kc_banks(3, 0, 0, False))
         kc_passes(low[3], 0)
         deal_narrow(wq_scales_dealt[:], wq_scales_raw[:])
+
+        for n in (1, 2, 3):
+            c_chunk(n)
+            kc_passes(low[n], 1)
         high = {1: kc_banks(1, 1, 3, False)}
         kc_passes(high[1], 0)
-
-        c_round(on_scalar, 1, 2 * CHUNK, 3 * CHUNK)
-        c_chunk(1)
-        kc_passes(low[1], 1)
-        c_round(on_vector, 1, 3 * CHUNK, J)
-        for n in (2, 3):
-            quantize(c_mx[1], n * CHUNK, (n + 1) * CHUNK)
-            kc_passes(low[n], 1)
         kc_passes(high[1], 1)
         kc_copy_out(low[1] + low[2][:1] + low[3][:1])
         store_kc32(0, 0, 2)
@@ -356,9 +348,7 @@ def tile_mix_kvw_outl_relu_kernel(
         store_kc32(1, 0, 4)
         kc_round_from_psum(high[3])
         deal_words(w8_dealt[:], w8_raw[:])
-        kc_round(0, CHUNK, 2 * CHUNK)
-        quantize(kc_mx[1], 0, CHUNK)
-        quantize(kc_mx[0], 0, 2 * CHUNK)
+        kc_round(0, CHUNK, BANK)
 
         places = [2 * pair + v for pair in (0, 3, 1, 2) for v in range(2)]
         x_begin(0)
@@ -368,7 +358,7 @@ def tile_mix_kvw_outl_relu_kernel(
         for n in range(6):
             qr_passes(banks[n], n, 0)
         x_begin(1)
-        kc_round(1, CHUNK, 2 * CHUNK)
+        quantize(kc_mx[0], 0, BANK)
         x_end(1)
         for n in range(BANKS):
             qr_passes(banks[n], n, 1)
@@ -376,8 +366,9 @@ def tile_mix_kvw_outl_relu_kernel(
                 qr_passes(banks[n + 5], n + 5, 0)
             round_bank(qr_mx[n // 4][0][:, PASS * (n % 4) : PASS * (n % 4 + 1)], banks[n])
 
-        quantize(kc_mx[1], CHUNK, 2 * CHUNK)
-        kc_round(0, 2 * CHUNK, J)
+        kc_round(1, CHUNK, BANK)
+        kc_round(0, BANK, J)
+        quantize(kc_mx[1], 0, BANK)
         qr_quantize(0)
         quantize(kc_mx[0], BANK, J)
         store_codes(0)
@@ -387,13 +378,13 @@ def tile_mix_kvw_outl_relu_kernel(
         store_codes(1)
         store_scales()
         qr_quantize(2)
-        score_bank(0, 0, True, places[0])
+        score_bank(0, 0, False, places[0])
+        score_bank(1, 0, True, places[1])
         qr_quantize(3)
-        score_bank(1, 0, False, places[1])
-        score_bank(0, 1, True, places[2])
-        score_bank(1, 1, False, places[3])
+        score_bank(0, 1, False, places[2])
+        score_bank(1, 1, True, places[3])
         store_scores(0)
         for g in (2, 3):
-            score_bank(g, 0, True, places[2 * g])
-            score_bank(g, 1, False, places[2 * g + 1])
+            score_bank(g, 0, False, places[2 * g])
+            score_bank(g, 1, True, places[2 * g + 1])
         store_scores(1)

@@ -28,7 +28,7 @@ ROW_W4, ROW_W8, ROW_WK, ROW_KC = 0, 4, 8, 12
 
 CHUNK = 256
 C_LOADS = (((0, 1024),), ((0, 256), (256, 512), (768, 256)))
-QR_AHEAD = 5
+QR_EARLY = BANKS - 2
 
 
 def tile_mix_kvw_outl_relu_kernel(
@@ -43,8 +43,8 @@ def tile_mix_kvw_outl_relu_kernel(
         def tile(name, shape, dtype):
             return sbuf.tile(shape, dtype, name=name, align_bytes=64)
 
-        def bank(n):
-            return psum.tile([P, BANK], F32, name="bank%d" % n)
+        def bank(place):
+            return psum.tile([P, BANK], F32, name="bank%d" % place)
 
         def as_words(codes):
             return codes.rearrange("p n t -> p (n t)").bitcast(I32)
@@ -58,9 +58,9 @@ def tile_mix_kvw_outl_relu_kernel(
         w8_raw = tile("w8_raw", [P, D], U32)
         w4_raw = tile("w4_raw", [P, 2 * D], U8)
         c_raw = {
-            (a, n): tile("c_raw%d%d" % (a, n), [P, PACK, width], F32)
+            (a, part): tile("c_raw%d%d" % (a, part), [P, PACK, width], F32)
             for a in range(2)
-            for n, (first, width) in enumerate(C_LOADS[a])
+            for part, (first, width) in enumerate(C_LOADS[a])
         }
         x_raw = [tile("x_raw%d" % a, [P, PACK, M], F32) for a in range(2)]
 
@@ -87,9 +87,9 @@ def tile_mix_kvw_outl_relu_kernel(
         def load_x(a):
             nc.sync.dma_start(out=x_raw[a][:], in_=four_rows(x[PASS * a : PASS * (a + 1), :]))
 
-        def load_c(a, n):
-            first, width = C_LOADS[a][n]
-            nc.sync.dma_start(out=c_raw[a, n][:], in_=four_rows(c[PASS * a : PASS * (a + 1), first : first + width]))
+        def load_c(a, part):
+            first, width = C_LOADS[a][part]
+            nc.sync.dma_start(out=c_raw[a, part][:], in_=four_rows(c[PASS * a : PASS * (a + 1), first : first + width]))
 
         load_wk(0)
         load_scales(wk_scales_raw, ROW_WK, wk_scales)
@@ -101,20 +101,20 @@ def tile_mix_kvw_outl_relu_kernel(
         load_c(1, 1)
         load_c(1, 2)
         load_w8()
-        load_x(0)
         load_w4()
+        load_x(0)
         load_x(1)
 
         def deal_words(dst, src):
             nc.vector.tensor_copy(
-                out=dst.bitcast(I32).rearrange("p (s t m) -> p s m t", s=2, t=PACK),
-                in_=src.bitcast(I32).rearrange("p (s m t) -> p s m t", s=2, t=PACK),
+                out=dst.bitcast(I32).rearrange("p (run t m) -> p run m t", run=2, t=PACK),
+                in_=src.bitcast(I32).rearrange("p (run m t) -> p run m t", run=2, t=PACK),
             )
 
         def deal_narrow(dst, src):
             nc.vector.tensor_copy(
-                out=dst.rearrange("p (s t m) -> p s t m", m=P, t=PACK),
-                in_=src.rearrange("p (s m t) -> p s t m", m=P, t=PACK),
+                out=dst.rearrange("p (run t m) -> p run t m", m=P, t=PACK),
+                in_=src.rearrange("p (run m t) -> p run t m", m=P, t=PACK),
             )
 
         def on_vector(out, in_):
@@ -159,16 +159,9 @@ def tile_mix_kvw_outl_relu_kernel(
             deal_words(wk_dealt[b][:], wk_raw[b][:].rearrange("p a n -> p (a n)"))
 
         def c_round(copy, a, lo, hi):
-            n = max(u for u, (first, width) in enumerate(C_LOADS[a]) if first <= lo)
-            first = C_LOADS[a][n][0]
-            round_columns(copy, c_mx[a][0][:, PACK * lo : PACK * hi], c_raw[a, n][:, :, lo - first : hi - first])
-
-        def c_chunk(n):
-            parts = (CHUNK * n, CHUNK * n + P)
-            for lo in parts:
-                c_round(on_vector, 1, lo, lo + P)
-            for lo in parts:
-                quantize(c_mx[1], lo, lo + P)
+            part = len([first for first, width in C_LOADS[a] if first <= lo]) - 1
+            first = C_LOADS[a][part][0]
+            round_columns(copy, c_mx[a][0][:, PACK * lo : PACK * hi], c_raw[a, part][:, :, lo - first : hi - first])
 
         def x_round(a, u, lo, hi):
             dst = x_mx[a][0][:, 2 * PASS * u : 2 * PASS * (u + 1)].rearrange("p (e n t) -> p e n t", e=2, t=PACK)
@@ -197,40 +190,40 @@ def tile_mix_kvw_outl_relu_kernel(
             for b in range(2)
         ]
 
-        def kc_banks(n, b, pair, by_column):
+        def kc_banks(chunk, b, pair, by_column):
             if by_column:
-                return [(bank(2 * pair + v), b, 0, CHUNK * n + P * v, P) for v in range(2)]
-            return [(bank(2 * pair + v), b, 2 * v, CHUNK * n, CHUNK) for v in range(2)]
+                return [(bank(2 * pair + v), b, 0, CHUNK * chunk + P * v, P) for v in range(2)]
+            return [(bank(2 * pair + v), b, 2 * v, CHUNK * chunk, CHUNK) for v in range(2)]
 
         def kc_passes(banks, a):
             for acc, b, t0, lo, width in banks:
                 tiles = BANK // width
-                for s in range(tiles):
-                    t = t0 + s
+                for slot in range(tiles):
+                    t = t0 + slot
                     scale_col = D * a + PASS * b + P * t
                     nc.tensor.matmul_mx(
-                        out=acc[:, width * s : width * (s + 1)],
+                        out=acc[:, width * slot : width * (slot + 1)],
                         lhsT=wk_dealt[b][:, PASS * a + P * t : PASS * a + P * (t + 1)].bitcast(FP8X4),
                         lhsT_scale=wk_scales_dealt[ROW_WK:, scale_col : scale_col + P],
                         rhs=c_mx[a][1][:, lo : lo + width].bitcast(FP8X4),
                         rhs_scale=c_mx[a][2][:, lo : lo + width],
-                        start=(a == 0 and s == 0),
-                        stop=(a == 1 and s == tiles - 1),
+                        start=(a == 0 and slot == 0),
+                        stop=(a == 1 and slot == tiles - 1),
                     )
 
         def kc_copy_out(banks):
             for acc, b, t0, lo, width in banks:
                 tiles = BANK // width
                 nc.scalar.copy(
-                    out=kc32[b][:, t0 : t0 + tiles, lo : lo + width], in_=acc[:].rearrange("p (s j) -> p s j", s=tiles)
+                    out=kc32[b][:, t0 : t0 + tiles, lo : lo + width], in_=acc[:].rearrange("p (t j) -> p t j", t=tiles)
                 )
 
         def kc_round_from_psum(banks):
             for acc, b, t0, lo, width in banks:
                 round_bank(kc_mx[b][0][:, PACK * lo : PACK * (lo + width)], acc)
 
-        def kc_round(b, lo, hi, copy=on_vector):
-            round_columns(copy, kc_mx[b][0][:, PACK * lo : PACK * hi], kc32[b][:, :, lo:hi])
+        def kc_round(b, lo, hi):
+            round_columns(on_vector, kc_mx[b][0][:, PACK * lo : PACK * hi], kc32[b][:, :, lo:hi])
 
         def store_kc32(b, t0, t1):
             nc.sync.dma_start(out=four_rows(out_1[PASS * b : PASS * (b + 1), :])[:, t0:t1, :], in_=kc32[b][:, t0:t1, :])
@@ -269,6 +262,9 @@ def tile_mix_kvw_outl_relu_kernel(
                     stop=(a == 1 and t == PACK - 1),
                 )
 
+        def qr_round(acc, n):
+            round_bank(qr_mx[n // 4][0][:, PASS * (n % 4) : PASS * (n % 4 + 1)], acc)
+
         def qr_quantize(g):
             lo = 2 * P * (g % 2)
             quantize(qr_mx[g // 2], lo, lo + 2 * P)
@@ -303,88 +299,91 @@ def tile_mix_kvw_outl_relu_kernel(
 
         deal_wk(0)
         deal_narrow(wk_scales_dealt[:], wk_scales_raw[:])
-        for n in (2, 3):
-            c_round(on_scalar, 0, CHUNK * n, CHUNK * (n + 1))
+        for chunk in (2, 3):
+            c_round(on_scalar, 0, CHUNK * chunk, CHUNK * (chunk + 1))
         c_round(on_vector, 0, 0, CHUNK)
         c_round(on_vector, 0, CHUNK, CHUNK + P)
         quantize(c_mx[0], 0, CHUNK)
-        low = [kc_banks(0, 0, 0, True)] + [kc_banks(n, 0, n, False) for n in (1, 2)]
+        low = {0: kc_banks(0, 0, 0, True)}
         kc_passes(low[0], 0)
-        c_chunk(0)
+        for lo in (0, P):
+            c_round(on_vector, 1, lo, lo + P)
+        for lo in (0, P):
+            quantize(c_mx[1], lo, lo + P)
         kc_passes(low[0], 1)
         kc_copy_out(low[0])
         kc_round_from_psum(low[0])
         deal_wk(1)
-        high = kc_banks(0, 1, 3, True)
-        kc_passes(high, 0)
-        kc_passes(high, 1)
-        kc_copy_out(high)
-        kc_round_from_psum(high)
-        c_round(on_vector, 0, CHUNK + P, BANK)
-        quantize(c_mx[0], BANK, J)
-        quantize(c_mx[0], CHUNK, BANK)
-        kc_passes(low[1], 0)
-        kc_passes(low[2], 0)
-        low.append(kc_banks(3, 0, 0, False))
-        kc_passes(low[3], 0)
+        high = {0: kc_banks(0, 1, 3, True)}
+        for a in range(2):
+            kc_passes(high[0], a)
+        kc_copy_out(high[0])
+        kc_round_from_psum(high[0])
+        c_round(on_vector, 0, CHUNK + P, 2 * CHUNK)
+        quantize(c_mx[0], 2 * CHUNK, J)
+        quantize(c_mx[0], CHUNK, 2 * CHUNK)
+        low.update({chunk: kc_banks(chunk, 0, chunk % 3, False) for chunk in (1, 2, 3)})
+        for chunk in (1, 2, 3):
+            kc_passes(low[chunk], 0)
         deal_narrow(wq_scales_dealt[:], wq_scales_raw[:])
 
-        for n in (1, 2, 3):
-            c_chunk(n)
-            kc_passes(low[n], 1)
-        high = {1: kc_banks(1, 1, 3, False)}
-        kc_passes(high[1], 0)
-        kc_passes(high[1], 1)
+        c_round(on_vector, 1, CHUNK, 2 * CHUNK)
+        for chunk in (1, 2):
+            c_round(on_vector, 1, CHUNK * (chunk + 1), CHUNK * (chunk + 2))
+            quantize(c_mx[1], CHUNK * chunk, CHUNK * (chunk + 1))
+            kc_passes(low[chunk], 1)
+        quantize(kc_mx[0], 0, CHUNK)
+        quantize(c_mx[1], 3 * CHUNK, J)
+        kc_passes(low[3], 1)
         kc_copy_out(low[1] + low[2][:1] + low[3][:1])
         store_kc32(0, 0, 2)
         kc_copy_out(low[2][1:] + low[3][1:])
         store_kc32(0, 2, 4)
-        kc_copy_out(high[1])
-        high.update({n: kc_banks(n, 1, pair, n == 3) for n, pair in ((2, 1), (3, 2))})
-        for n in (2, 3):
-            kc_passes(high[n], 0)
-            kc_passes(high[n], 1)
-            kc_copy_out(high[n])
+        high.update({chunk: kc_banks(chunk, 1, pair, chunk == 3) for chunk, pair in ((1, 3), (2, 1), (3, 2))})
+        for chunk in (1, 2, 3):
+            for a in range(2):
+                kc_passes(high[chunk], a)
+            kc_copy_out(high[chunk])
         store_kc32(1, 0, 4)
         kc_round_from_psum(high[3])
         deal_words(w8_dealt[:], w8_raw[:])
-        kc_round(0, CHUNK, BANK)
+        deal_narrow(w4_dealt[:].bitcast(U16), w4_raw[:].bitcast(U16))
+        kc_round(0, CHUNK, 2 * CHUNK)
+        quantize(kc_mx[1], 0, CHUNK)
 
         places = [2 * pair + v for pair in (0, 3, 1, 2) for v in range(2)]
         x_begin(0)
-        deal_narrow(w4_dealt[:].bitcast(U16), w4_raw[:].bitcast(U16))
+        quantize(kc_mx[0], CHUNK, 2 * CHUNK)
         x_end(0)
-        banks = [bank(place) for place in places]
-        for n in range(6):
-            qr_passes(banks[n], n, 0)
+        qr_banks = [bank(place) for place in places]
+        for n in range(QR_EARLY):
+            qr_passes(qr_banks[n], n, 0)
         x_begin(1)
-        quantize(kc_mx[0], 0, BANK)
+        kc_round(1, CHUNK, 2 * CHUNK)
         x_end(1)
         for n in range(BANKS):
-            qr_passes(banks[n], n, 1)
-            if n in (1, 2):
-                qr_passes(banks[n + 5], n + 5, 0)
-            round_bank(qr_mx[n // 4][0][:, PASS * (n % 4) : PASS * (n % 4 + 1)], banks[n])
+            qr_passes(qr_banks[n], n, 1)
+            late = QR_EARLY + n - 1
+            if QR_EARLY <= late < BANKS:
+                qr_passes(qr_banks[late], late, 0)
+            qr_round(qr_banks[n], n)
 
-        kc_round(1, CHUNK, BANK)
-        kc_round(0, BANK, J)
-        quantize(kc_mx[1], 0, BANK)
+        kc_round(0, 2 * CHUNK, J)
+        quantize(kc_mx[1], CHUNK, 2 * CHUNK)
         qr_quantize(0)
-        quantize(kc_mx[0], BANK, J)
+        quantize(kc_mx[0], 2 * CHUNK, J)
         store_codes(0)
         kc_round(1, 2 * CHUNK, 3 * CHUNK)
         qr_quantize(1)
-        quantize(kc_mx[1], BANK, J)
+        quantize(kc_mx[1], 2 * CHUNK, J)
         store_codes(1)
         store_scales()
-        qr_quantize(2)
-        score_bank(0, 0, False, places[0])
-        score_bank(1, 0, True, places[1])
-        qr_quantize(3)
-        score_bank(0, 1, False, places[2])
-        score_bank(1, 1, True, places[3])
+        for h in range(2):
+            qr_quantize(2 + h)
+            for g in range(2):
+                score_bank(g, h, g == 0, places[2 * h + g])
         store_scores(0)
         for g in (2, 3):
-            score_bank(g, 0, False, places[2 * g])
-            score_bank(g, 1, True, places[2 * g + 1])
+            for h in range(2):
+                score_bank(g, h, h == 0, places[2 * g + h])
         store_scores(1)

@@ -54,7 +54,7 @@ def tile_mix_kvw_outl_relu_kernel(
 
         wk_scales_raw = tile("wk_scales_raw", [P, 2 * D], U8)
         wq_scales_raw = tile("wq_scales_raw", [P, D], U8)
-        wk_raw = [tile("wk_raw%d" % b, [P, 2, PASS], U32) for b in range(2)]
+        wk_raw = [tile("wk_raw%d" % a, [P, D], U32) for a in range(2)]
         w8_raw = tile("w8_raw", [P, D], U32)
         w4_raw = tile("w4_raw", [P, 2 * D], U8)
         c_raw = {
@@ -74,9 +74,8 @@ def tile_mix_kvw_outl_relu_kernel(
                     in_=scales[:, r:16:4, :].rearrange("a q d -> q a d").bitcast(I32),
                 )
 
-        def load_wk(b):
-            words = wk_words.rearrange("a p n t -> p a (n t)").bitcast(I32)
-            nc.sync.dma_start(out=wk_raw[b][:].bitcast(I32), in_=words[:, :, PASS * b : PASS * (b + 1)])
+        def load_wk(a):
+            nc.sync.dma_start(out=wk_raw[a][:].bitcast(I32), in_=as_words(wk_words[a]))
 
         def load_w8():
             nc.sync.dma_start(out=w8_raw[:].bitcast(I32), in_=as_words(w8_words[0]))
@@ -94,11 +93,11 @@ def tile_mix_kvw_outl_relu_kernel(
         load_wk(0)
         load_scales(wk_scales_raw, ROW_WK, wk_scales)
         load_c(0, 0)
-        load_scales(wq_scales_raw, ROW_W8, w8_scales)
         load_c(1, 0)
         load_wk(1)
-        load_scales(wq_scales_raw, ROW_W4, w4_scales)
+        load_scales(wq_scales_raw, ROW_W8, w8_scales)
         load_c(1, 1)
+        load_scales(wq_scales_raw, ROW_W4, w4_scales)
         load_c(1, 2)
         load_w8()
         load_w4()
@@ -107,8 +106,8 @@ def tile_mix_kvw_outl_relu_kernel(
 
         def deal_words(dst, src):
             nc.vector.tensor_copy(
-                out=dst.bitcast(I32).rearrange("p (run t m) -> p run m t", run=2, t=PACK),
-                in_=src.bitcast(I32).rearrange("p (run m t) -> p run m t", run=2, t=PACK),
+                out=dst.bitcast(I32).rearrange("p (run t m) -> p run m t", m=P, t=PACK),
+                in_=src.bitcast(I32).rearrange("p (run m t) -> p run m t", m=P, t=PACK),
             )
 
         def deal_narrow(dst, src):
@@ -147,7 +146,7 @@ def tile_mix_kvw_outl_relu_kernel(
                 tile(name + "_scales", [P, width], U8),
             )
 
-        wk_dealt = [tile("wk_dealt%d" % b, [P, 2 * PASS], U32) for b in range(2)]
+        wk_dealt = [tile("wk_dealt%d" % a, [P, D], U32) for a in range(2)]
         w8_dealt = tile("w8_dealt", [P, D], U32)
         w4_dealt = tile("w4_dealt", [P, 2 * D], U8)
         wk_scales_dealt = tile("wk_scales_dealt", [P, 2 * D], U8)
@@ -155,8 +154,8 @@ def tile_mix_kvw_outl_relu_kernel(
         c_mx = [mx_operand("c%d" % a, J) for a in range(2)]
         x_mx = [mx_operand("x%d" % a, M) for a in range(2)]
 
-        def deal_wk(b):
-            deal_words(wk_dealt[b][:], wk_raw[b][:].rearrange("p a n -> p (a n)"))
+        def deal_wk(a, lo, hi):
+            deal_words(wk_dealt[a][:, lo:hi], wk_raw[a][:, lo:hi])
 
         def c_round(copy, a, lo, hi):
             part = len([first for first, width in C_LOADS[a] if first <= lo]) - 1
@@ -203,7 +202,7 @@ def tile_mix_kvw_outl_relu_kernel(
                     scale_col = D * a + PASS * b + P * t
                     nc.tensor.matmul_mx(
                         out=acc[:, width * slot : width * (slot + 1)],
-                        lhsT=wk_dealt[b][:, PASS * a + P * t : PASS * a + P * (t + 1)].bitcast(FP8X4),
+                        lhsT=wk_dealt[a][:, PASS * b + P * t : PASS * b + P * (t + 1)].bitcast(FP8X4),
                         lhsT_scale=wk_scales_dealt[ROW_WK:, scale_col : scale_col + P],
                         rhs=c_mx[a][1][:, lo : lo + width].bitcast(FP8X4),
                         rhs_scale=c_mx[a][2][:, lo : lo + width],
@@ -211,12 +210,10 @@ def tile_mix_kvw_outl_relu_kernel(
                         stop=(a == 1 and slot == tiles - 1),
                     )
 
-        def kc_copy_out(banks):
+        def kc_copy_out(banks, copy=nc.scalar.copy):
             for acc, b, t0, lo, width in banks:
                 tiles = BANK // width
-                nc.scalar.copy(
-                    out=kc32[b][:, t0 : t0 + tiles, lo : lo + width], in_=acc[:].rearrange("p (t j) -> p t j", t=tiles)
-                )
+                copy(out=kc32[b][:, t0 : t0 + tiles, lo : lo + width], in_=acc[:].rearrange("p (t j) -> p t j", t=tiles))
 
         def kc_round_from_psum(banks):
             for acc, b, t0, lo, width in banks:
@@ -297,7 +294,7 @@ def tile_mix_kvw_outl_relu_kernel(
                 in_=scores[:, 2 * u : 2 * u + 2, :],
             )
 
-        deal_wk(0)
+        deal_wk(0, 0, D)
         deal_narrow(wk_scales_dealt[:], wk_scales_raw[:])
         for chunk in (2, 3):
             c_round(on_scalar, 0, CHUNK * chunk, CHUNK * (chunk + 1))
@@ -305,33 +302,34 @@ def tile_mix_kvw_outl_relu_kernel(
         c_round(on_vector, 0, CHUNK, CHUNK + P)
         quantize(c_mx[0], 0, CHUNK)
         low = {0: kc_banks(0, 0, 0, True)}
-        kc_passes(low[0], 0)
-        for lo in (0, P):
-            c_round(on_vector, 1, lo, lo + P)
-        for lo in (0, P):
-            quantize(c_mx[1], lo, lo + P)
-        kc_passes(low[0], 1)
-        kc_copy_out(low[0])
-        kc_round_from_psum(low[0])
-        deal_wk(1)
         high = {0: kc_banks(0, 1, 3, True)}
+        kc_passes(low[0], 0)
+        c_round(on_vector, 1, 0, CHUNK)
+        c_round(on_vector, 0, CHUNK + P, 2 * CHUNK)
+        quantize(c_mx[1], 0, CHUNK)
+        for b in range(2):
+            deal_wk(1, PASS * b, PASS * (b + 1))
+        kc_passes(low[0], 1)
         for a in range(2):
             kc_passes(high[0], a)
+        quantize(c_mx[0], CHUNK, 2 * CHUNK)
+        quantize(c_mx[0], 2 * CHUNK, J)
+        kc_copy_out(low[0][:1])
+        kc_round_from_psum(low[0][:1])
+        kc_copy_out(low[0][1:], on_vector)
+        kc_round_from_psum(low[0][1:])
         kc_copy_out(high[0])
         kc_round_from_psum(high[0])
-        c_round(on_vector, 0, CHUNK + P, 2 * CHUNK)
-        quantize(c_mx[0], 2 * CHUNK, J)
-        quantize(c_mx[0], CHUNK, 2 * CHUNK)
         low.update({chunk: kc_banks(chunk, 0, chunk % 3, False) for chunk in (1, 2, 3)})
         for chunk in (1, 2, 3):
             kc_passes(low[chunk], 0)
-        deal_narrow(wq_scales_dealt[:], wq_scales_raw[:])
 
         c_round(on_vector, 1, CHUNK, 2 * CHUNK)
+        c_round(on_vector, 1, 2 * CHUNK, 3 * CHUNK)
         for chunk in (1, 2):
-            c_round(on_vector, 1, CHUNK * (chunk + 1), CHUNK * (chunk + 2))
             quantize(c_mx[1], CHUNK * chunk, CHUNK * (chunk + 1))
             kc_passes(low[chunk], 1)
+        c_round(on_vector, 1, 3 * CHUNK, J)
         quantize(kc_mx[0], 0, CHUNK)
         quantize(c_mx[1], 3 * CHUNK, J)
         kc_passes(low[3], 1)
@@ -346,6 +344,7 @@ def tile_mix_kvw_outl_relu_kernel(
             kc_copy_out(high[chunk])
         store_kc32(1, 0, 4)
         kc_round_from_psum(high[3])
+        deal_narrow(wq_scales_dealt[:], wq_scales_raw[:])
         deal_words(w8_dealt[:], w8_raw[:])
         deal_narrow(w4_dealt[:].bitcast(U16), w4_raw[:].bitcast(U16))
         kc_round(0, CHUNK, 2 * CHUNK)

@@ -27,7 +27,7 @@ SCORE_SCALE = 0.03125
 ROW_W4, ROW_W8, ROW_WK, ROW_KC = 0, 4, 8, 12
 
 CHUNK = 256
-C_LOADS = (((0, 1024),), ((0, 256), (256, 512), (768, 256)))
+C_LOADS = (((0, 1024),), ((0, 256), (256, 768)))
 QR_EARLY = BANKS - 2
 
 
@@ -98,7 +98,6 @@ def tile_mix_kvw_outl_relu_kernel(
         load_scales(wq_scales_raw, ROW_W8, w8_scales)
         load_c(1, 1)
         load_scales(wq_scales_raw, ROW_W4, w4_scales)
-        load_c(1, 2)
         load_w8()
         load_w4()
         load_x(0)
@@ -296,6 +295,17 @@ def tile_mix_kvw_outl_relu_kernel(
 
         deal_wk(0, 0, D)
         deal_narrow(wk_scales_dealt[:], wk_scales_raw[:])
+        warm = bank(7)
+        for n in range(8):
+            nc.tensor.matmul_mx(
+                out=warm[:],
+                lhsT=wk_dealt[0][:, 0:P].bitcast(FP8X4),
+                lhsT_scale=wk_scales_dealt[ROW_WK:, 0:P],
+                rhs=wk_dealt[0][:, 0:BANK].bitcast(FP8X4),
+                rhs_scale=wk_scales_dealt[ROW_WK:, 0:BANK],
+                start=True,
+                stop=True,
+            )
         for chunk in (2, 3):
             c_round(on_scalar, 0, CHUNK * chunk, CHUNK * (chunk + 1))
         c_round(on_vector, 0, 0, CHUNK)
@@ -303,54 +313,55 @@ def tile_mix_kvw_outl_relu_kernel(
         quantize(c_mx[0], 0, CHUNK)
         low = {0: kc_banks(0, 0, 0, True)}
         high = {0: kc_banks(0, 1, 3, True)}
-        kc_passes(low[0], 0)
+        kc_passes(low[0] + high[0], 0)
         c_round(on_vector, 1, 0, CHUNK)
         c_round(on_vector, 0, CHUNK + P, 2 * CHUNK)
         quantize(c_mx[1], 0, CHUNK)
         for b in range(2):
             deal_wk(1, PASS * b, PASS * (b + 1))
-        kc_passes(low[0], 1)
-        for a in range(2):
-            kc_passes(high[0], a)
+        kc_passes(low[0] + high[0], 1)
         quantize(c_mx[0], CHUNK, 2 * CHUNK)
         quantize(c_mx[0], 2 * CHUNK, J)
         kc_copy_out(low[0][:1])
         kc_round_from_psum(low[0][:1])
         kc_copy_out(low[0][1:], on_vector)
         kc_round_from_psum(low[0][1:])
-        kc_copy_out(high[0])
+        kc_copy_out(high[0], on_vector)
         kc_round_from_psum(high[0])
         low.update({chunk: kc_banks(chunk, 0, chunk % 3, False) for chunk in (1, 2, 3)})
         for chunk in (1, 2, 3):
             kc_passes(low[chunk], 0)
 
-        c_round(on_vector, 1, CHUNK, 2 * CHUNK)
-        c_round(on_vector, 1, 2 * CHUNK, 3 * CHUNK)
-        for chunk in (1, 2):
-            quantize(c_mx[1], CHUNK * chunk, CHUNK * (chunk + 1))
-            kc_passes(low[chunk], 1)
-        c_round(on_vector, 1, 3 * CHUNK, J)
+        high.update({1: kc_banks(1, 1, 3, False)})
+        kc_passes(high[1], 0)
         quantize(kc_mx[0], 0, CHUNK)
+        c_round(on_scalar, 1, 3 * CHUNK, J)
+        c_round(on_scalar, 1, 2 * CHUNK + P, 3 * CHUNK)
+        c_round(on_vector, 1, CHUNK, 2 * CHUNK)
+        c_round(on_vector, 1, 2 * CHUNK, 2 * CHUNK + P)
+        quantize(c_mx[1], CHUNK, 2 * CHUNK)
+        quantize(kc_mx[1], 0, CHUNK)
         quantize(c_mx[1], 3 * CHUNK, J)
-        kc_passes(low[3], 1)
-        kc_copy_out(low[1] + low[2][:1] + low[3][:1])
+        deal_words(w8_dealt[:, :PASS], w8_raw[:, :PASS])
+        quantize(c_mx[1], 2 * CHUNK, 3 * CHUNK)
+        kc_passes(low[1] + low[3][:1] + low[2][:1] + low[3][1:] + low[2][1:], 1)
+        kc_copy_out(low[1] + low[3][:1] + low[2][:1])
         store_kc32(0, 0, 2)
-        kc_copy_out(low[2][1:] + low[3][1:])
+        kc_copy_out(low[3][1:] + low[2][1:])
         store_kc32(0, 2, 4)
-        high.update({chunk: kc_banks(chunk, 1, pair, chunk == 3) for chunk, pair in ((1, 3), (2, 1), (3, 2))})
+        high.update({chunk: kc_banks(chunk, 1, pair, chunk == 3) for chunk, pair in ((2, 1), (3, 0))})
         for chunk in (1, 2, 3):
-            for a in range(2):
+            for a in range(1 if chunk == 1 else 0, 2):
                 kc_passes(high[chunk], a)
             kc_copy_out(high[chunk])
         store_kc32(1, 0, 4)
         kc_round_from_psum(high[3])
         deal_narrow(wq_scales_dealt[:], wq_scales_raw[:])
-        deal_words(w8_dealt[:], w8_raw[:])
+        deal_words(w8_dealt[:, PASS:], w8_raw[:, PASS:])
         deal_narrow(w4_dealt[:].bitcast(U16), w4_raw[:].bitcast(U16))
-        kc_round(0, CHUNK, 2 * CHUNK)
-        quantize(kc_mx[1], 0, CHUNK)
 
-        places = [2 * pair + v for pair in (0, 3, 1, 2) for v in range(2)]
+        places = [4, 5, 6, 7, 2, 3, 0, 1]
+        kc_round(0, CHUNK, 2 * CHUNK)
         x_begin(0)
         quantize(kc_mx[0], CHUNK, 2 * CHUNK)
         x_end(0)

@@ -295,17 +295,6 @@ def tile_mix_kvw_outl_relu_kernel(
 
         deal_wk(0, 0, D)
         deal_narrow(wk_scales_dealt[:], wk_scales_raw[:])
-        warm = bank(7)
-        for n in range(8):
-            nc.tensor.matmul_mx(
-                out=warm[:],
-                lhsT=wk_dealt[0][:, 0:P].bitcast(FP8X4),
-                lhsT_scale=wk_scales_dealt[ROW_WK:, 0:P],
-                rhs=wk_dealt[0][:, 0:BANK].bitcast(FP8X4),
-                rhs_scale=wk_scales_dealt[ROW_WK:, 0:BANK],
-                start=True,
-                stop=True,
-            )
         for chunk in (2, 3):
             c_round(on_scalar, 0, CHUNK * chunk, CHUNK * (chunk + 1))
         c_round(on_vector, 0, 0, CHUNK)

@@ -29,6 +29,7 @@ ROW_W4, ROW_W8, ROW_WK, ROW_KC = 0, 4, 8, 12
 CHUNK = 256
 C_LOADS = (((0, 1024),), ((0, 256), (256, 768)))
 QR_EARLY = BANKS - 2
+SCALAR_FROM = CHUNK + P
 
 
 def tile_mix_kvw_outl_relu_kernel(
@@ -103,6 +104,9 @@ def tile_mix_kvw_outl_relu_kernel(
         load_x(0)
         load_x(1)
 
+        def half(words, b):
+            return words[:, PASS * b : PASS * (b + 1)]
+
         def deal_words(dst, src):
             nc.vector.tensor_copy(
                 out=dst.bitcast(I32).rearrange("p (run t m) -> p run m t", m=P, t=PACK),
@@ -152,9 +156,6 @@ def tile_mix_kvw_outl_relu_kernel(
         wq_scales_dealt = tile("wq_scales_dealt", [P, D], U8)
         c_mx = [mx_operand("c%d" % a, J) for a in range(2)]
         x_mx = [mx_operand("x%d" % a, M) for a in range(2)]
-
-        def deal_wk(a, lo, hi):
-            deal_words(wk_dealt[a][:, lo:hi], wk_raw[a][:, lo:hi])
 
         def c_round(copy, a, lo, hi):
             part = len([first for first, width in C_LOADS[a] if first <= lo]) - 1
@@ -209,7 +210,7 @@ def tile_mix_kvw_outl_relu_kernel(
                         stop=(a == 1 and slot == tiles - 1),
                     )
 
-        def kc_copy_out(banks, copy=nc.scalar.copy):
+        def kc_copy_out(copy, banks):
             for acc, b, t0, lo, width in banks:
                 tiles = BANK // width
                 copy(out=kc32[b][:, t0 : t0 + tiles, lo : lo + width], in_=acc[:].rearrange("p (t j) -> p t j", t=tiles))
@@ -218,11 +219,11 @@ def tile_mix_kvw_outl_relu_kernel(
             for acc, b, t0, lo, width in banks:
                 round_bank(kc_mx[b][0][:, PACK * lo : PACK * (lo + width)], acc)
 
-        def kc_round(b, lo, hi):
-            round_columns(on_vector, kc_mx[b][0][:, PACK * lo : PACK * hi], kc32[b][:, :, lo:hi])
+        def kc_round(copy, b, lo, hi):
+            round_columns(copy, kc_mx[b][0][:, PACK * lo : PACK * hi], kc32[b][:, :, lo:hi])
 
-        def store_kc32(b, t0, t1):
-            nc.sync.dma_start(out=four_rows(out_1[PASS * b : PASS * (b + 1), :])[:, t0:t1, :], in_=kc32[b][:, t0:t1, :])
+        def store_kc32(b):
+            nc.sync.dma_start(out=four_rows(out_1[PASS * b : PASS * (b + 1), :]), in_=kc32[b][:])
 
         def store_codes(b):
             nc.sync.dma_start(out=as_words(out_2[b]), in_=kc_mx[b][1][:].bitcast(I32))
@@ -293,36 +294,38 @@ def tile_mix_kvw_outl_relu_kernel(
                 in_=scores[:, 2 * u : 2 * u + 2, :],
             )
 
-        deal_wk(0, 0, D)
+        deal_words(wk_dealt[0][:], wk_raw[0][:])
         deal_narrow(wk_scales_dealt[:], wk_scales_raw[:])
         for chunk in (2, 3):
             c_round(on_scalar, 0, CHUNK * chunk, CHUNK * (chunk + 1))
-        c_round(on_vector, 0, 0, CHUNK)
+        c_round(on_vector, 0, 0, P)
+        c_round(on_vector, 0, P, CHUNK)
+        quantize(c_mx[0], 0, P)
         c_round(on_vector, 0, CHUNK, CHUNK + P)
-        quantize(c_mx[0], 0, CHUNK)
+        quantize(c_mx[0], P, CHUNK)
         low = {0: kc_banks(0, 0, 0, True)}
         high = {0: kc_banks(0, 1, 3, True)}
-        kc_passes(low[0] + high[0], 0)
+        kc_passes(low[0] + high[0][:1], 0)
         c_round(on_vector, 1, 0, CHUNK)
         c_round(on_vector, 0, CHUNK + P, 2 * CHUNK)
         quantize(c_mx[1], 0, CHUNK)
         for b in range(2):
-            deal_wk(1, PASS * b, PASS * (b + 1))
-        kc_passes(low[0] + high[0], 1)
+            deal_words(half(wk_dealt[1], b), half(wk_raw[1], b))
+        kc_passes(low[0], 1)
+        kc_passes(high[0][1:], 0)
+        kc_passes(high[0], 1)
         quantize(c_mx[0], CHUNK, 2 * CHUNK)
         quantize(c_mx[0], 2 * CHUNK, J)
-        kc_copy_out(low[0][:1])
+        kc_copy_out(nc.scalar.copy, low[0][:1])
         kc_round_from_psum(low[0][:1])
-        kc_copy_out(low[0][1:], on_vector)
+        kc_copy_out(on_vector, low[0][1:])
         kc_round_from_psum(low[0][1:])
-        kc_copy_out(high[0], on_vector)
+        kc_copy_out(on_vector, high[0])
         kc_round_from_psum(high[0])
         low.update({chunk: kc_banks(chunk, 0, chunk % 3, False) for chunk in (1, 2, 3)})
-        for chunk in (1, 2, 3):
-            kc_passes(low[chunk], 0)
-
         high.update({1: kc_banks(1, 1, 3, False)})
-        kc_passes(high[1], 0)
+        kc_passes(low[1] + low[2] + low[3] + high[1], 0)
+
         quantize(kc_mx[0], 0, CHUNK)
         c_round(on_scalar, 1, 3 * CHUNK, J)
         c_round(on_scalar, 1, 2 * CHUNK + P, 3 * CHUNK)
@@ -331,34 +334,35 @@ def tile_mix_kvw_outl_relu_kernel(
         quantize(c_mx[1], CHUNK, 2 * CHUNK)
         quantize(kc_mx[1], 0, CHUNK)
         quantize(c_mx[1], 3 * CHUNK, J)
-        deal_words(w8_dealt[:, :PASS], w8_raw[:, :PASS])
+        deal_words(half(w8_dealt, 0), half(w8_raw, 0))
         quantize(c_mx[1], 2 * CHUNK, 3 * CHUNK)
-        kc_passes(low[1] + low[3][:1] + low[2][:1] + low[3][1:] + low[2][1:], 1)
-        kc_copy_out(low[1] + low[3][:1] + low[2][:1])
-        store_kc32(0, 0, 2)
-        kc_copy_out(low[3][1:] + low[2][1:])
-        store_kc32(0, 2, 4)
-        high.update({chunk: kc_banks(chunk, 1, pair, chunk == 3) for chunk, pair in ((2, 1), (3, 0))})
-        for chunk in (1, 2, 3):
-            for a in range(1 if chunk == 1 else 0, 2):
-                kc_passes(high[chunk], a)
-            kc_copy_out(high[chunk])
-        store_kc32(1, 0, 4)
-        kc_round_from_psum(high[3])
+        kc_passes(low[1] + low[3] + low[2], 1)
+        kc_copy_out(nc.scalar.copy, low[1] + low[3][:1] + low[2][:1])
         deal_narrow(wq_scales_dealt[:], wq_scales_raw[:])
-        deal_words(w8_dealt[:, PASS:], w8_raw[:, PASS:])
+        kc_copy_out(on_vector, low[3][1:] + low[2][1:])
+        store_kc32(0)
+        kc_passes(high[1], 1)
+        kc_copy_out(nc.scalar.copy, high[1])
+        for chunk, pair in ((2, 1), (3, 0)):
+            high.update({chunk: kc_banks(chunk, 1, pair, chunk == 3)})
+            for a in range(2):
+                kc_passes(high[chunk], a)
+            kc_copy_out(nc.scalar.copy, high[chunk])
+        store_kc32(1)
+        kc_round_from_psum(high[3])
+        kc_round(on_scalar, 1, SCALAR_FROM, 3 * CHUNK)
+        deal_words(half(w8_dealt, 1), half(w8_raw, 1))
         deal_narrow(w4_dealt[:].bitcast(U16), w4_raw[:].bitcast(U16))
 
-        places = [4, 5, 6, 7, 2, 3, 0, 1]
-        kc_round(0, CHUNK, 2 * CHUNK)
+        places = [2 * pair + v for pair in (2, 3, 1, 0) for v in range(2)]
         x_begin(0)
-        quantize(kc_mx[0], CHUNK, 2 * CHUNK)
+        kc_round(on_vector, 0, CHUNK, 2 * CHUNK)
         x_end(0)
         qr_banks = [bank(place) for place in places]
         for n in range(QR_EARLY):
             qr_passes(qr_banks[n], n, 0)
         x_begin(1)
-        kc_round(1, CHUNK, 2 * CHUNK)
+        quantize(kc_mx[0], CHUNK, 2 * CHUNK)
         x_end(1)
         for n in range(BANKS):
             qr_passes(qr_banks[n], n, 1)
@@ -367,12 +371,12 @@ def tile_mix_kvw_outl_relu_kernel(
                 qr_passes(qr_banks[late], late, 0)
             qr_round(qr_banks[n], n)
 
-        kc_round(0, 2 * CHUNK, J)
+        kc_round(on_vector, 1, CHUNK, SCALAR_FROM)
+        kc_round(on_vector, 0, 2 * CHUNK, J)
         quantize(kc_mx[1], CHUNK, 2 * CHUNK)
         qr_quantize(0)
         quantize(kc_mx[0], 2 * CHUNK, J)
         store_codes(0)
-        kc_round(1, 2 * CHUNK, 3 * CHUNK)
         qr_quantize(1)
         quantize(kc_mx[1], 2 * CHUNK, J)
         store_codes(1)

@@ -42,7 +42,7 @@ def tile_mix_kvw_outl_relu_kernel(
         ctx.enter_context(tc.manual_schedule())
 
         def tile(name, shape, dtype):
-            return sbuf.tile(shape, dtype, name=name, align_bytes=64)
+            return sbuf.tile(shape, dtype, name=name, align_bytes=256)
 
         def bank(place):
             return psum.tile([P, BANK], F32, name="bank%d" % place)

@@ -42,7 +42,7 @@ def tile_mix_kvw_outl_relu_kernel(
         ctx.enter_context(tc.manual_schedule())
 
         def tile(name, shape, dtype):
-            return sbuf.tile(shape, dtype, name=name, align_bytes=256)
+            return sbuf.tile(shape, dtype, name=name, align_bytes=512)
 
         def bank(place):
             return psum.tile([P, BANK], F32, name="bank%d" % place)

from contextlib import ExitStack

import concourse.mybir as mybir

K, D, M, J = 1024, 1024, 512, 1024
FLOPS = 2 * K * D * M + 2 * K * D * J + 2 * D * M * J

F32 = mybir.dt.float32
BF16 = mybir.dt.bfloat16
I32 = mybir.dt.int32
U32 = mybir.dt.uint32
U16 = mybir.dt.uint16
U8 = mybir.dt.uint8
FP8X4 = mybir.dt.float8_e4m3fn_x4
FP4X4 = mybir.dt.float4_e2m1fn_x4
ACT = mybir.ActivationFunctionType
ALU = mybir.AluOpType

P = 128
PACK = 4
PASS = P * PACK
BANK = 512
BANKS = 8
LINE = 4
SCORE_SCALE = 0.03125

ROW_W4, ROW_W8, ROW_WK, ROW_KC = 0, 4, 8, 12

CHUNK = 256
C_LOADS = (((0, 1024),), ((0, 256), (256, 768)))
QR_EARLY = BANKS - 2
SCALAR_FROM = CHUNK + P


def tile_mix_kvw_outl_relu_kernel(
    tc, x, w8_words, w8_scales, w4_words, w4_scales, c, wk_words, wk_scales, out_0, out_1, out_2, out_3
):
    nc = tc.nc
    with ExitStack() as ctx:
        sbuf = ctx.enter_context(tc.tile_pool(name="sbuf", bufs=1))
        psum = ctx.enter_context(tc.psum_pool(name="psum", bufs=1))
        ctx.enter_context(tc.manual_schedule())

        def tile(name, shape, dtype):
            return sbuf.tile(shape, dtype, name=name, align_bytes=512)

        def bank(place):
            return psum.tile([P, BANK], F32, name="bank%d" % place)

        def as_words(codes):
            return codes.rearrange("p n t -> p (n t)").bitcast(I32)

        def four_rows(rows):
            return rows.rearrange("(p t) n -> p t n", t=PACK)

        wk_scales_raw = tile("wk_scales_raw", [P, 2 * D], U8)
        wq_scales_raw = tile("wq_scales_raw", [P, D], U8)
        wk_raw = [tile("wk_raw%d" % a, [P, D], U32) for a in range(2)]
        w8_raw = tile("w8_raw", [P, D], U32)
        w4_raw = tile("w4_raw", [P, 2 * D], U8)
        c_raw = {
            (a, part): tile("c_raw%d%d" % (a, part), [P, PACK, width], F32)
            for a in range(2)
            for part, (first, width) in enumerate(C_LOADS[a])
        }
        x_raw = [tile("x_raw%d" % a, [P, PACK, M], F32) for a in range(2)]

        nc.vector.memset(wk_scales_raw[:].bitcast(I32), 0)
        nc.vector.memset(wq_scales_raw[:].bitcast(I32), 0)

        def load_scales(dst, row, scales):
            for r in range(4):
                nc.sync.dma_start(
                    out=dst[row + r : P : 32, :].rearrange("q (a d) -> q a d", d=D).bitcast(I32),
                    in_=scales[:, r:16:4, :].rearrange("a q d -> q a d").bitcast(I32),
                )

        def load_wk(a):
            nc.sync.dma_start(out=wk_raw[a][:].bitcast(I32), in_=as_words(wk_words[a]))

        def load_w8():
            nc.sync.dma_start(out=w8_raw[:].bitcast(I32), in_=as_words(w8_words[0]))

        def load_w4():
            nc.sync.dma_start(out=w4_raw[:].bitcast(I32), in_=w4_words[0].bitcast(I32))

        def load_x(a):
            nc.sync.dma_start(out=x_raw[a][:], in_=four_rows(x[PASS * a : PASS * (a + 1), :]))

        def load_c(a, part):
            first, width = C_LOADS[a][part]
            nc.sync.dma_start(out=c_raw[a, part][:], in_=four_rows(c[PASS * a : PASS * (a + 1), first : first + width]))

        load_wk(0)
        load_scales(wk_scales_raw, ROW_WK, wk_scales)
        load_c(0, 0)
        load_c(1, 0)
        load_wk(1)
        load_scales(wq_scales_raw, ROW_W8, w8_scales)
        load_c(1, 1)
        load_scales(wq_scales_raw, ROW_W4, w4_scales)
        load_w8()
        load_w4()
        load_x(0)
        load_x(1)

        def half(words, b):
            return words[:, PASS * b : PASS * (b + 1)]

        def deal_words(dst, src):
            nc.vector.tensor_copy(
                out=dst.bitcast(I32).rearrange("p (run t m) -> p run m t", m=P, t=PACK),
                in_=src.bitcast(I32).rearrange("p (run m t) -> p run m t", m=P, t=PACK),
            )

        def deal_narrow(dst, src):
            nc.vector.tensor_copy(
                out=dst.rearrange("p (run t m) -> p run t m", m=P, t=PACK),
                in_=src.rearrange("p (run m t) -> p run t m", m=P, t=PACK),
            )

        def on_vector(out, in_):
            nc.vector.tensor_copy(out=out, in_=in_)

        def on_scalar(out, in_):
            nc.scalar.activation(out=out, in_=in_, func=ACT.Copy)

        def round_columns(copy, dst, src):
            copy(
                dst.rearrange("p (n i t) -> p n t i", i=LINE, t=PACK),
                src.rearrange("p t (n i) -> p n t i", i=LINE),
            )

        def round_bank(dst, acc):
            nc.scalar.copy(
                out=dst.rearrange("p (n t) -> p n t", t=PACK), in_=acc[:].rearrange("p (t n) -> p n t", t=PACK)
            )

        def quantize(operand, lo, hi):
            rounded, codes, scales = operand
            nc.vector.quantize_mx(
                out=codes[:, lo:hi].bitcast(FP8X4), scales=scales[:, lo:hi], in_=rounded[:, PACK * lo : PACK * hi]
            )

        def mx_operand(name, width):
            return (
                tile(name + "_rounded", [P, PACK * width], BF16),
                tile(name + "_codes", [P, width], U32),
                tile(name + "_scales", [P, width], U8),
            )

        wk_dealt = [tile("wk_dealt%d" % a, [P, D], U32) for a in range(2)]
        w8_dealt = tile("w8_dealt", [P, D], U32)
        w4_dealt = tile("w4_dealt", [P, 2 * D], U8)
        wk_scales_dealt = tile("wk_scales_dealt", [P, 2 * D], U8)
        wq_scales_dealt = tile("wq_scales_dealt", [P, D], U8)
        c_mx = [mx_operand("c%d" % a, J) for a in range(2)]
        x_mx = [mx_operand("x%d" % a, M) for a in range(2)]

        def c_round(copy, a, lo, hi):
            part = len([first for first, width in C_LOADS[a] if first <= lo]) - 1
            first = C_LOADS[a][part][0]
            round_columns(copy, c_mx[a][0][:, PACK * lo : PACK * hi], c_raw[a, part][:, :, lo - first : hi - first])

        def x_round(a, u, lo, hi):
            dst = x_mx[a][0][:, 2 * PASS * u : 2 * PASS * (u + 1)].rearrange("p (e n t) -> p e n t", e=2, t=PACK)
            nc.vector.tensor_copy(
                out=dst[:, :, lo:hi, :].rearrange("p e (n i) t -> p n t i e", i=2),
                in_=x_raw[a][:, :, 2 * (P * u + lo) : 2 * (P * u + hi)].rearrange("p t (n i e) -> p n t i e", i=2, e=2),
            )

        def x_begin(a):
            x_round(a, 0, 0, P)
            x_round(a, 1, 0, P // 2)
            quantize(x_mx[a], 0, 2 * P)
            x_round(a, 1, P // 2, P)

        def x_end(a):
            quantize(x_mx[a], 2 * P, 4 * P)

        kc32 = [tile("kc32_%d" % b, [P, PACK, J], F32) for b in range(2)]
        kc_scales = tile("kc_scales", [P, 2 * J], U8)
        kc_mx = [
            (
                tile("kc_rounded%d" % b, [P, PACK * J], BF16),
                tile("kc_codes%d" % b, [P, J], U32),
                kc_scales[ROW_KC:, J * b : J * (b + 1)],
            )
            for b in range(2)
        ]

        def kc_banks(chunk, b, pair, by_column):
            if by_column:
                return [(bank(2 * pair + v), b, 0, CHUNK * chunk + P * v, P) for v in range(2)]
            return [(bank(2 * pair + v), b, 2 * v, CHUNK * chunk, CHUNK) for v in range(2)]

        def kc_passes(banks, a):
            for acc, b, t0, lo, width in banks:
                tiles = BANK // width
                for slot in range(tiles):
                    t = t0 + slot
                    scale_col = D * a + PASS * b + P * t
                    nc.tensor.matmul_mx(
                        out=acc[:, width * slot : width * (slot + 1)],
                        lhsT=wk_dealt[a][:, PASS * b + P * t : PASS * b + P * (t + 1)].bitcast(FP8X4),
                        lhsT_scale=wk_scales_dealt[ROW_WK:, scale_col : scale_col + P],
                        rhs=c_mx[a][1][:, lo : lo + width].bitcast(FP8X4),
                        rhs_scale=c_mx[a][2][:, lo : lo + width],
                        start=(a == 0 and slot == 0),
                        stop=(a == 1 and slot == tiles - 1),
                    )

        def kc_copy_out(copy, banks):
            for acc, b, t0, lo, width in banks:
                tiles = BANK // width
                copy(out=kc32[b][:, t0 : t0 + tiles, lo : lo + width], in_=acc[:].rearrange("p (t j) -> p t j", t=tiles))

        def kc_round_from_psum(banks):
            for acc, b, t0, lo, width in banks:
                round_bank(kc_mx[b][0][:, PACK * lo : PACK * (lo + width)], acc)

        def kc_round(copy, b, lo, hi):
            round_columns(copy, kc_mx[b][0][:, PACK * lo : PACK * hi], kc32[b][:, :, lo:hi])

        def store_kc32(b):
            nc.sync.dma_start(out=four_rows(out_1[PASS * b : PASS * (b + 1), :]), in_=kc32[b][:])

        def store_codes(b):
            nc.sync.dma_start(out=as_words(out_2[b]), in_=kc_mx[b][1][:].bitcast(I32))

        def store_scales():
            for r in range(4):
                nc.sync.dma_start(
                    out=out_3[:, r:16:4, :].rearrange("b q j -> q b j").bitcast(I32),
                    in_=kc_scales[ROW_KC + r : P : 32, :].rearrange("q (b j) -> q b j", b=2).bitcast(I32),
                )

        qr_mx = [mx_operand("qr%d" % u, 4 * P) for u in range(2)]
        scores = tile("scores", [P, 4, J], F32)

        def qr_passes(acc, n, a):
            g, b = divmod(n, 2)
            tokens = slice(P * g, P * (g + 1))
            for t in range(PACK):
                i = PACK * b + t
                if a == 0:
                    weights = w8_dealt[:, P * i : P * (i + 1)].bitcast(FP8X4)
                    weight_scales = wq_scales_dealt[ROW_W8:, P * i : P * (i + 1)]
                else:
                    weights = w4_dealt[:, 2 * P * i : 2 * P * (i + 1)].bitcast(FP4X4)
                    weight_scales = wq_scales_dealt[ROW_W4:, P * i : P * (i + 1)]
                nc.tensor.matmul_mx(
                    out=acc[:, P * t : P * (t + 1)],
                    lhsT=weights,
                    lhsT_scale=weight_scales,
                    rhs=x_mx[a][1][:, tokens].bitcast(FP8X4),
                    rhs_scale=x_mx[a][2][:, tokens],
                    start=(a == 0 and t == 0),
                    stop=(a == 1 and t == PACK - 1),
                )

        def qr_round(acc, n):
            round_bank(qr_mx[n // 4][0][:, PASS * (n % 4) : PASS * (n % 4 + 1)], acc)

        def qr_quantize(g):
            lo = 2 * P * (g % 2)
            quantize(qr_mx[g // 2], lo, lo + 2 * P)

        def score_bank(g, h, on_vector_engine, place):
            acc = bank(place)
            keys = slice(BANK * h, BANK * (h + 1))
            for b in range(2):
                n = 2 * g + b
                cols = slice(P * (n % 4), P * (n % 4 + 1))
                nc.tensor.matmul_mx(
                    out=acc[:],
                    lhsT=qr_mx[n // 4][1][:, cols].bitcast(FP8X4),
                    lhsT_scale=qr_mx[n // 4][2][:, cols],
                    rhs=kc_mx[b][1][:, keys].bitcast(FP8X4),
                    rhs_scale=kc_mx[b][2][:, keys],
                    start=(b == 0),
                    stop=(b == 1),
                )
            if on_vector_engine:
                nc.vector.tensor_scalar(
                    out=scores[:, g, keys], in0=acc[:], scalar1=0.0, scalar2=SCORE_SCALE, op0=ALU.max, op1=ALU.mult
                )
            else:
                nc.scalar.activation(out=scores[:, g, keys], in_=acc[:], func=ACT.Relu, scale=SCORE_SCALE)

        def store_scores(u):
            nc.sync.dma_start(
                out=out_0[2 * P * u : 2 * P * (u + 1), :].rearrange("(p e) j -> p e j", e=2),
                in_=scores[:, 2 * u : 2 * u + 2, :],
            )

        deal_words(wk_dealt[0][:], wk_raw[0][:])
        deal_narrow(wk_scales_dealt[:], wk_scales_raw[:])
        for chunk in (2, 3):
            c_round(on_scalar, 0, CHUNK * chunk, CHUNK * (chunk + 1))
        c_round(on_vector, 0, 0, P)
        c_round(on_vector, 0, P, CHUNK)
        quantize(c_mx[0], 0, P)
        c_round(on_vector, 0, CHUNK, CHUNK + P)
        quantize(c_mx[0], P, CHUNK)
        low = {0: kc_banks(0, 0, 0, True)}
        high = {0: kc_banks(0, 1, 3, True)}
        kc_passes(low[0] + high[0][:1], 0)
        c_round(on_vector, 1, 0, CHUNK)
        c_round(on_vector, 0, CHUNK + P, 2 * CHUNK)
        quantize(c_mx[1], 0, CHUNK)
        for b in range(2):
            deal_words(half(wk_dealt[1], b), half(wk_raw[1], b))
        kc_passes(low[0], 1)
        kc_passes(high[0][1:], 0)
        kc_passes(high[0], 1)
        quantize(c_mx[0], CHUNK, 2 * CHUNK)
        quantize(c_mx[0], 2 * CHUNK, J)
        kc_copy_out(nc.scalar.copy, low[0][:1])
        kc_round_from_psum(low[0][:1])
        kc_copy_out(on_vector, low[0][1:])
        kc_round_from_psum(low[0][1:])
        kc_copy_out(on_vector, high[0])
        kc_round_from_psum(high[0])
        low.update({chunk: kc_banks(chunk, 0, chunk % 3, False) for chunk in (1, 2, 3)})
        high.update({1: kc_banks(1, 1, 3, False)})
        kc_passes(low[1] + low[2] + low[3] + high[1], 0)

        quantize(kc_mx[0], 0, CHUNK)
        c_round(on_scalar, 1, 3 * CHUNK, J)
        c_round(on_scalar, 1, 2 * CHUNK + P, 3 * CHUNK)
        c_round(on_vector, 1, CHUNK, 2 * CHUNK)
        c_round(on_vector, 1, 2 * CHUNK, 2 * CHUNK + P)
        quantize(c_mx[1], CHUNK, 2 * CHUNK)
        quantize(kc_mx[1], 0, CHUNK)
        quantize(c_mx[1], 3 * CHUNK, J)
        deal_words(half(w8_dealt, 0), half(w8_raw, 0))
        quantize(c_mx[1], 2 * CHUNK, 3 * CHUNK)
        kc_passes(low[1] + low[3] + low[2], 1)
        kc_copy_out(nc.scalar.copy, low[1] + low[3][:1] + low[2][:1])
        deal_narrow(wq_scales_dealt[:], wq_scales_raw[:])
        kc_copy_out(on_vector, low[3][1:] + low[2][1:])
        store_kc32(0)
        kc_passes(high[1], 1)
        kc_copy_out(nc.scalar.copy, high[1])
        for chunk, pair in ((2, 1), (3, 0)):
            high.update({chunk: kc_banks(chunk, 1, pair, chunk == 3)})
            for a in range(2):
                kc_passes(high[chunk], a)
            kc_copy_out(nc.scalar.copy, high[chunk])
        store_kc32(1)
        kc_round_from_psum(high[3])
        kc_round(on_scalar, 1, SCALAR_FROM, 3 * CHUNK)
        deal_words(half(w8_dealt, 1), half(w8_raw, 1))
        deal_narrow(w4_dealt[:].bitcast(U16), w4_raw[:].bitcast(U16))

        places = [2 * pair + v for pair in (2, 3, 1, 0) for v in range(2)]
        x_begin(0)
        kc_round(on_vector, 0, CHUNK, 2 * CHUNK)
        x_end(0)
        qr_banks = [bank(place) for place in places]
        for n in range(QR_EARLY):
            qr_passes(qr_banks[n], n, 0)
        x_begin(1)
        quantize(kc_mx[0], CHUNK, 2 * CHUNK)
        x_end(1)
        for n in range(BANKS):
            qr_passes(qr_banks[n], n, 1)
            late = QR_EARLY + n - 1
            if QR_EARLY <= late < BANKS:
                qr_passes(qr_banks[late], late, 0)
            qr_round(qr_banks[n], n)

        kc_round(on_vector, 1, CHUNK, SCALAR_FROM)
        kc_round(on_vector, 0, 2 * CHUNK, J)
        quantize(kc_mx[1], CHUNK, 2 * CHUNK)
        qr_quantize(0)
        quantize(kc_mx[0], 2 * CHUNK, J)
        store_codes(0)
        qr_quantize(1)
        quantize(kc_mx[1], 2 * CHUNK, J)
        store_codes(1)
        store_scales()
        for h in range(2):
            qr_quantize(2 + h)
            for g in range(2):
                score_bank(g, h, g == 0, places[2 * h + g])
        store_scores(0)
        for g in (2, 3):
            for h in range(2):
                score_bank(g, h, h == 0, places[2 * g + h])
        store_scores(1)
